import numpy as np
import ml_dtypes


def mxq(x, axis, fmt="e4m3"):
    dtype, down = {"e4m3": (ml_dtypes.float8_e4m3fn, 7), "e5m2": (ml_dtypes.float8_e5m2, 14)}[fmt]
    v = np.moveaxis(np.asarray(x, np.float32).astype(ml_dtypes.bfloat16).astype(np.float64), axis, -1)
    blocks = v.reshape(v.shape[:-1] + (-1, 32))
    amax = np.abs(blocks).max(-1, keepdims=True)
    byte = np.maximum(np.where(amax > 0, np.frexp(amax)[1] - 1 + 127, 0) - down, 1)
    scale = np.exp2(byte - 127.0)
    codes = (blocks / scale).astype(np.float32).astype(dtype).astype(np.float64)
    return np.moveaxis((codes * scale).reshape(v.shape), -1, axis)


WIDE = False


def mx_kscale(k):
    if not WIDE:
        return np.ones(k)
    levels = np.array([10, -10, 5, -5, 0])
    if k % 512:
        return np.exp2(np.random.permutation(np.resize(levels, k // 32))).repeat(32)
    a = np.empty((k // 512, 16))
    for p in range(k // 512):
        a[p, :8] = np.random.permutation(np.resize(levels, 8))
        for g in range(8):
            far = levels[np.abs(levels - a[p, g]) >= 10]
            a[p, g + 8] = far[np.random.randint(len(far))]
    return np.exp2(a.ravel()).repeat(32)


def f64(x):
    return np.asarray(x).astype(np.float64)


def striped(idx):
    return np.tile(idx.reshape(-1, 16).T, (8, 1)).astype(np.uint16)


def unstriped(offs):
    return offs[:16].T.reshape(-1).astype(np.int64)


E2M1 = np.array([0.0, 0.5, 1.0, 1.5, 2.0, 3.0, 4.0, 6.0, -0.0, -0.5, -1.0, -1.5, -2.0, -3.0, -4.0, -6.0])


def pack_weight(w, fmt):
    k, n = w.shape
    w = f64(np.asarray(w, np.float32).astype(ml_dtypes.bfloat16)).reshape(k // 32, 32, n)
    amax = np.abs(w).max(1)
    if fmt == "e4m3":
        byte = np.frexp(amax)[1] - 1 + 127 - 7
    else:
        mant, ex = np.frexp(amax / 6.0)
        byte = np.where(mant > 0.5, ex, ex - 1) + 127
    byte = np.clip(np.where(amax > 0, byte, 1), 1, 254)
    scaled = (w * np.exp2(127.0 - byte)[:, None, :]).reshape(k, n).astype(np.float32)
    by_word = np.ascontiguousarray(scaled.reshape(k // 512, 128, 4, n).transpose(0, 1, 3, 2))
    if fmt == "e4m3":
        words = by_word.astype(ml_dtypes.float8_e4m3fn).view(np.uint8)
    else:
        c = by_word.astype(ml_dtypes.float4_e2m1fn).view(np.uint8) & 0xF
        words = (c[..., 0::2] | (c[..., 1::2] << 4)).reshape(k // 512, 128, 2 * n)
    return np.ascontiguousarray(words), np.ascontiguousarray(byte.astype(np.uint8).reshape(k // 512, 16, n))


def unpack_weight(words, scales, fmt):
    g, _, n = scales.shape
    words = np.ascontiguousarray(words).reshape(g, 128, n, -1)
    if fmt == "e4m3":
        vals = words.view(ml_dtypes.float8_e4m3fn).astype(np.float64)
    else:
        nib = np.empty((g, 128, n, 4), np.uint8)
        nib[..., 0::2] = words & 0xF
        nib[..., 1::2] = words >> 4
        vals = E2M1[nib]
    vals = vals * np.repeat(np.exp2(scales.astype(np.float64) - 127.0), 8, axis=1)[..., None]
    return vals.transpose(0, 1, 3, 2).reshape(g * 512, n)


K, T, E, C, N = 2048, 768, 2, 256, 128


def by_expert(wq, xq):
    return np.concatenate([wq[e].T @ xq[:, e * C:(e + 1) * C] for e in range(E)], axis=1)


def setup_inputs():
    n = np.random.standard_normal
    s = mx_kscale(K)[:, None]
    w = [pack_weight(m, "e2m1") for m in n((E + 1, K, N)) / np.sqrt(K) / s[None]]
    return {
        "xT": (n((K, T)) * s).astype(np.float32),
        "w_words": np.stack([m[0] for m in w]),
        "w_scales": np.stack([m[1] for m in w]),
        "gate": np.tile(np.random.uniform(0.2, 1.0, E * C), (N, 1)).astype(np.float32),
        "offs": striped(np.random.permutation(T)[:E * C]),
    }


def reference(xT, w_words, w_scales, gate, offs):
    idx = unstriped(offs)
    w = np.stack([unpack_weight(w_words[e], w_scales[e], "e2m1") for e in range(E + 1)])
    wq = w
    xs = mxq(f64(xT), 0, "e4m3")
    ys = wq[E].T @ xs
    xq = mxq(f64(xT)[:, idx], 0, "e4m3")
    y = by_expert(w, xq)
    out = ys
    out[:, idx] += f64(gate) * y
    return out

@@ -1,0 +1,195 @@
+from contextlib import ExitStack
+
+import concourse.mybir as mybir
+
+F32 = mybir.dt.float32
+BF16 = mybir.dt.bfloat16
+I32 = mybir.dt.int32
+U32 = mybir.dt.uint32
+U16 = mybir.dt.uint16
+U8 = mybir.dt.uint8
+FP8X4 = mybir.dt.float8_e4m3fn_x4
+FP4X4 = mybir.dt.float4_e2m1fn_x4
+MULT = mybir.AluOpType.mult
+ADD = mybir.AluOpType.add
+
+P = 128
+K, T, E, C, N = 2048, 768, 2, 256, 128
+S = E * C
+PASSES = K // 512
+FLOPS = 2 * K * N * (T + S)
+
+
+def tile_moe_shr_lin_none_kernel(tc, xT, w_words, w_scales, gate, offs, out):
+    nc = tc.nc
+    with ExitStack() as ctx:
+        keep = ctx.enter_context(tc.tile_pool(name="keep", bufs=1))
+        psum = ctx.enter_context(tc.psum_pool(name="psum", bufs=1))
+
+        x_view = xT.rearrange("(g p u e) w -> g u p e w", p=P, u=2, e=2)
+        half = T // 2
+        third = T // 3
+        offsets = keep.tile([P, S // 16], U16, name="offsets")
+        raw = []
+        for g in range(PASSES):
+            for u in range(2):
+                r = keep.tile([P, 2, T], F32, name=f"raw{g}{u}")
+                cuts = 3 if g == u == 0 else 2 if g == 0 else 1
+                for i in range(cuts):
+                    cols = slice(i * T // cuts, (i + 1) * T // cuts)
+                    nc.sync.dma_start(r[:, :, cols], x_view[g, u, :, :, cols])
+                if g == u == 0:
+                    nc.sync.dma_start(offsets[:], offs)
+                raw.append(r)
+
+        planes = keep.tile([P, (E + 1) * PASSES * N], U8, name="planes", align_bytes=64)
+        nc.gpsimd.memset(planes[:].bitcast(I32), 0)
+        window = keep.tile([P, T], F32, name="window")
+        nc.gpsimd.memset(window[:], 0.0)
+
+        words = keep.tile([P, (E + 1) * PASSES, 2 * N], U8, name="words", align_bytes=64)
+        s_view = w_scales.rearrange("e a q n -> q (e a) n")
+        for q in range(4):
+            nc.sync.dma_start(
+                planes[32 * q : 32 * q + 4, :].rearrange("p (m n) -> p m n", n=N).bitcast(I32),
+                s_view[4 * q : 4 * q + 4].bitcast(I32),
+            )
+        nc.sync.dma_start(words[:].bitcast(I32), w_words.rearrange("e a p b -> p (e a) b").bitcast(I32))
+        gate_sb = keep.tile([P, S], F32, name="gate_sb")
+        nc.sync.dma_start(gate_sb[:], gate)
+
+        pairs = [keep.tile([P, 2, T, 2], BF16, name=f"pairs{g}", align_bytes=64) for g in range(PASSES)]
+        got = [keep.tile([P, 2, S, 2], BF16, name=f"got{g}", align_bytes=64) for g in range(PASSES)]
+        x_in = [keep.tile([P, 4 * T], BF16, name=f"x_in{g}", align_bytes=64) for g in range(PASSES)]
+        r_in = [keep.tile([P, 4 * S], BF16, name=f"r_in{g}", align_bytes=64) for g in range(PASSES)]
+        x_codes = [keep.tile([P, T], U32, name=f"x_codes{g}", align_bytes=64) for g in range(PASSES)]
+        x_scales = [keep.tile([P, T], U8, name=f"x_scales{g}", align_bytes=64) for g in range(PASSES)]
+        r_codes = [keep.tile([P, S], U32, name=f"r_codes{g}", align_bytes=64) for g in range(PASSES)]
+        r_scales = [keep.tile([P, S], U8, name=f"r_scales{g}", align_bytes=64) for g in range(PASSES)]
+        x_bank0 = psum.tile([P, 512], F32, name="x_bank0")
+        x_bank1 = psum.tile([P, 256], F32, name="x_bank1")
+        r_bank0 = psum.tile([P, 128], F32, name="r_bank0")
+        r_bank1 = psum.tile([P, 128], F32, name="r_bank1")
+        r_bank2 = psum.tile([P, 256], F32, name="r_bank2")
+
+        def pair_up(engine_copy, g, u, a, b):
+            engine_copy(out=pairs[g][:, u, a:b, :], in_=raw[2 * g + u][:, :, a:b].rearrange("p e w -> p w e"))
+
+        def gather(g, u):
+            nc.vector.tensor_copy(
+                got[g][:, u].rearrange("p s e -> p (s e)").bitcast(U32),
+                pairs[g][:, u].rearrange("p w e -> p (w e)").bitcast(U32).indirect(offsets[:]),
+            )
+
+        def quad_vector(dst, src, a, b):
+            nc.vector.tensor_copy(
+                out=dst[:].bitcast(I32).rearrange("p (w u) -> p w u", u=2)[:, a:b],
+                in_=src[:].rearrange("p u w e -> p (u w e)").bitcast(I32).rearrange("p (u w) -> p w u", u=2)[:, a:b],
+            )
+
+        def quad_scalar(dst, src, a, b):
+            nc.scalar.copy(
+                out=dst[:].bitcast(U32).rearrange("p (w u) -> p w u", u=2)[:, a:b],
+                in_=src[:].rearrange("p u w e -> p (u w e)").bitcast(U32).rearrange("p (u w) -> p w u", u=2)[:, a:b],
+            )
+
+        def quantize_tokens(g):
+            for a, b in ((0, 512), (512, T)):
+                nc.vector.quantize_mx(
+                    out=x_codes[g][:, a:b].bitcast(FP8X4), scales=x_scales[g][:, a:b], in_=x_in[g][:, 4 * a : 4 * b]
+                )
+
+        def quantize_slots(g):
+            nc.vector.quantize_mx(out=r_codes[g][:].bitcast(FP8X4), scales=r_scales[g][:], in_=r_in[g][:])
+
+        def product(bank, e, g, codes, scales, c, w):
+            m = e * PASSES + g
+            nc.tensor.matmul_mx(
+                out=bank,
+                lhsT=words[:, m, :].bitcast(FP4X4),
+                lhsT_scale=planes[:, m * N : (m + 1) * N],
+                rhs=codes[:, c : c + w].bitcast(FP8X4),
+                rhs_scale=scales[:, c : c + w],
+                start=(g == 0),
+                stop=(g == PASSES - 1),
+            )
+
+        def multiply_tokens(g):
+            product(x_bank0[:], E, g, x_codes[g], x_scales[g], 0, 512)
+            product(x_bank1[:, 0:128], E, g, x_codes[g], x_scales[g], 512, 128)
+            if g == PASSES - 1:
+                for a in range(PASSES):
+                    product(x_bank1[:, 128:256], E, a, x_codes[a], x_scales[a], 640, 128)
+
+        def multiply_slots(g):
+            product(r_bank0[:], 0, g, r_codes[g], r_scales[g], 0, 128)
+            product(r_bank1[:], 0, g, r_codes[g], r_scales[g], 128, 128)
+            product(r_bank2[:, 0:128], 1, g, r_codes[g], r_scales[g], 256, 128)
+            if g == PASSES - 1:
+                for a in range(PASSES):
+                    product(r_bank2[:, 128:256], 1, a, r_codes[a], r_scales[a], 384, 128)
+
+        y_sb = [keep.tile([P, C], F32, name=f"y_sb{e}") for e in range(E)]
+
+        def scatter(e):
+            nc.vector.tensor_tensor(
+                window[:].indirect(offsets[:, e * (C // 16) : (e + 1) * (C // 16)]),
+                y_sb[e][:],
+                gate_sb[:, e * C : (e + 1) * C],
+                MULT,
+            )
+
+        pair_up(nc.scalar.copy, 0, 0, 0, third)
+        pair_up(nc.vector.tensor_copy, 0, 0, third, 2 * third)
+        pair_up(nc.vector.tensor_copy, 0, 0, 2 * third, T)
+        pair_up(nc.scalar.copy, 0, 1, 0, half)
+        gather(0, 0)
+        pair_up(nc.vector.tensor_copy, 0, 1, half, T)
+        gather(0, 1)
+        pair_up(nc.scalar.copy, 1, 0, 0, T)
+        quad_vector(x_in[0], pairs[0], 0, T)
+        quad_vector(r_in[0], got[0], 0, S)
+        pair_up(nc.scalar.copy, 1, 1, 0, T)
+        quantize_tokens(0)
+        quantize_slots(0)
+        gather(1, 0)
+        pair_up(nc.scalar.copy, 2, 0, 0, T)
+        gather(1, 1)
+        pair_up(nc.scalar.copy, 2, 1, 0, T)
+        gather(2, 0)
+        quad_vector(r_in[1], got[1], 0, S)
+        pair_up(nc.scalar.copy, 3, 0, 0, T)
+        gather(2, 1)
+        pair_up(nc.scalar.copy, 3, 1, 0, T)
+        gather(3, 0)
+        quad_scalar(x_in[1], pairs[1], 0, T)
+        gather(3, 1)
+        quantize_slots(1)
+        quad_scalar(r_in[2], got[2], 0, S)
+        quantize_tokens(1)
+        multiply_tokens(0)
+        multiply_slots(0)
+        multiply_tokens(1)
+        multiply_slots(1)
+        quad_vector(r_in[3], got[3], 0, S)
+        quantize_slots(2)
+        multiply_slots(2)
+        quad_scalar(x_in[2], pairs[2], 0, T)
+        quantize_slots(3)
+        multiply_slots(3)
+        quad_scalar(x_in[3], pairs[3], 0, T)
+        quantize_tokens(2)
+        multiply_tokens(2)
+        nc.scalar.copy(out=y_sb[0][:, 0:128], in_=r_bank0[:])
+        nc.scalar.copy(out=y_sb[0][:, 128:256], in_=r_bank1[:])
+        nc.scalar.copy(out=y_sb[1][:], in_=r_bank2[:])
+        scatter(0)
+        quantize_tokens(3)
+        multiply_tokens(3)
+        scatter(1)
+
+        result = keep.tile([P, T], F32, name="result")
+        nc.vector.tensor_tensor(result[:, 0:512], x_bank0[:], window[:, 0:512], ADD)
+        nc.sync.dma_start(out[:, 0:512], result[:, 0:512])
+        nc.vector.tensor_tensor(result[:, 512:T], x_bank1[:], window[:, 512:T], ADD)
+        nc.sync.dma_start(out[:, 512:T], result[:, 512:T])

@@ -27,20 +27,28 @@ def tile_moe_shr_lin_none_kernel(tc, xT, w_words, w_scales, gate, offs, out):
         psum = ctx.enter_context(tc.psum_pool(name="psum", bufs=1))
 
         x_view = xT.rearrange("(g p u e) w -> g u p e w", p=P, u=2, e=2)
-        half = T // 2
-        third = T // 3
         offsets = keep.tile([P, S // 16], U16, name="offsets")
-        raw = []
+        raw = {}
+        middle = keep.tile([P, 5 * 2 * T], F32, name="middle", align_bytes=64)
         for g in range(PASSES):
             for u in range(2):
-                r = keep.tile([P, 2, T], F32, name=f"raw{g}{u}")
-                cuts = 3 if g == u == 0 else 2 if g == 0 else 1
+                cuts = 3 if g == u == 0 else 2 if g == 0 or (g, u) == (3, 1) else 1
                 for i in range(cuts):
-                    cols = slice(i * T // cuts, (i + 1) * T // cuts)
-                    nc.sync.dma_start(r[:, :, cols], x_view[g, u, :, :, cols])
+                    a, b = i * T // cuts, (i + 1) * T // cuts
+                    tag = f"raw{g}{u}" + "x" * i
+                    if cuts == 1:
+                        h = 2 * g + u - 2
+                        r = middle[:, h * 2 * T : (h + 1) * 2 * T].rearrange("p (e w) -> p e w", e=2)
+                    else:
+                        r = keep.tile([P, 2, b - a], F32, name=tag, tag=tag, align_bytes=64)[:]
+                    nc.sync.dma_start(r, x_view[g, u, :, :, a:b])
+                    raw[g, u, a] = r
                 if g == u == 0:
                     nc.sync.dma_start(offsets[:], offs)
-                raw.append(r)
+
+        def rows(g, u, a, b):
+            first = max(c for (i, j, c) in raw if (i, j) == (g, u) and c <= a)
+            return raw[g, u, first][:, :, a - first : b - first]
 
         planes = keep.tile([P, (E + 1) * PASSES * N], U8, name="planes", align_bytes=64)
         nc.gpsimd.memset(planes[:].bitcast(I32), 0)
@@ -58,13 +66,14 @@ def tile_moe_shr_lin_none_kernel(tc, xT, w_words, w_scales, gate, offs, out):
         gate_sb = keep.tile([P, S], F32, name="gate_sb")
         nc.sync.dma_start(gate_sb[:], gate)
 
-        pairs = [keep.tile([P, 2, T, 2], BF16, name=f"pairs{g}", align_bytes=64) for g in range(PASSES)]
-        got = [keep.tile([P, 2, S, 2], BF16, name=f"got{g}", align_bytes=64) for g in range(PASSES)]
-        x_in = [keep.tile([P, 4 * T], BF16, name=f"x_in{g}", align_bytes=64) for g in range(PASSES)]
-        r_in = [keep.tile([P, 4 * S], BF16, name=f"r_in{g}", align_bytes=64) for g in range(PASSES)]
+        pairs = [keep.tile([P, 4 * T], BF16, name=f"pairs{g}", align_bytes=64) for g in range(PASSES)]
+        got = [keep.tile([P, 4 * S], BF16, name=f"got{g}", align_bytes=64) for g in range(PASSES)]
+        r_last = keep.tile([P, 4 * S], BF16, name="r_last", align_bytes=64)
+        x_first = keep.tile([P, 4 * T], BF16, name="x_first", align_bytes=64)
+        x_late = keep.tile([P, 4 * (2 * T + 256 + S)], BF16, name="x_late", tag="raw31", align_bytes=64)
         x_codes = [keep.tile([P, T], U32, name=f"x_codes{g}", align_bytes=64) for g in range(PASSES)]
         x_scales = [keep.tile([P, T], U8, name=f"x_scales{g}", align_bytes=64) for g in range(PASSES)]
-        r_codes = [keep.tile([P, S], U32, name=f"r_codes{g}", align_bytes=64) for g in range(PASSES)]
+        r_codes = [keep.tile([P, S], U32, name=f"r_codes{g}", tag=f"r_codes{g}", align_bytes=64) for g in range(PASSES)]
         r_scales = [keep.tile([P, S], U8, name=f"r_scales{g}", align_bytes=64) for g in range(PASSES)]
         x_bank0 = psum.tile([P, 512], F32, name="x_bank0")
         x_bank1 = psum.tile([P, 256], F32, name="x_bank1")
@@ -72,35 +81,50 @@ def tile_moe_shr_lin_none_kernel(tc, xT, w_words, w_scales, gate, offs, out):
         r_bank1 = psum.tile([P, 128], F32, name="r_bank1")
         r_bank2 = psum.tile([P, 256], F32, name="r_bank2")
 
+        def gpsimd_cast(out, in_):
+            nc.gpsimd.tensor_scalar(out, in_, 1.0, 0.0, MULT, ADD)
+
+        on_scalar, on_vector, on_gpsimd = nc.scalar.copy, nc.vector.tensor_copy, gpsimd_cast
+
         def pair_up(engine_copy, g, u, a, b):
-            engine_copy(out=pairs[g][:, u, a:b, :], in_=raw[2 * g + u][:, :, a:b].rearrange("p e w -> p w e"))
+            engine_copy(
+                out=pairs[g][:, 2 * (u * T + a) : 2 * (u * T + b)].rearrange("p (w e) -> p w e", e=2),
+                in_=rows(g, u, a, b).rearrange("p e w -> p w e"),
+            )
 
         def gather(g, u):
             nc.vector.tensor_copy(
-                got[g][:, u].rearrange("p s e -> p (s e)").bitcast(U32),
-                pairs[g][:, u].rearrange("p w e -> p (w e)").bitcast(U32).indirect(offsets[:]),
+                got[g][:, 2 * u * S : 2 * (u + 1) * S].bitcast(U32),
+                pairs[g][:, 2 * u * T : 2 * (u + 1) * T].bitcast(U32).indirect(offsets[:]),
             )
 
-        def quad_vector(dst, src, a, b):
-            nc.vector.tensor_copy(
-                out=dst[:].bitcast(I32).rearrange("p (w u) -> p w u", u=2)[:, a:b],
-                in_=src[:].rearrange("p u w e -> p (u w e)").bitcast(I32).rearrange("p (u w) -> p w u", u=2)[:, a:b],
+        def quad(engine_copy, dst, src, a, b):
+            word = U32 if engine_copy is on_scalar else I32
+            engine_copy(
+                out=dst.bitcast(word).rearrange("p (w u) -> p w u", u=2),
+                in_=src[:].bitcast(word).rearrange("p (u w) -> p w u", u=2)[:, a:b],
             )
 
-        def quad_scalar(dst, src, a, b):
-            nc.scalar.copy(
-                out=dst[:].bitcast(U32).rearrange("p (w u) -> p w u", u=2)[:, a:b],
-                in_=src[:].rearrange("p u w e -> p (u w e)").bitcast(U32).rearrange("p (u w) -> p w u", u=2)[:, a:b],
+        def token_quads(g, a, b):
+            if a < 512:
+                return x_wide[g][:, 4 * a : 4 * b]
+            return x_rest[g][:, 4 * (a - 512) : 4 * (b - 512)]
+
+        def quad_tokens(engine_copy, g, a, b):
+            quad(engine_copy, token_quads(g, a, b), pairs[g], a, b)
+
+        def quad_slots(engine_copy, g, a, b):
+            quad(engine_copy, r_in[g][:, 4 * a : 4 * b], got[g], a, b)
+
+        def quantize_tokens(g, a, b):
+            nc.vector.quantize_mx(
+                out=x_codes[g][:, a:b].bitcast(FP8X4), scales=x_scales[g][:, a:b], in_=token_quads(g, a, b)
             )
 
-        def quantize_tokens(g):
-            for a, b in ((0, 512), (512, T)):
-                nc.vector.quantize_mx(
-                    out=x_codes[g][:, a:b].bitcast(FP8X4), scales=x_scales[g][:, a:b], in_=x_in[g][:, 4 * a : 4 * b]
-                )
-
-        def quantize_slots(g):
-            nc.vector.quantize_mx(out=r_codes[g][:].bitcast(FP8X4), scales=r_scales[g][:], in_=r_in[g][:])
+        def quantize_slots(g, a, b):
+            nc.vector.quantize_mx(
+                out=r_codes[g][:, a:b].bitcast(FP8X4), scales=r_scales[g][:, a:b], in_=r_in[g][:, 4 * a : 4 * b]
+            )
 
         def product(bank, e, g, codes, scales, c, w):
             m = e * PASSES + g
@@ -139,53 +163,85 @@ def tile_moe_shr_lin_none_kernel(tc, xT, w_words, w_scales, gate, offs, out):
                 MULT,
             )
 
-        pair_up(nc.scalar.copy, 0, 0, 0, third)
-        pair_up(nc.vector.tensor_copy, 0, 0, third, 2 * third)
-        pair_up(nc.vector.tensor_copy, 0, 0, 2 * third, T)
-        pair_up(nc.scalar.copy, 0, 1, 0, half)
+        def leave_banks():
+            nc.scalar.copy(out=y_sb[0][:, 0:128], in_=r_bank0[:])
+            nc.scalar.copy(out=y_sb[0][:, 128:256], in_=r_bank1[:])
+            nc.scalar.copy(out=y_sb[1][:], in_=r_bank2[:])
+
+        x_last = keep.tile([P, 4 * 512], BF16, name="x_last", tag="r_codes3", align_bytes=64)
+        x_wide = [x_first[:, 0:2048], x_late[:, 0:2048], x_late[:, 4 * T : 4 * T + 2048], x_last[:]]
+        x_rest = [x_first[:, 2048:], x_late[:, 2048 : 4 * T], x_late[:, 4 * T + 2048 : 8 * T], x_late[:, 8 * T : 8 * T + 1024]]
+        r_in = [middle[:, (2 * g + 1) * 2 * T + 384 - 2 * S : (2 * g + 1) * 2 * T + 384].bitcast(BF16) for g in range(2)]
+        r_in = r_in + [x_late[:, 8 * T + 1024 :], r_last[:]]
+
+        def leave_bank(e):
+            if e == 0:
+                nc.scalar.copy(out=y_sb[0][:, 0:128], in_=r_bank0[:])
+                nc.scalar.copy(out=y_sb[0][:, 128:256], in_=r_bank1[:])
+            else:
+                nc.scalar.copy(out=y_sb[1][:], in_=r_bank2[:])
+
+        pair_up(on_scalar, 0, 0, 0, 256)
+        pair_up(on_vector, 0, 0, 256, 512)
+        pair_up(on_vector, 0, 0, 512, T)
+        pair_up(on_scalar, 0, 1, 0, 384)
         gather(0, 0)
-        pair_up(nc.vector.tensor_copy, 0, 1, half, T)
+        pair_up(on_vector, 0, 1, 384, T)
         gather(0, 1)
-        pair_up(nc.scalar.copy, 1, 0, 0, T)
-        quad_vector(x_in[0], pairs[0], 0, T)
-        quad_vector(r_in[0], got[0], 0, S)
-        pair_up(nc.scalar.copy, 1, 1, 0, T)
-        quantize_tokens(0)
-        quantize_slots(0)
+        quad_tokens(on_scalar, 0, 0, 384)
+        quad_tokens(on_scalar, 0, 384, 512)
+        quad_tokens(on_scalar, 0, 512, T)
+        quantize_tokens(0, 0, 512)
+        pair_up(on_scalar, 1, 0, 0, 512)
+        pair_up(on_vector, 1, 0, 512, T)
+        quantize_tokens(0, 512, T)
         gather(1, 0)
-        pair_up(nc.scalar.copy, 2, 0, 0, T)
+        pair_up(on_gpsimd, 1, 1, 384, T)
+        pair_up(on_scalar, 1, 1, 0, 384)
         gather(1, 1)
-        pair_up(nc.scalar.copy, 2, 1, 0, T)
+        quad_slots(on_scalar, 0, 0, S)
+        quantize_slots(0, 0, S)
+        pair_up(on_gpsimd, 2, 0, 384, T)
+        pair_up(on_scalar, 2, 0, 0, 384)
         gather(2, 0)
-        quad_vector(r_in[1], got[1], 0, S)
-        pair_up(nc.scalar.copy, 3, 0, 0, T)
+        pair_up(on_gpsimd, 2, 1, 384, T)
+        pair_up(on_scalar, 2, 1, 0, 384)
         gather(2, 1)
-        pair_up(nc.scalar.copy, 3, 1, 0, T)
+        quad_slots(on_scalar, 1, 0, S)
+        quantize_slots(1, 0, S)
+        pair_up(on_gpsimd, 3, 0, 384, T)
+        pair_up(on_scalar, 3, 0, 0, 384)
         gather(3, 0)
-        quad_scalar(x_in[1], pairs[1], 0, T)
+        pair_up(on_gpsimd, 3, 1, 384, T)
+        pair_up(on_scalar, 3, 1, 0, 384)
         gather(3, 1)
-        quantize_slots(1)
-        quad_scalar(r_in[2], got[2], 0, S)
-        quantize_tokens(1)
-        multiply_tokens(0)
+        quad_slots(on_scalar, 2, 0, S)
+        quantize_slots(2, 0, S)
+        quad_tokens(on_scalar, 1, 0, 512)
+        quantize_tokens(1, 0, 512)
+        quad_slots(on_vector, 3, 0, S)
+        quantize_slots(3, 0, S)
         multiply_slots(0)
-        multiply_tokens(1)
         multiply_slots(1)
-        quad_vector(r_in[3], got[3], 0, S)
-        quantize_slots(2)
         multiply_slots(2)
-        quad_scalar(x_in[2], pairs[2], 0, T)
-        quantize_slots(3)
         multiply_slots(3)
-        quad_scalar(x_in[3], pairs[3], 0, T)
-        quantize_tokens(2)
+        quad_tokens(on_scalar, 1, 512, T)
+        quantize_tokens(1, 512, T)
+        multiply_tokens(0)
+        multiply_tokens(1)
+        quad_tokens(on_scalar, 2, 0, 512)
+        quantize_tokens(2, 0, 512)
+        quad_tokens(on_scalar, 2, 512, T)
+        quantize_tokens(2, 512, T)
         multiply_tokens(2)
-        nc.scalar.copy(out=y_sb[0][:, 0:128], in_=r_bank0[:])
-        nc.scalar.copy(out=y_sb[0][:, 128:256], in_=r_bank1[:])
-        nc.scalar.copy(out=y_sb[1][:], in_=r_bank2[:])
+        quad_tokens(on_scalar, 3, 512, T)
+        quantize_tokens(3, 512, T)
+        leave_bank(0)
         scatter(0)
-        quantize_tokens(3)
+        quad_tokens(on_scalar, 3, 0, 512)
+        quantize_tokens(3, 0, 512)
         multiply_tokens(3)
+        leave_bank(1)
         scatter(1)
 
         result = keep.tile([P, T], F32, name="result")

@@ -29,16 +29,16 @@ def tile_moe_shr_lin_none_kernel(tc, xT, w_words, w_scales, gate, offs, out):
         x_view = xT.rearrange("(g p u e) w -> g u p e w", p=P, u=2, e=2)
         offsets = keep.tile([P, S // 16], U16, name="offsets")
         raw = {}
-        middle = keep.tile([P, 5 * 2 * T], F32, name="middle", align_bytes=64)
+        middle = keep.tile([P, 6 * 2 * T], F32, name="middle", align_bytes=64)
         for g in range(PASSES):
             for u in range(2):
                 cuts = 3 if g == u == 0 else 2 if g == 0 or (g, u) == (3, 1) else 1
                 for i in range(cuts):
                     a, b = i * T // cuts, (i + 1) * T // cuts
                     tag = f"raw{g}{u}" + "x" * i
-                    if cuts == 1:
+                    if g > 0:
                         h = 2 * g + u - 2
-                        r = middle[:, h * 2 * T : (h + 1) * 2 * T].rearrange("p (e w) -> p e w", e=2)
+                        r = middle[:, h * 2 * T : (h + 1) * 2 * T].rearrange("p (e w) -> p e w", e=2)[:, :, a:b]
                     else:
                         r = keep.tile([P, 2, b - a], F32, name=tag, tag=tag, align_bytes=64)[:]
                     nc.sync.dma_start(r, x_view[g, u, :, :, a:b])
@@ -67,10 +67,10 @@ def tile_moe_shr_lin_none_kernel(tc, xT, w_words, w_scales, gate, offs, out):
         nc.sync.dma_start(gate_sb[:], gate)
 
         pairs = [keep.tile([P, 4 * T], BF16, name=f"pairs{g}", align_bytes=64) for g in range(PASSES)]
-        got = [keep.tile([P, 4 * S], BF16, name=f"got{g}", align_bytes=64) for g in range(PASSES)]
-        r_last = keep.tile([P, 4 * S], BF16, name="r_last", align_bytes=64)
+        got = [keep.tile([P, 4 * S], BF16, name=f"got{g}", tag=f"got{g}", align_bytes=64) for g in range(PASSES)]
         x_first = keep.tile([P, 4 * T], BF16, name="x_first", align_bytes=64)
-        x_late = keep.tile([P, 4 * (2 * T + 256 + S)], BF16, name="x_late", tag="raw31", align_bytes=64)
+        behind = keep.tile([P, 4096], BF16, name="behind", tag="got2", align_bytes=64)
+        x_tail = keep.tile([P, 1024], BF16, name="x_tail", align_bytes=64)
         x_codes = [keep.tile([P, T], U32, name=f"x_codes{g}", align_bytes=64) for g in range(PASSES)]
         x_scales = [keep.tile([P, T], U8, name=f"x_scales{g}", align_bytes=64) for g in range(PASSES)]
         r_codes = [keep.tile([P, S], U32, name=f"r_codes{g}", tag=f"r_codes{g}", align_bytes=64) for g in range(PASSES)]
@@ -169,10 +169,14 @@ def tile_moe_shr_lin_none_kernel(tc, xT, w_words, w_scales, gate, offs, out):
             nc.scalar.copy(out=y_sb[1][:], in_=r_bank2[:])
 
         x_last = keep.tile([P, 4 * 512], BF16, name="x_last", tag="r_codes3", align_bytes=64)
-        x_wide = [x_first[:, 0:2048], x_late[:, 0:2048], x_late[:, 4 * T : 4 * T + 2048], x_last[:]]
-        x_rest = [x_first[:, 2048:], x_late[:, 2048 : 4 * T], x_late[:, 4 * T + 2048 : 8 * T], x_late[:, 8 * T : 8 * T + 1024]]
-        r_in = [middle[:, (2 * g + 1) * 2 * T + 384 - 2 * S : (2 * g + 1) * 2 * T + 384].bitcast(BF16) for g in range(2)]
-        r_in = r_in + [x_late[:, 8 * T + 1024 :], r_last[:]]
+
+        def spent(h, words):
+            end = h * 2 * T + 192
+            return middle[:, end - words : end].bitcast(BF16)
+
+        x_wide = [x_first[:, 0:2048], middle[:, 10 * T + 192 : 10 * T + 192 + 1024].bitcast(BF16), behind[:, 0:2048], x_last[:]]
+        x_rest = [x_first[:, 2048:], spent(2, 512), spent(4, 512), x_tail[:]]
+        r_in = [spent(1, 1024), spent(3, 1024), spent(5, 1024), behind[:, 2048:]]
 
         def leave_bank(e):
             if e == 0:
@@ -197,47 +201,54 @@ def tile_moe_shr_lin_none_kernel(tc, xT, w_words, w_scales, gate, offs, out):
         quantize_tokens(0, 512, T)
         gather(1, 0)
         pair_up(on_gpsimd, 1, 1, 384, T)
-        pair_up(on_scalar, 1, 1, 0, 384)
+        pair_up(on_scalar, 1, 1, 0, 192)
+        pair_up(on_scalar, 1, 1, 192, 384)
         gather(1, 1)
         quad_slots(on_scalar, 0, 0, S)
         quantize_slots(0, 0, S)
         pair_up(on_gpsimd, 2, 0, 384, T)
-        pair_up(on_scalar, 2, 0, 0, 384)
+        pair_up(on_scalar, 2, 0, 0, 192)
+        pair_up(on_scalar, 2, 0, 192, 384)
         gather(2, 0)
+        quad_tokens(on_scalar, 1, 512, T)
+        quantize_tokens(1, 512, T)
         pair_up(on_gpsimd, 2, 1, 384, T)
-        pair_up(on_scalar, 2, 1, 0, 384)
+        pair_up(on_scalar, 2, 1, 0, 192)
+        pair_up(on_scalar, 2, 1, 192, 384)
         gather(2, 1)
         quad_slots(on_scalar, 1, 0, S)
         quantize_slots(1, 0, S)
         pair_up(on_gpsimd, 3, 0, 384, T)
-        pair_up(on_scalar, 3, 0, 0, 384)
+        pair_up(on_scalar, 3, 0, 0, 192)
+        pair_up(on_scalar, 3, 0, 192, 384)
         gather(3, 0)
+        quad_tokens(on_scalar, 2, 512, T)
+        quantize_tokens(2, 512, T)
         pair_up(on_gpsimd, 3, 1, 384, T)
-        pair_up(on_scalar, 3, 1, 0, 384)
+        pair_up(on_scalar, 3, 1, 0, 192)
+        pair_up(on_scalar, 3, 1, 192, 384)
         gather(3, 1)
         quad_slots(on_scalar, 2, 0, S)
         quantize_slots(2, 0, S)
-        quad_tokens(on_scalar, 1, 0, 512)
-        quantize_tokens(1, 0, 512)
-        quad_slots(on_vector, 3, 0, S)
-        quantize_slots(3, 0, S)
+        quad_slots(on_vector, 3, 0, 256)
+        quad_slots(on_vector, 3, 256, S)
+        quantize_slots(3, 0, 256)
+        quantize_slots(3, 256, S)
         multiply_slots(0)
         multiply_slots(1)
         multiply_slots(2)
         multiply_slots(3)
-        quad_tokens(on_scalar, 1, 512, T)
-        quantize_tokens(1, 512, T)
+        quad_tokens(on_scalar, 1, 0, 512)
+        quantize_tokens(1, 0, 512)
         multiply_tokens(0)
         multiply_tokens(1)
         quad_tokens(on_scalar, 2, 0, 512)
         quantize_tokens(2, 0, 512)
-        quad_tokens(on_scalar, 2, 512, T)
-        quantize_tokens(2, 512, T)
         multiply_tokens(2)
-        quad_tokens(on_scalar, 3, 512, T)
-        quantize_tokens(3, 512, T)
         leave_bank(0)
         scatter(0)
+        quad_tokens(on_scalar, 3, 512, T)
+        quantize_tokens(3, 512, T)
         quad_tokens(on_scalar, 3, 0, 512)
         quantize_tokens(3, 0, 512)
         multiply_tokens(3)

@@ -55,16 +55,19 @@ def tile_moe_shr_lin_none_kernel(tc, xT, w_words, w_scales, gate, offs, out):
         window = keep.tile([P, T], F32, name="window")
         nc.gpsimd.memset(window[:], 0.0)
 
-        words = keep.tile([P, (E + 1) * PASSES, 2 * N], U8, name="words", align_bytes=64)
+        words = [keep.tile([P, PASSES, 2 * N], U8, name=f"words{e}", align_bytes=64) for e in range(E + 1)]
         s_view = w_scales.rearrange("e a q n -> q (e a) n")
         for q in range(4):
             nc.sync.dma_start(
                 planes[32 * q : 32 * q + 4, :].rearrange("p (m n) -> p m n", n=N).bitcast(I32),
                 s_view[4 * q : 4 * q + 4].bitcast(I32),
             )
-        nc.sync.dma_start(words[:].bitcast(I32), w_words.rearrange("e a p b -> p (e a) b").bitcast(I32))
+        w_view = w_words.rearrange("e a p b -> e p a b").bitcast(I32)
         gate_sb = keep.tile([P, S], F32, name="gate_sb")
+        for e in range(E):
+            nc.sync.dma_start(words[e][:].bitcast(I32), w_view[e])
         nc.sync.dma_start(gate_sb[:], gate)
+        nc.sync.dma_start(words[E][:].bitcast(I32), w_view[E])
 
         pairs = [keep.tile([P, 4 * T], BF16, name=f"pairs{g}", align_bytes=64) for g in range(PASSES)]
         got = [keep.tile([P, 4 * S], BF16, name=f"got{g}", tag=f"got{g}", align_bytes=64) for g in range(PASSES)]
@@ -73,7 +76,14 @@ def tile_moe_shr_lin_none_kernel(tc, xT, w_words, w_scales, gate, offs, out):
         x_tail = keep.tile([P, 1024], BF16, name="x_tail", align_bytes=64)
         x_codes = [keep.tile([P, T], U32, name=f"x_codes{g}", align_bytes=64) for g in range(PASSES)]
         x_scales = [keep.tile([P, T], U8, name=f"x_scales{g}", align_bytes=64) for g in range(PASSES)]
-        r_codes = [keep.tile([P, S], U32, name=f"r_codes{g}", tag=f"r_codes{g}", align_bytes=64) for g in range(PASSES)]
+        r_codes = [keep.tile([P, S], U32, name=f"r_codes{g}", align_bytes=64) for g in range(PASSES - 1)]
+        r_codes_last = [keep.tile([P, C], U32, name=f"r_codes_last{e}", tag=f"r_codes_last{e}", align_bytes=64) for e in range(E)]
+
+        def slot_codes(g, a, b):
+            if g < PASSES - 1:
+                return r_codes[g][:, a:b]
+            return r_codes_last[a // C][:, a % C : a % C + b - a]
+
         r_scales = [keep.tile([P, S], U8, name=f"r_scales{g}", align_bytes=64) for g in range(PASSES)]
         x_bank0 = psum.tile([P, 512], F32, name="x_bank0")
         x_bank1 = psum.tile([P, 256], F32, name="x_bank1")
@@ -123,35 +133,37 @@ def tile_moe_shr_lin_none_kernel(tc, xT, w_words, w_scales, gate, offs, out):
 
         def quantize_slots(g, a, b):
             nc.vector.quantize_mx(
-                out=r_codes[g][:, a:b].bitcast(FP8X4), scales=r_scales[g][:, a:b], in_=r_in[g][:, 4 * a : 4 * b]
+                out=slot_codes(g, a, b).bitcast(FP8X4), scales=r_scales[g][:, a:b], in_=r_in[g][:, 4 * a : 4 * b]
             )
 
         def product(bank, e, g, codes, scales, c, w):
             m = e * PASSES + g
             nc.tensor.matmul_mx(
                 out=bank,
-                lhsT=words[:, m, :].bitcast(FP4X4),
+                lhsT=words[e][:, g, :].bitcast(FP4X4),
                 lhsT_scale=planes[:, m * N : (m + 1) * N],
-                rhs=codes[:, c : c + w].bitcast(FP8X4),
+                rhs=codes.bitcast(FP8X4),
                 rhs_scale=scales[:, c : c + w],
                 start=(g == 0),
                 stop=(g == PASSES - 1),
             )
 
         def multiply_tokens(g):
-            product(x_bank0[:], E, g, x_codes[g], x_scales[g], 0, 512)
-            product(x_bank1[:, 0:128], E, g, x_codes[g], x_scales[g], 512, 128)
+            product(x_bank0[:], E, g, x_codes[g][:, 0:512], x_scales[g], 0, 512)
+            product(x_bank1[:, 0:128], E, g, x_codes[g][:, 512:640], x_scales[g], 512, 128)
             if g == PASSES - 1:
                 for a in range(PASSES):
-                    product(x_bank1[:, 128:256], E, a, x_codes[a], x_scales[a], 640, 128)
+                    product(x_bank1[:, 128:256], E, a, x_codes[a][:, 640:T], x_scales[a], 640, 128)
 
-        def multiply_slots(g):
-            product(r_bank0[:], 0, g, r_codes[g], r_scales[g], 0, 128)
-            product(r_bank1[:], 0, g, r_codes[g], r_scales[g], 128, 128)
-            product(r_bank2[:, 0:128], 1, g, r_codes[g], r_scales[g], 256, 128)
-            if g == PASSES - 1:
-                for a in range(PASSES):
-                    product(r_bank2[:, 128:256], 1, a, r_codes[a], r_scales[a], 384, 128)
+        def multiply_slots(e):
+            if e == 0:
+                for g in range(PASSES):
+                    product(r_bank0[:], 0, g, slot_codes(g, 0, 128), r_scales[g], 0, 128)
+                    product(r_bank1[:], 0, g, slot_codes(g, 128, 256), r_scales[g], 128, 128)
+            else:
+                for half in range(2):
+                    for g in range(PASSES):
+                        product(r_bank2[:, 128 * half : 128 * (half + 1)], 1, g, slot_codes(g, 256 + 128 * half, 384 + 128 * half), r_scales[g], 256 + 128 * half, 128)
 
         y_sb = [keep.tile([P, C], F32, name=f"y_sb{e}") for e in range(E)]
 
@@ -168,7 +180,7 @@ def tile_moe_shr_lin_none_kernel(tc, xT, w_words, w_scales, gate, offs, out):
             nc.scalar.copy(out=y_sb[0][:, 128:256], in_=r_bank1[:])
             nc.scalar.copy(out=y_sb[1][:], in_=r_bank2[:])
 
-        x_last = keep.tile([P, 4 * 512], BF16, name="x_last", tag="r_codes3", align_bytes=64)
+        x_last = keep.tile([P, 4 * 512], BF16, name="x_last", tag="r_codes_last0", align_bytes=64)
 
         def spent(h, words):
             end = h * 2 * T + 192
@@ -236,8 +248,6 @@ def tile_moe_shr_lin_none_kernel(tc, xT, w_words, w_scales, gate, offs, out):
         quantize_slots(3, 256, S)
         multiply_slots(0)
         multiply_slots(1)
-        multiply_slots(2)
-        multiply_slots(3)
         quad_tokens(on_scalar, 1, 0, 512)
         quantize_tokens(1, 0, 512)
         multiply_tokens(0)

@@ -24,17 +24,18 @@ def tile_moe_shr_lin_none_kernel(tc, xT, w_words, w_scales, gate, offs, out):
     nc = tc.nc
     with ExitStack() as ctx:
         keep = ctx.enter_context(tc.tile_pool(name="keep", bufs=1))
+        late = ctx.enter_context(tc.tile_pool(name="late", bufs=1))
         psum = ctx.enter_context(tc.psum_pool(name="psum", bufs=1))
 
         x_view = xT.rearrange("(g p u e) w -> g u p e w", p=P, u=2, e=2)
         offsets = keep.tile([P, S // 16], U16, name="offsets")
         raw = {}
-        middle = keep.tile([P, 6 * 2 * T], F32, name="middle", align_bytes=64)
+        middle = keep.tile([P, 6 * 2 * T + 192], F32, name="middle", align_bytes=64)
         for g in range(PASSES):
             for u in range(2):
                 cuts = 3 if g == u == 0 else 2 if g == 0 or (g, u) == (3, 1) else 1
                 for i in range(cuts):
-                    a, b = i * T // cuts, (i + 1) * T // cuts
+                    a, b = (i * T // cuts, (i + 1) * T // cuts) if g == 0 else ((0, T) if cuts == 1 else ((0, 576), (576, T))[i])
                     tag = f"raw{g}{u}" + "x" * i
                     if g > 0:
                         h = 2 * g + u - 2
@@ -70,9 +71,10 @@ def tile_moe_shr_lin_none_kernel(tc, xT, w_words, w_scales, gate, offs, out):
         nc.sync.dma_start(words[E][:].bitcast(I32), w_view[E])
 
         pairs = [keep.tile([P, 4 * T], BF16, name=f"pairs{g}", align_bytes=64) for g in range(PASSES)]
-        got = [keep.tile([P, 4 * S], BF16, name=f"got{g}", tag=f"got{g}", align_bytes=64) for g in range(PASSES)]
+        got = [keep.tile([P, 4 * S], BF16, name=f"got{g}", align_bytes=64) for g in (0, 1)]
+        got = got + [late.tile([P, 4 * S], BF16, name="got2", align_bytes=64, offset=2048), keep.tile([P, 4 * S], BF16, name="got3", align_bytes=64)]
         x_first = keep.tile([P, 4 * T], BF16, name="x_first", align_bytes=64)
-        behind = keep.tile([P, 4096], BF16, name="behind", tag="got2", align_bytes=64)
+        behind = late.tile([P, 2048], BF16, name="behind", align_bytes=64, offset=4224)
         x_tail = keep.tile([P, 1024], BF16, name="x_tail", align_bytes=64)
         x_codes = [keep.tile([P, T], U32, name=f"x_codes{g}", align_bytes=64) for g in range(PASSES)]
         x_scales = [keep.tile([P, T], U8, name=f"x_scales{g}", align_bytes=64) for g in range(PASSES)]
@@ -85,11 +87,11 @@ def tile_moe_shr_lin_none_kernel(tc, xT, w_words, w_scales, gate, offs, out):
             return r_codes_last[a // C][:, a % C : a % C + b - a]
 
         r_scales = [keep.tile([P, S], U8, name=f"r_scales{g}", align_bytes=64) for g in range(PASSES)]
-        x_bank0 = psum.tile([P, 512], F32, name="x_bank0")
-        x_bank1 = psum.tile([P, 256], F32, name="x_bank1")
-        r_bank0 = psum.tile([P, 128], F32, name="r_bank0")
-        r_bank1 = psum.tile([P, 128], F32, name="r_bank1")
+        r_bank0 = psum.tile([P, 128], F32, name="r_bank0", tag="bank0")
+        r_bank1 = psum.tile([P, 128], F32, name="r_bank1", tag="bank1")
         r_bank2 = psum.tile([P, 256], F32, name="r_bank2")
+        x_bank0 = psum.tile([P, 512], F32, name="x_bank0", tag="bank0")
+        x_bank1 = psum.tile([P, 256], F32, name="x_bank1", tag="bank1")
 
         def gpsimd_cast(out, in_):
             nc.gpsimd.tensor_scalar(out, in_, 1.0, 0.0, MULT, ADD)
@@ -109,6 +111,12 @@ def tile_moe_shr_lin_none_kernel(tc, xT, w_words, w_scales, gate, offs, out):
             )
 
         def quad(engine_copy, dst, src, a, b):
+            if engine_copy is on_gpsimd:
+                engine_copy(
+                    out=dst.rearrange("p (w u e) -> p w u e", u=2, e=2),
+                    in_=src[:].rearrange("p (u w e) -> p w u e", u=2, e=2)[:, a:b],
+                )
+                return
             word = U32 if engine_copy is on_scalar else I32
             engine_copy(
                 out=dst.bitcast(word).rearrange("p (w u) -> p w u", u=2),
@@ -124,16 +132,16 @@ def tile_moe_shr_lin_none_kernel(tc, xT, w_words, w_scales, gate, offs, out):
             quad(engine_copy, token_quads(g, a, b), pairs[g], a, b)
 
         def quad_slots(engine_copy, g, a, b):
-            quad(engine_copy, r_in[g][:, 4 * a : 4 * b], got[g], a, b)
+            quad(engine_copy, slot_quads(g, a, b), got[g], a, b)
 
         def quantize_tokens(g, a, b):
             nc.vector.quantize_mx(
-                out=x_codes[g][:, a:b].bitcast(FP8X4), scales=x_scales[g][:, a:b], in_=token_quads(g, a, b)
+                out=token_codes(g, a, b).bitcast(FP8X4), scales=x_scales[g][:, a:b], in_=token_quads(g, a, b)
             )
 
         def quantize_slots(g, a, b):
             nc.vector.quantize_mx(
-                out=slot_codes(g, a, b).bitcast(FP8X4), scales=r_scales[g][:, a:b], in_=r_in[g][:, 4 * a : 4 * b]
+                out=slot_codes(g, a, b).bitcast(FP8X4), scales=r_scales[g][:, a:b], in_=slot_quads(g, a, b)
             )
 
         def product(bank, e, g, codes, scales, c, w):
@@ -149,11 +157,11 @@ def tile_moe_shr_lin_none_kernel(tc, xT, w_words, w_scales, gate, offs, out):
             )
 
         def multiply_tokens(g):
-            product(x_bank0[:], E, g, x_codes[g][:, 0:512], x_scales[g], 0, 512)
-            product(x_bank1[:, 0:128], E, g, x_codes[g][:, 512:640], x_scales[g], 512, 128)
+            product(x_bank0[:], E, g, token_codes(g, 0, 512), x_scales[g], 0, 512)
+            product(x_bank1[:, 0:128], E, g, token_codes(g, 512, 640), x_scales[g], 512, 128)
             if g == PASSES - 1:
                 for a in range(PASSES):
-                    product(x_bank1[:, 128:256], E, a, x_codes[a][:, 640:T], x_scales[a], 640, 128)
+                    product(x_bank1[:, 128:256], E, a, token_codes(a, 640, T), x_scales[a], 640, 128)
 
         def multiply_slots(e):
             if e == 0:
@@ -187,8 +195,21 @@ def tile_moe_shr_lin_none_kernel(tc, xT, w_words, w_scales, gate, offs, out):
             return middle[:, end - words : end].bitcast(BF16)
 
         x_wide = [x_first[:, 0:2048], middle[:, 10 * T + 192 : 10 * T + 192 + 1024].bitcast(BF16), behind[:, 0:2048], x_last[:]]
-        x_rest = [x_first[:, 2048:], spent(2, 512), spent(4, 512), x_tail[:]]
-        r_in = [spent(1, 1024), spent(3, 1024), spent(5, 1024), behind[:, 2048:]]
+        x_rest = [x_first[:, 2048:], spent(2, 512), middle[:, 10 * T + 1216 :].bitcast(BF16), x_tail[:]]
+        r_in = [spent(1, 1024), spent(3, 1024), spent(5, 1024)]
+        r_last = [late.tile([P, 4 * C], BF16, name="r_last0", align_bytes=64, offset=128), keep.tile([P, 4 * C], BF16, name="r_last1", align_bytes=64)]
+        x_codes_rest = {g: late.tile([P, 256], U32, name=f"x_codes_rest{g}", align_bytes=64, offset=1152 + 1024 * g) for g in (1, 2)}
+
+        def slot_quads(g, a, b):
+            if g < PASSES - 1:
+                return r_in[g][:, 4 * a : 4 * b]
+            return r_last[a // C][:]
+
+        def token_codes(g, a, b):
+            if g in x_codes_rest and a >= 512:
+                return x_codes_rest[g][:, a - 512 : b - 512]
+            return x_codes[g][:, a:b]
+
 
         def leave_bank(e):
             if e == 0:
@@ -205,12 +226,12 @@ def tile_moe_shr_lin_none_kernel(tc, xT, w_words, w_scales, gate, offs, out):
         pair_up(on_vector, 0, 1, 384, T)
         gather(0, 1)
         quad_tokens(on_scalar, 0, 0, 384)
-        quad_tokens(on_scalar, 0, 384, 512)
         quad_tokens(on_scalar, 0, 512, T)
-        quantize_tokens(0, 0, 512)
-        pair_up(on_scalar, 1, 0, 0, 512)
-        pair_up(on_vector, 1, 0, 512, T)
+        quad_tokens(on_scalar, 0, 384, 512)
         quantize_tokens(0, 512, T)
+        quantize_tokens(0, 0, 512)
+        pair_up(on_gpsimd, 1, 0, 576, T)
+        pair_up(on_scalar, 1, 0, 0, 576)
         gather(1, 0)
         pair_up(on_gpsimd, 1, 1, 384, T)
         pair_up(on_scalar, 1, 1, 0, 192)
@@ -223,42 +244,44 @@ def tile_moe_shr_lin_none_kernel(tc, xT, w_words, w_scales, gate, offs, out):
         pair_up(on_scalar, 2, 0, 192, 384)
         gather(2, 0)
         quad_tokens(on_scalar, 1, 512, T)
-        quantize_tokens(1, 512, T)
-        pair_up(on_gpsimd, 2, 1, 384, T)
+        quad_slots(on_gpsimd, 1, 0, 64)
+        pair_up(on_gpsimd, 2, 1, 576, T)
         pair_up(on_scalar, 2, 1, 0, 192)
-        pair_up(on_scalar, 2, 1, 192, 384)
+        pair_up(on_scalar, 2, 1, 192, 576)
         gather(2, 1)
-        quad_slots(on_scalar, 1, 0, S)
+        quad_slots(on_scalar, 1, 64, S)
         quantize_slots(1, 0, S)
         pair_up(on_gpsimd, 3, 0, 384, T)
         pair_up(on_scalar, 3, 0, 0, 192)
         pair_up(on_scalar, 3, 0, 192, 384)
         gather(3, 0)
-        quad_tokens(on_scalar, 2, 512, T)
-        quantize_tokens(2, 512, T)
-        pair_up(on_gpsimd, 3, 1, 384, T)
+        quad_slots(on_gpsimd, 2, 0, 64)
+        pair_up(on_gpsimd, 3, 1, 576, T)
         pair_up(on_scalar, 3, 1, 0, 192)
-        pair_up(on_scalar, 3, 1, 192, 384)
+        pair_up(on_scalar, 3, 1, 192, 576)
         gather(3, 1)
-        quad_slots(on_scalar, 2, 0, S)
+        quad_slots(on_scalar, 2, 64, S)
         quantize_slots(2, 0, S)
         quad_slots(on_vector, 3, 0, 256)
-        quad_slots(on_vector, 3, 256, S)
+        quantize_tokens(1, 512, T)
         quantize_slots(3, 0, 256)
-        quantize_slots(3, 256, S)
-        multiply_slots(0)
-        multiply_slots(1)
+        quad_tokens(on_scalar, 2, 512, T)
+        quantize_tokens(2, 512, T)
         quad_tokens(on_scalar, 1, 0, 512)
         quantize_tokens(1, 0, 512)
-        multiply_tokens(0)
-        multiply_tokens(1)
+        quad_slots(on_scalar, 3, 256, S)
+        quantize_slots(3, 256, S)
         quad_tokens(on_scalar, 2, 0, 512)
         quantize_tokens(2, 0, 512)
-        multiply_tokens(2)
-        leave_bank(0)
-        scatter(0)
+        multiply_slots(0)
+        multiply_slots(1)
         quad_tokens(on_scalar, 3, 512, T)
         quantize_tokens(3, 512, T)
+        leave_bank(0)
+        scatter(0)
+        multiply_tokens(0)
+        multiply_tokens(1)
+        multiply_tokens(2)
         quad_tokens(on_scalar, 3, 0, 512)
         quantize_tokens(3, 0, 512)
         multiply_tokens(3)

@@ -17,7 +17,19 @@ P = 128
 K, T, E, C, N = 2048, 768, 2, 256, 128
 S = E * C
 PASSES = K // 512
+LAST = PASSES - 1
 FLOPS = 2 * K * N * (T + S)
+
+ROWS = 2 * T
+WIDE = 512
+NARROW = T - WIDE
+GROUP = 128
+
+CUT_WHOLE_GATHER = 384
+CUT_AFTER_LEAD = 544
+CUT_LATE_LOAD = 576
+LEAD_SLOTS = 32
+FRONT = 192
 
 
 def tile_moe_shr_lin_none_kernel(tc, xT, w_words, w_scales, gate, offs, out):
@@ -29,151 +41,196 @@ def tile_moe_shr_lin_none_kernel(tc, xT, w_words, w_scales, gate, offs, out):
 
         x_view = xT.rearrange("(g p u e) w -> g u p e w", p=P, u=2, e=2)
         offsets = keep.tile([P, S // 16], U16, name="offsets")
-        raw = {}
-        middle = keep.tile([P, 6 * 2 * T + 192], F32, name="middle", align_bytes=64)
+        stream = keep.tile([P, 2 * LAST * ROWS + FRONT], F32, name="stream", align_bytes=64)
+
+        def stream_start(g, u):
+            return (2 * (g - 1) + u) * ROWS
+
+        cuts = {(0, 0): (0, T // 3, 2 * T // 3, T), (0, 1): (0, T // 2, T), (LAST, 1): (0, CUT_AFTER_LEAD, T)}
+        loaded = {}
         for g in range(PASSES):
             for u in range(2):
-                cuts = 3 if g == u == 0 else 2 if g == 0 or (g, u) == (3, 1) else 1
-                for i in range(cuts):
-                    a, b = (i * T // cuts, (i + 1) * T // cuts) if g == 0 else ((0, T) if cuts == 1 else ((0, 576), (576, T))[i])
-                    tag = f"raw{g}{u}" + "x" * i
-                    if g > 0:
-                        h = 2 * g + u - 2
-                        r = middle[:, h * 2 * T : (h + 1) * 2 * T].rearrange("p (e w) -> p e w", e=2)[:, :, a:b]
+                edges = cuts.get((g, u), (0, T))
+                for a, b in zip(edges, edges[1:]):
+                    if g == 0:
+                        piece = keep.tile([P, 2, b - a], F32, name=f"first{u}_{a}", align_bytes=64)[:]
                     else:
-                        r = keep.tile([P, 2, b - a], F32, name=tag, tag=tag, align_bytes=64)[:]
-                    nc.sync.dma_start(r, x_view[g, u, :, :, a:b])
-                    raw[g, u, a] = r
+                        both_rows = stream[:, stream_start(g, u) : stream_start(g, u) + ROWS]
+                        piece = both_rows.rearrange("p (e w) -> p e w", e=2)[:, :, a:b]
+                    nc.sync.dma_start(piece, x_view[g, u, :, :, a:b])
+                    loaded[g, u, a] = piece
                 if g == u == 0:
                     nc.sync.dma_start(offsets[:], offs)
 
         def rows(g, u, a, b):
-            first = max(c for (i, j, c) in raw if (i, j) == (g, u) and c <= a)
-            return raw[g, u, first][:, :, a - first : b - first]
+            first = max(c for (i, j, c) in loaded if (i, j) == (g, u) and c <= a)
+            return loaded[g, u, first][:, :, a - first : b - first]
 
-        planes = keep.tile([P, (E + 1) * PASSES * N], U8, name="planes", align_bytes=64)
-        nc.gpsimd.memset(planes[:].bitcast(I32), 0)
+        w_planes = keep.tile([P, (E + 1) * PASSES * N], U8, name="w_planes", align_bytes=64)
+        nc.gpsimd.memset(w_planes[:].bitcast(I32), 0)
         window = keep.tile([P, T], F32, name="window")
         nc.gpsimd.memset(window[:], 0.0)
 
-        words = [keep.tile([P, PASSES, 2 * N], U8, name=f"words{e}", align_bytes=64) for e in range(E + 1)]
-        s_view = w_scales.rearrange("e a q n -> q (e a) n")
-        for q in range(4):
+        w_codes = [keep.tile([P, PASSES, 2 * N], U8, name=f"w_codes{e}", align_bytes=64) for e in range(E + 1)]
+        scale_rows = w_scales.rearrange("e a q n -> q (e a) n")
+        for quadrant in range(4):
             nc.sync.dma_start(
-                planes[32 * q : 32 * q + 4, :].rearrange("p (m n) -> p m n", n=N).bitcast(I32),
-                s_view[4 * q : 4 * q + 4].bitcast(I32),
+                w_planes[32 * quadrant : 32 * quadrant + 4, :].rearrange("p (m n) -> p m n", n=N).bitcast(I32),
+                scale_rows[4 * quadrant : 4 * quadrant + 4].bitcast(I32),
             )
         w_view = w_words.rearrange("e a p b -> e p a b").bitcast(I32)
         gate_sb = keep.tile([P, S], F32, name="gate_sb")
         for e in range(E):
-            nc.sync.dma_start(words[e][:].bitcast(I32), w_view[e])
+            nc.sync.dma_start(w_codes[e][:].bitcast(I32), w_view[e])
         nc.sync.dma_start(gate_sb[:], gate)
-        nc.sync.dma_start(words[E][:].bitcast(I32), w_view[E])
+        nc.sync.dma_start(w_codes[E][:].bitcast(I32), w_view[E])
 
-        pairs = [keep.tile([P, 4 * T], BF16, name=f"pairs{g}", align_bytes=64) for g in range(PASSES)]
-        got = [keep.tile([P, 4 * S], BF16, name=f"got{g}", align_bytes=64) for g in (0, 1)]
-        got = got + [late.tile([P, 4 * S], BF16, name="got2", align_bytes=64, offset=2048), keep.tile([P, 4 * S], BF16, name="got3", align_bytes=64)]
-        x_first = keep.tile([P, 4 * T], BF16, name="x_first", align_bytes=64)
-        behind = late.tile([P, 2048], BF16, name="behind", align_bytes=64, offset=4224)
-        x_tail = keep.tile([P, 1024], BF16, name="x_tail", align_bytes=64)
-        x_codes = [keep.tile([P, T], U32, name=f"x_codes{g}", align_bytes=64) for g in range(PASSES)]
-        x_scales = [keep.tile([P, T], U8, name=f"x_scales{g}", align_bytes=64) for g in range(PASSES)]
-        r_codes = [keep.tile([P, S], U32, name=f"r_codes{g}", align_bytes=64) for g in range(PASSES - 1)]
-        r_codes_last = [keep.tile([P, C], U32, name=f"r_codes_last{e}", tag=f"r_codes_last{e}", align_bytes=64) for e in range(E)]
+        late_pairs_at = 8 * C
+        late_slot_quads_at = 128
+        late_codes_at = late_slot_quads_at + 8 * C
+        late_token_quads_at = late_codes_at + 2 * 4 * NARROW
+        token_pairs = [keep.tile([P, 4 * T], BF16, name=f"token_pairs{g}", align_bytes=64) for g in range(PASSES)]
+        slot_pairs = [
+            keep.tile([P, 4 * S], BF16, name="slot_pairs0", align_bytes=64),
+            keep.tile([P, 4 * S], BF16, name="slot_pairs1", align_bytes=64),
+            late.tile([P, 4 * S], BF16, name="slot_pairs2", align_bytes=64, offset=late_pairs_at),
+            keep.tile([P, 4 * S], BF16, name="slot_pairs3", align_bytes=64),
+        ]
+        quads_pass0 = keep.tile([P, 4 * T], BF16, name="quads_pass0", align_bytes=64)
+        wide_quads_pass2 = late.tile([P, 4 * WIDE], BF16, name="wide_quads_pass2", align_bytes=64, offset=late_token_quads_at)
+        narrow_quads_pass3 = keep.tile([P, 4 * NARROW], BF16, name="narrow_quads_pass3", align_bytes=64)
+        token_codes = [keep.tile([P, T], U32, name=f"token_codes{g}", align_bytes=64) for g in range(PASSES)]
+        token_scales = [keep.tile([P, T], U8, name=f"token_scales{g}", align_bytes=64) for g in range(PASSES)]
+        slot_codes = [keep.tile([P, S], U32, name=f"slot_codes{g}", align_bytes=64) for g in range(LAST)]
+        last_slot_codes = [
+            keep.tile([P, C], U32, name=f"last_slot_codes{e}", tag=f"last_slot_codes{e}", align_bytes=64) for e in range(E)
+        ]
+        slot_scales = [keep.tile([P, S], U8, name=f"slot_scales{g}", align_bytes=64) for g in range(PASSES)]
 
-        def slot_codes(g, a, b):
-            if g < PASSES - 1:
-                return r_codes[g][:, a:b]
-            return r_codes_last[a // C][:, a % C : a % C + b - a]
+        expert0_banks = [psum.tile([P, GROUP], F32, name=f"expert0_bank{i}", tag=f"bank{i}") for i in range(2)]
+        expert1_bank = psum.tile([P, C], F32, name="expert1_bank")
+        wide_bank = psum.tile([P, WIDE], F32, name="wide_bank", tag="bank0")
+        narrow_bank = psum.tile([P, NARROW], F32, name="narrow_bank", tag="bank1")
+        y_sb = [keep.tile([P, C], F32, name=f"y_sb{e}") for e in range(E)]
 
-        r_scales = [keep.tile([P, S], U8, name=f"r_scales{g}", align_bytes=64) for g in range(PASSES)]
-        r_bank0 = psum.tile([P, 128], F32, name="r_bank0", tag="bank0")
-        r_bank1 = psum.tile([P, 128], F32, name="r_bank1", tag="bank1")
-        r_bank2 = psum.tile([P, 256], F32, name="r_bank2")
-        x_bank0 = psum.tile([P, 512], F32, name="x_bank0", tag="bank0")
-        x_bank1 = psum.tile([P, 256], F32, name="x_bank1", tag="bank1")
+        wide_quads_pass3 = keep.tile([P, 4 * WIDE], BF16, name="wide_quads_pass3", tag="last_slot_codes0", align_bytes=64)
 
-        def gpsimd_cast(out, in_):
+        def ending_in_front(g, u, columns):
+            end = stream_start(g, u) + FRONT
+            return stream[:, end - 2 * columns : end].bitcast(BF16)
+
+        after_front = stream_start(LAST, 1) + FRONT
+        wide_quads = [
+            quads_pass0[:, 0 : 4 * WIDE],
+            stream[:, after_front : after_front + 2 * WIDE].bitcast(BF16),
+            wide_quads_pass2[:],
+            wide_quads_pass3[:],
+        ]
+        narrow_quads = [
+            quads_pass0[:, 4 * WIDE :],
+            ending_in_front(2, 0, NARROW),
+            stream[:, after_front + 2 * WIDE :].bitcast(BF16),
+            narrow_quads_pass3[:],
+        ]
+        slot_quads = [ending_in_front(g + 1, 1, S) for g in range(LAST)]
+        last_slot_quads = [
+            late.tile([P, 4 * C], BF16, name="last_slot_quads0", align_bytes=64, offset=late_slot_quads_at),
+            keep.tile([P, 4 * C], BF16, name="last_slot_quads1", align_bytes=64),
+        ]
+        held_codes = {
+            g: late.tile([P, NARROW], U32, name=f"held_codes{g}", align_bytes=64, offset=late_codes_at + 4 * NARROW * (g - 1))
+            for g in (1, 2)
+        }
+
+        def token_quads_of(g, a, b):
+            if a < WIDE:
+                return wide_quads[g][:, 4 * a : 4 * b]
+            return narrow_quads[g][:, 4 * (a - WIDE) : 4 * (b - WIDE)]
+
+        def token_codes_of(g, a, b):
+            if g in held_codes and a >= WIDE:
+                return held_codes[g][:, a - WIDE : b - WIDE]
+            return token_codes[g][:, a:b]
+
+        def slot_quads_of(g, a, b):
+            if g < LAST:
+                return slot_quads[g][:, 4 * a : 4 * b]
+            return last_slot_quads[a // C][:]
+
+        def slot_codes_of(g, a, b):
+            if g < LAST:
+                return slot_codes[g][:, a:b]
+            return last_slot_codes[a // C][:, a % C : a % C + b - a]
+
+        def gpsimd_values(out, in_):
             nc.gpsimd.tensor_scalar(out, in_, 1.0, 0.0, MULT, ADD)
 
-        on_scalar, on_vector, on_gpsimd = nc.scalar.copy, nc.vector.tensor_copy, gpsimd_cast
-
-        def pair_up(engine_copy, g, u, a, b):
-            engine_copy(
-                out=pairs[g][:, 2 * (u * T + a) : 2 * (u * T + b)].rearrange("p (w e) -> p w e", e=2),
+        def cast(copy, g, u, a, b):
+            copy(
+                out=token_pairs[g][:, 2 * (u * T + a) : 2 * (u * T + b)].rearrange("p (w e) -> p w e", e=2),
                 in_=rows(g, u, a, b).rearrange("p e w -> p w e"),
             )
 
+        def shared_cast(g, u, cut):
+            cast(gpsimd_values, g, u, cut, T)
+            cast(nc.scalar.copy, g, u, 0, FRONT)
+            cast(nc.scalar.copy, g, u, FRONT, cut)
+
         def gather(g, u):
             nc.vector.tensor_copy(
-                got[g][:, 2 * u * S : 2 * (u + 1) * S].bitcast(U32),
-                pairs[g][:, 2 * u * T : 2 * (u + 1) * T].bitcast(U32).indirect(offsets[:]),
+                slot_pairs[g][:, 2 * u * S : 2 * (u + 1) * S].bitcast(U32),
+                token_pairs[g][:, 2 * u * T : 2 * (u + 1) * T].bitcast(U32).indirect(offsets[:]),
             )
 
-        def quad(engine_copy, dst, src, a, b):
-            if engine_copy is on_gpsimd:
-                engine_copy(
-                    out=dst.rearrange("p (w u e) -> p w u e", u=2, e=2),
-                    in_=src[:].rearrange("p (u w e) -> p w u e", u=2, e=2)[:, a:b],
-                )
-                return
-            word = U32 if engine_copy is on_scalar else I32
-            engine_copy(
-                out=dst.bitcast(word).rearrange("p (w u) -> p w u", u=2),
-                in_=src[:].bitcast(word).rearrange("p (u w) -> p w u", u=2)[:, a:b],
+        def copy_pairs(copy, word, quads, pairs, a, b):
+            copy(
+                out=quads.bitcast(word).rearrange("p (w u) -> p w u", u=2),
+                in_=pairs[:].bitcast(word).rearrange("p (u w) -> p w u", u=2)[:, a:b],
             )
 
-        def token_quads(g, a, b):
-            if a < 512:
-                return x_wide[g][:, 4 * a : 4 * b]
-            return x_rest[g][:, 4 * (a - 512) : 4 * (b - 512)]
+        def token_quads_on_scalar(g, a, b):
+            copy_pairs(nc.scalar.copy, U32, token_quads_of(g, a, b), token_pairs[g], a, b)
 
-        def quad_tokens(engine_copy, g, a, b):
-            quad(engine_copy, token_quads(g, a, b), pairs[g], a, b)
+        def slot_quads_on_scalar(g, a, b):
+            copy_pairs(nc.scalar.copy, U32, slot_quads_of(g, a, b), slot_pairs[g], a, b)
 
-        def quad_slots(engine_copy, g, a, b):
-            quad(engine_copy, slot_quads(g, a, b), got[g], a, b)
+        def lead_slot_quads(g):
+            gpsimd_values(
+                out=slot_quads_of(g, 0, LEAD_SLOTS).rearrange("p (w u e) -> p w u e", u=2, e=2),
+                in_=slot_pairs[g][:].rearrange("p (u w e) -> p w u e", u=2, e=2)[:, 0:LEAD_SLOTS],
+            )
 
         def quantize_tokens(g, a, b):
             nc.vector.quantize_mx(
-                out=token_codes(g, a, b).bitcast(FP8X4), scales=x_scales[g][:, a:b], in_=token_quads(g, a, b)
+                out=token_codes_of(g, a, b).bitcast(FP8X4), scales=token_scales[g][:, a:b], in_=token_quads_of(g, a, b)
             )
 
         def quantize_slots(g, a, b):
             nc.vector.quantize_mx(
-                out=slot_codes(g, a, b).bitcast(FP8X4), scales=r_scales[g][:, a:b], in_=slot_quads(g, a, b)
+                out=slot_codes_of(g, a, b).bitcast(FP8X4), scales=slot_scales[g][:, a:b], in_=slot_quads_of(g, a, b)
             )
 
-        def product(bank, e, g, codes, scales, c, w):
-            m = e * PASSES + g
+        def product(bank, e, g, codes, scales):
+            plane = e * PASSES + g
             nc.tensor.matmul_mx(
                 out=bank,
-                lhsT=words[e][:, g, :].bitcast(FP4X4),
-                lhsT_scale=planes[:, m * N : (m + 1) * N],
+                lhsT=w_codes[e][:, g, :].bitcast(FP4X4),
+                lhsT_scale=w_planes[:, plane * N : (plane + 1) * N],
                 rhs=codes.bitcast(FP8X4),
-                rhs_scale=scales[:, c : c + w],
+                rhs_scale=scales,
                 start=(g == 0),
-                stop=(g == PASSES - 1),
+                stop=(g == LAST),
             )
 
-        def multiply_tokens(g):
-            product(x_bank0[:], E, g, token_codes(g, 0, 512), x_scales[g], 0, 512)
-            product(x_bank1[:, 0:128], E, g, token_codes(g, 512, 640), x_scales[g], 512, 128)
-            if g == PASSES - 1:
-                for a in range(PASSES):
-                    product(x_bank1[:, 128:256], E, a, token_codes(a, 640, T), x_scales[a], 640, 128)
+        def slot_product(bank, g, a):
+            product(bank, a // C, g, slot_codes_of(g, a, a + GROUP), slot_scales[g][:, a : a + GROUP])
 
-        def multiply_slots(e):
-            if e == 0:
-                for g in range(PASSES):
-                    product(r_bank0[:], 0, g, slot_codes(g, 0, 128), r_scales[g], 0, 128)
-                    product(r_bank1[:], 0, g, slot_codes(g, 128, 256), r_scales[g], 128, 128)
-            else:
-                for half in range(2):
-                    for g in range(PASSES):
-                        product(r_bank2[:, 128 * half : 128 * (half + 1)], 1, g, slot_codes(g, 256 + 128 * half, 384 + 128 * half), r_scales[g], 256 + 128 * half, 128)
+        def token_product(bank, g, a, b):
+            product(bank, E, g, token_codes_of(g, a, b), token_scales[g][:, a:b])
 
-        y_sb = [keep.tile([P, C], F32, name=f"y_sb{e}") for e in range(E)]
+        def token_products(g):
+            token_product(wide_bank[:], g, 0, WIDE)
+            token_product(narrow_bank[:, 0:GROUP], g, WIDE, WIDE + GROUP)
 
         def scatter(e):
             nc.vector.tensor_tensor(
@@ -183,113 +240,72 @@ def tile_moe_shr_lin_none_kernel(tc, xT, w_words, w_scales, gate, offs, out):
                 MULT,
             )
 
-        def leave_banks():
-            nc.scalar.copy(out=y_sb[0][:, 0:128], in_=r_bank0[:])
-            nc.scalar.copy(out=y_sb[0][:, 128:256], in_=r_bank1[:])
-            nc.scalar.copy(out=y_sb[1][:], in_=r_bank2[:])
-
-        x_last = keep.tile([P, 4 * 512], BF16, name="x_last", tag="r_codes_last0", align_bytes=64)
-
-        def spent(h, words):
-            end = h * 2 * T + 192
-            return middle[:, end - words : end].bitcast(BF16)
-
-        x_wide = [x_first[:, 0:2048], middle[:, 10 * T + 192 : 10 * T + 192 + 1024].bitcast(BF16), behind[:, 0:2048], x_last[:]]
-        x_rest = [x_first[:, 2048:], spent(2, 512), middle[:, 10 * T + 1216 :].bitcast(BF16), x_tail[:]]
-        r_in = [spent(1, 1024), spent(3, 1024), spent(5, 1024)]
-        r_last = [late.tile([P, 4 * C], BF16, name="r_last0", align_bytes=64, offset=128), keep.tile([P, 4 * C], BF16, name="r_last1", align_bytes=64)]
-        x_codes_rest = {g: late.tile([P, 256], U32, name=f"x_codes_rest{g}", align_bytes=64, offset=1152 + 1024 * g) for g in (1, 2)}
-
-        def slot_quads(g, a, b):
-            if g < PASSES - 1:
-                return r_in[g][:, 4 * a : 4 * b]
-            return r_last[a // C][:]
-
-        def token_codes(g, a, b):
-            if g in x_codes_rest and a >= 512:
-                return x_codes_rest[g][:, a - 512 : b - 512]
-            return x_codes[g][:, a:b]
-
-
-        def leave_bank(e):
-            if e == 0:
-                nc.scalar.copy(out=y_sb[0][:, 0:128], in_=r_bank0[:])
-                nc.scalar.copy(out=y_sb[0][:, 128:256], in_=r_bank1[:])
-            else:
-                nc.scalar.copy(out=y_sb[1][:], in_=r_bank2[:])
-
-        pair_up(on_scalar, 0, 0, 0, 256)
-        pair_up(on_vector, 0, 0, 256, 512)
-        pair_up(on_vector, 0, 0, 512, T)
-        pair_up(on_scalar, 0, 1, 0, 384)
+        cast(nc.scalar.copy, 0, 0, 0, T // 3)
+        cast(nc.vector.tensor_copy, 0, 0, T // 3, 2 * T // 3)
+        cast(nc.vector.tensor_copy, 0, 0, 2 * T // 3, T)
+        cast(nc.scalar.copy, 0, 1, 0, T // 2)
         gather(0, 0)
-        pair_up(on_vector, 0, 1, 384, T)
+        cast(nc.vector.tensor_copy, 0, 1, T // 2, T)
         gather(0, 1)
-        quad_tokens(on_scalar, 0, 0, 384)
-        quad_tokens(on_scalar, 0, 512, T)
-        quad_tokens(on_scalar, 0, 384, 512)
-        quantize_tokens(0, 512, T)
-        quantize_tokens(0, 0, 512)
-        pair_up(on_gpsimd, 1, 0, 576, T)
-        pair_up(on_scalar, 1, 0, 0, 576)
+        token_quads_on_scalar(0, 0, T // 2)
+        token_quads_on_scalar(0, WIDE, T)
+        token_quads_on_scalar(0, T // 2, WIDE)
+        quantize_tokens(0, WIDE, T)
+        quantize_tokens(0, 0, WIDE)
+
+        cast(gpsimd_values, 1, 0, CUT_LATE_LOAD, T)
+        cast(nc.scalar.copy, 1, 0, 0, CUT_LATE_LOAD)
         gather(1, 0)
-        pair_up(on_gpsimd, 1, 1, 384, T)
-        pair_up(on_scalar, 1, 1, 0, 192)
-        pair_up(on_scalar, 1, 1, 192, 384)
+        shared_cast(1, 1, CUT_WHOLE_GATHER)
         gather(1, 1)
-        quad_slots(on_scalar, 0, 0, S)
+        slot_quads_on_scalar(0, 0, S)
         quantize_slots(0, 0, S)
-        pair_up(on_gpsimd, 2, 0, 384, T)
-        pair_up(on_scalar, 2, 0, 0, 192)
-        pair_up(on_scalar, 2, 0, 192, 384)
-        gather(2, 0)
-        quad_tokens(on_scalar, 1, 512, T)
-        quad_slots(on_gpsimd, 1, 0, 64)
-        pair_up(on_gpsimd, 2, 1, 576, T)
-        pair_up(on_scalar, 2, 1, 0, 192)
-        pair_up(on_scalar, 2, 1, 192, 576)
-        gather(2, 1)
-        quad_slots(on_scalar, 1, 64, S)
-        quantize_slots(1, 0, S)
-        pair_up(on_gpsimd, 3, 0, 384, T)
-        pair_up(on_scalar, 3, 0, 0, 192)
-        pair_up(on_scalar, 3, 0, 192, 384)
-        gather(3, 0)
-        quad_slots(on_gpsimd, 2, 0, 64)
-        pair_up(on_gpsimd, 3, 1, 576, T)
-        pair_up(on_scalar, 3, 1, 0, 192)
-        pair_up(on_scalar, 3, 1, 192, 576)
-        gather(3, 1)
-        quad_slots(on_scalar, 2, 64, S)
-        quantize_slots(2, 0, S)
-        quad_slots(on_vector, 3, 0, 256)
-        quantize_tokens(1, 512, T)
-        quantize_slots(3, 0, 256)
-        quad_tokens(on_scalar, 2, 512, T)
-        quantize_tokens(2, 512, T)
-        quad_tokens(on_scalar, 1, 0, 512)
-        quantize_tokens(1, 0, 512)
-        quad_slots(on_scalar, 3, 256, S)
-        quantize_slots(3, 256, S)
-        quad_tokens(on_scalar, 2, 0, 512)
-        quantize_tokens(2, 0, 512)
-        multiply_slots(0)
-        multiply_slots(1)
-        quad_tokens(on_scalar, 3, 512, T)
-        quantize_tokens(3, 512, T)
-        leave_bank(0)
+
+        for g in (2, 3):
+            shared_cast(g, 0, CUT_WHOLE_GATHER)
+            gather(g, 0)
+            if g == 2:
+                token_quads_on_scalar(1, WIDE, T)
+            lead_slot_quads(g - 1)
+            shared_cast(g, 1, CUT_AFTER_LEAD)
+            gather(g, 1)
+            slot_quads_on_scalar(g - 1, LEAD_SLOTS, S)
+            quantize_slots(g - 1, 0, S)
+
+        copy_pairs(nc.vector.tensor_copy, I32, slot_quads_of(LAST, 0, C), slot_pairs[LAST], 0, C)
+        quantize_tokens(1, WIDE, T)
+        quantize_slots(LAST, 0, C)
+        token_quads_on_scalar(2, WIDE, T)
+        quantize_tokens(2, WIDE, T)
+        token_quads_on_scalar(1, 0, WIDE)
+        quantize_tokens(1, 0, WIDE)
+        slot_quads_on_scalar(LAST, C, S)
+        quantize_slots(LAST, C, S)
+        token_quads_on_scalar(2, 0, WIDE)
+        quantize_tokens(2, 0, WIDE)
+        for g in range(PASSES):
+            for i in range(2):
+                slot_product(expert0_banks[i][:], g, GROUP * i)
+        for i in range(2):
+            for g in range(PASSES):
+                slot_product(expert1_bank[:, GROUP * i : GROUP * (i + 1)], g, C + GROUP * i)
+        copy_pairs(nc.gpsimd.tensor_copy, I32, token_quads_of(LAST, WIDE, T), token_pairs[LAST], WIDE, T)
+        quantize_tokens(LAST, WIDE, T)
+
+        for i in range(2):
+            nc.scalar.copy(out=y_sb[0][:, GROUP * i : GROUP * (i + 1)], in_=expert0_banks[i][:])
         scatter(0)
-        multiply_tokens(0)
-        multiply_tokens(1)
-        multiply_tokens(2)
-        quad_tokens(on_scalar, 3, 0, 512)
-        quantize_tokens(3, 0, 512)
-        multiply_tokens(3)
-        leave_bank(1)
+        for g in range(LAST):
+            token_products(g)
+        token_quads_on_scalar(LAST, 0, WIDE)
+        quantize_tokens(LAST, 0, WIDE)
+        token_products(LAST)
+        for g in range(PASSES):
+            token_product(narrow_bank[:, GROUP:NARROW], g, WIDE + GROUP, T)
+        nc.scalar.copy(out=y_sb[1][:], in_=expert1_bank[:])
         scatter(1)
 
         result = keep.tile([P, T], F32, name="result")
-        nc.vector.tensor_tensor(result[:, 0:512], x_bank0[:], window[:, 0:512], ADD)
-        nc.sync.dma_start(out[:, 0:512], result[:, 0:512])
-        nc.vector.tensor_tensor(result[:, 512:T], x_bank1[:], window[:, 512:T], ADD)
-        nc.sync.dma_start(out[:, 512:T], result[:, 512:T])
+        for bank, a, b in ((wide_bank, 0, WIDE), (narrow_bank, WIDE, T)):
+            nc.vector.tensor_tensor(result[:, a:b], bank[:], window[:, a:b], ADD)
+            nc.sync.dma_start(out[:, a:b], result[:, a:b])

@@ -21,15 +21,11 @@ LAST = PASSES - 1
 FLOPS = 2 * K * N * (T + S)
 
 ROWS = 2 * T
-WIDE = 512
-NARROW = T - WIDE
+NARROW = 256
+WIDE = T - NARROW
 GROUP = 128
-
-CUT_WHOLE_GATHER = 384
-CUT_AFTER_LEAD = 544
-CUT_LATE_LOAD = 576
-LEAD_SLOTS = 32
-FRONT = 192
+HOLD = 16
+SHARE = {1: 192, 2: 192, 3: 224}
 
 
 def tile_moe_shr_lin_none_kernel(tc, xT, w_words, w_scales, gate, offs, out):
@@ -41,22 +37,20 @@ def tile_moe_shr_lin_none_kernel(tc, xT, w_words, w_scales, gate, offs, out):
 
         x_view = xT.rearrange("(g p u e) w -> g u p e w", p=P, u=2, e=2)
         offsets = keep.tile([P, S // 16], U16, name="offsets")
-        stream = keep.tile([P, 2 * LAST * ROWS + FRONT], F32, name="stream", align_bytes=64)
+        room = 2 * S - HOLD
+        stream_at = {(1, 0): 0, (1, 1): ROWS, (2, 0): 2 * ROWS, (2, 1): 3 * ROWS, (3, 0): 4 * ROWS + room, (3, 1): 5 * ROWS + 2 * room}
+        stream = keep.tile([P, 6 * ROWS + 3 * room], F32, name="stream", align_bytes=64)
 
-        def stream_start(g, u):
-            return (2 * (g - 1) + u) * ROWS
-
-        cuts = {(0, 0): (0, T // 3, 2 * T // 3, T), (0, 1): (0, T // 2, T), (LAST, 1): (0, CUT_AFTER_LEAD, T)}
+        cuts = {(0, 0): (0, T // 3, 2 * T // 3, T), (0, 1): (0, T // 2, T)}
         loaded = {}
         for g in range(PASSES):
             for u in range(2):
                 edges = cuts.get((g, u), (0, T))
                 for a, b in zip(edges, edges[1:]):
                     if g == 0:
-                        piece = keep.tile([P, 2, b - a], F32, name=f"first{u}_{a}", align_bytes=64)[:]
+                        piece = keep.tile([P, 2, b - a], F32, name=f"first{u}_{a}", tag=f"first{u}_{a}", align_bytes=64)[:]
                     else:
-                        both_rows = stream[:, stream_start(g, u) : stream_start(g, u) + ROWS]
-                        piece = both_rows.rearrange("p (e w) -> p e w", e=2)[:, :, a:b]
+                        piece = stream[:, stream_at[g, u] : stream_at[g, u] + ROWS].rearrange("p (e w) -> p e w", e=2)
                     nc.sync.dma_start(piece, x_view[g, u, :, :, a:b])
                     loaded[g, u, a] = piece
                 if g == u == 0:
@@ -85,77 +79,86 @@ def tile_moe_shr_lin_none_kernel(tc, xT, w_words, w_scales, gate, offs, out):
         nc.sync.dma_start(gate_sb[:], gate)
         nc.sync.dma_start(w_codes[E][:].bitcast(I32), w_view[E])
 
-        late_pairs_at = 8 * C
-        late_slot_quads_at = 128
-        late_codes_at = late_slot_quads_at + 8 * C
-        late_token_quads_at = late_codes_at + 2 * 4 * NARROW
-        token_pairs = [keep.tile([P, 4 * T], BF16, name=f"token_pairs{g}", align_bytes=64) for g in range(PASSES)]
-        slot_pairs = [
-            keep.tile([P, 4 * S], BF16, name="slot_pairs0", align_bytes=64),
-            keep.tile([P, 4 * S], BF16, name="slot_pairs1", align_bytes=64),
-            late.tile([P, 4 * S], BF16, name="slot_pairs2", align_bytes=64, offset=late_pairs_at),
-            keep.tile([P, 4 * S], BF16, name="slot_pairs3", align_bytes=64),
+        tail = 4 * T - 2 * HOLD
+        codes0_at = 8 * WIDE - 4 * HOLD
+        pairs2_at = codes0_at + 4 * C - 4 * HOLD
+        codes1_at = pairs2_at + 4 * HOLD
+        narrow_codes_at = codes1_at + 4 * C
+        codes_pass2_at = narrow_codes_at + 4 * NARROW
+        slot_pairs1_at = pairs2_at + 2 * (tail + 4 * NARROW)
+        slot_pairs3_at = slot_pairs1_at + 8 * S - 4 * HOLD
+        front = 4 * NARROW - 2 * HOLD
+        pairs1_at = slot_pairs3_at + 2 * (front + 4 * S)
+        slot_pairs3_tile = late.tile([P, front + 4 * S], BF16, name="slot_pairs3", align_bytes=64, offset=slot_pairs3_at)
+        pairs_tiles = [
+            keep.tile([P, 4 * T], BF16, name="pairs0", align_bytes=64),
+            late.tile([P, tail + 4 * WIDE], BF16, name="pairs1", align_bytes=64, offset=pairs1_at),
+            late.tile([P, tail + 4 * NARROW], BF16, name="pairs2", align_bytes=64, offset=pairs2_at),
+            keep.tile([P, tail + 4 * NARROW], BF16, name="pairs3", align_bytes=64),
         ]
-        quads_pass0 = keep.tile([P, 4 * T], BF16, name="quads_pass0", align_bytes=64)
-        wide_quads_pass2 = late.tile([P, 4 * WIDE], BF16, name="wide_quads_pass2", align_bytes=64, offset=late_token_quads_at)
-        narrow_quads_pass3 = keep.tile([P, 4 * NARROW], BF16, name="narrow_quads_pass3", align_bytes=64)
-        token_codes = [keep.tile([P, T], U32, name=f"token_codes{g}", align_bytes=64) for g in range(PASSES)]
+        token_pairs = [t[:, 0 : 4 * T] for t in pairs_tiles]
+        slot_pairs = [
+            keep.tile([P, 4 * S], BF16, name="slot_pairs0", align_bytes=64)[:],
+            late.tile([P, 4 * S], BF16, name="slot_pairs1", align_bytes=64, offset=slot_pairs1_at)[:],
+            late.tile([P, 4 * S], BF16, name="slot_pairs2", align_bytes=64, offset=pairs1_at)[:],
+            slot_pairs3_tile[:, front:],
+        ]
+        narrow_quads = [
+            keep.tile([P, 4 * NARROW], BF16, name="narrow_quads0", align_bytes=64)[:],
+            pairs_tiles[2][:, tail:],
+            pairs_tiles[3][:, tail:],
+            slot_pairs3_tile[:, 0 : 4 * NARROW],
+        ]
+
+        def behind(g, u):
+            start = stream_at[g, u] + ROWS - HOLD
+            return stream[:, start : start + 2 * S].bitcast(BF16)
+
+        def ahead_of(g, u):
+            end = stream_at[g, u] + HOLD
+            return stream[:, end - 2 * S : end].bitcast(BF16)
+
+        wide_quads = [
+            pairs_tiles[1][:, tail:],
+            keep.tile([P, 4 * WIDE], BF16, name="wide_quads1", align_bytes=64)[:],
+            behind(3, 1),
+            late.tile([P, 4 * WIDE], BF16, name="wide_quads3", align_bytes=64, offset=0)[:],
+        ]
+        slot_quads = [
+            pairs_tiles[0][:, 0 : 4 * S],
+            behind(2, 1),
+            ahead_of(3, 1),
+            keep.tile([P, 4 * S], BF16, name="slot_quads3", align_bytes=64)[:],
+        ]
+        narrow_codes = [
+            keep.tile([P, NARROW], U32, name="narrow_codes0", tag=f"first1_{T // 2}", align_bytes=64),
+            late.tile([P, NARROW], U32, name="narrow_codes1", align_bytes=64, offset=pairs1_at + 8 * S),
+            late.tile([P, NARROW], U32, name="narrow_codes2", align_bytes=64, offset=slot_pairs1_at),
+            late.tile([P, NARROW], U32, name="narrow_codes3", align_bytes=64, offset=narrow_codes_at),
+        ]
+        wide_codes = [keep.tile([P, WIDE], U32, name=f"wide_codes{g}", align_bytes=64) for g in range(PASSES)]
         token_scales = [keep.tile([P, T], U8, name=f"token_scales{g}", align_bytes=64) for g in range(PASSES)]
-        slot_codes = [keep.tile([P, S], U32, name=f"slot_codes{g}", align_bytes=64) for g in range(LAST)]
+        slot_codes = [keep.tile([P, S], U32, name=f"slot_codes{g}", align_bytes=64) for g in range(2)]
+        slot_codes.append(late.tile([P, S], U32, name="slot_codes2", align_bytes=64, offset=codes_pass2_at))
         last_slot_codes = [
-            keep.tile([P, C], U32, name=f"last_slot_codes{e}", tag=f"last_slot_codes{e}", align_bytes=64) for e in range(E)
+            late.tile([P, C], U32, name=f"last_slot_codes{e}", align_bytes=64, offset=at) for e, at in enumerate((codes0_at, codes1_at))
         ]
         slot_scales = [keep.tile([P, S], U8, name=f"slot_scales{g}", align_bytes=64) for g in range(PASSES)]
 
-        expert0_banks = [psum.tile([P, GROUP], F32, name=f"expert0_bank{i}", tag=f"bank{i}") for i in range(2)]
-        expert1_bank = psum.tile([P, C], F32, name="expert1_bank")
+        slot_banks = [psum.tile([P, GROUP], F32, name=f"slot_bank{i}", tag=f"bank{i}") for i in range(S // GROUP)]
         wide_bank = psum.tile([P, WIDE], F32, name="wide_bank", tag="bank0")
         narrow_bank = psum.tile([P, NARROW], F32, name="narrow_bank", tag="bank1")
         y_sb = [keep.tile([P, C], F32, name=f"y_sb{e}") for e in range(E)]
 
-        wide_quads_pass3 = keep.tile([P, 4 * WIDE], BF16, name="wide_quads_pass3", tag="last_slot_codes0", align_bytes=64)
-
-        def ending_in_front(g, u, columns):
-            end = stream_start(g, u) + FRONT
-            return stream[:, end - 2 * columns : end].bitcast(BF16)
-
-        after_front = stream_start(LAST, 1) + FRONT
-        wide_quads = [
-            quads_pass0[:, 0 : 4 * WIDE],
-            stream[:, after_front : after_front + 2 * WIDE].bitcast(BF16),
-            wide_quads_pass2[:],
-            wide_quads_pass3[:],
-        ]
-        narrow_quads = [
-            quads_pass0[:, 4 * WIDE :],
-            ending_in_front(2, 0, NARROW),
-            stream[:, after_front + 2 * WIDE :].bitcast(BF16),
-            narrow_quads_pass3[:],
-        ]
-        slot_quads = [ending_in_front(g + 1, 1, S) for g in range(LAST)]
-        last_slot_quads = [
-            late.tile([P, 4 * C], BF16, name="last_slot_quads0", align_bytes=64, offset=late_slot_quads_at),
-            keep.tile([P, 4 * C], BF16, name="last_slot_quads1", align_bytes=64),
-        ]
-        held_codes = {
-            g: late.tile([P, NARROW], U32, name=f"held_codes{g}", align_bytes=64, offset=late_codes_at + 4 * NARROW * (g - 1))
-            for g in (1, 2)
-        }
-
         def token_quads_of(g, a, b):
-            if a < WIDE:
-                return wide_quads[g][:, 4 * a : 4 * b]
-            return narrow_quads[g][:, 4 * (a - WIDE) : 4 * (b - WIDE)]
+            if a < NARROW:
+                return narrow_quads[g][:, 4 * a : 4 * b]
+            return wide_quads[g][:, 4 * (a - NARROW) : 4 * (b - NARROW)]
 
         def token_codes_of(g, a, b):
-            if g in held_codes and a >= WIDE:
-                return held_codes[g][:, a - WIDE : b - WIDE]
-            return token_codes[g][:, a:b]
-
-        def slot_quads_of(g, a, b):
-            if g < LAST:
-                return slot_quads[g][:, 4 * a : 4 * b]
-            return last_slot_quads[a // C][:]
+            if a < NARROW:
+                return narrow_codes[g][:, a:b]
+            return wide_codes[g][:, a - NARROW : b - NARROW]
 
         def slot_codes_of(g, a, b):
             if g < LAST:
@@ -171,34 +174,31 @@ def tile_moe_shr_lin_none_kernel(tc, xT, w_words, w_scales, gate, offs, out):
                 in_=rows(g, u, a, b).rearrange("p e w -> p w e"),
             )
 
-        def shared_cast(g, u, cut):
-            cast(gpsimd_values, g, u, cut, T)
-            cast(nc.scalar.copy, g, u, 0, FRONT)
-            cast(nc.scalar.copy, g, u, FRONT, cut)
+        def shared_cast(g):
+            cast(gpsimd_values, g, 1, T - SHARE[g], T)
+            cast(nc.scalar.copy, g, 1, 0, NARROW)
+            cast(nc.scalar.copy, g, 1, NARROW, T - SHARE[g])
 
-        def gather(g, u):
+        def gather(g, u, a=0, b=S):
             nc.vector.tensor_copy(
-                slot_pairs[g][:, 2 * u * S : 2 * (u + 1) * S].bitcast(U32),
-                token_pairs[g][:, 2 * u * T : 2 * (u + 1) * T].bitcast(U32).indirect(offsets[:]),
+                slot_pairs[g][:, 2 * (u * S + a) : 2 * (u * S + b)].bitcast(U32),
+                token_pairs[g][:, 2 * u * T : 2 * (u + 1) * T].bitcast(U32).indirect(offsets[:, a // 16 : b // 16]),
             )
 
-        def copy_pairs(copy, word, quads, pairs, a, b):
-            copy(
-                out=quads.bitcast(word).rearrange("p (w u) -> p w u", u=2),
-                in_=pairs[:].bitcast(word).rearrange("p (u w) -> p w u", u=2)[:, a:b],
+        word_of = {"scalar": U32, "vector": I32, "gpsimd": I32}
+        copy_of = {"scalar": nc.scalar.copy, "vector": nc.vector.tensor_copy, "gpsimd": nc.gpsimd.tensor_copy}
+
+        def copy_pairs(engine, quads, pairs, a, b):
+            copy_of[engine](
+                out=quads.bitcast(word_of[engine]).rearrange("p (w u) -> p w u", u=2),
+                in_=pairs.bitcast(word_of[engine]).rearrange("p (u w) -> p w u", u=2)[:, a:b],
             )
 
-        def token_quads_on_scalar(g, a, b):
-            copy_pairs(nc.scalar.copy, U32, token_quads_of(g, a, b), token_pairs[g], a, b)
+        def token_quads(engine, g, a, b):
+            copy_pairs(engine, token_quads_of(g, a, b), token_pairs[g], a, b)
 
-        def slot_quads_on_scalar(g, a, b):
-            copy_pairs(nc.scalar.copy, U32, slot_quads_of(g, a, b), slot_pairs[g], a, b)
-
-        def lead_slot_quads(g):
-            gpsimd_values(
-                out=slot_quads_of(g, 0, LEAD_SLOTS).rearrange("p (w u e) -> p w u e", u=2, e=2),
-                in_=slot_pairs[g][:].rearrange("p (u w e) -> p w u e", u=2, e=2)[:, 0:LEAD_SLOTS],
-            )
+        def slot_quads_on(engine, g, a, b):
+            copy_pairs(engine, slot_quads[g][:, 4 * a : 4 * b], slot_pairs[g], a, b)
 
         def quantize_tokens(g, a, b):
             nc.vector.quantize_mx(
@@ -207,7 +207,7 @@ def tile_moe_shr_lin_none_kernel(tc, xT, w_words, w_scales, gate, offs, out):
 
         def quantize_slots(g, a, b):
             nc.vector.quantize_mx(
-                out=slot_codes_of(g, a, b).bitcast(FP8X4), scales=slot_scales[g][:, a:b], in_=slot_quads_of(g, a, b)
+                out=slot_codes_of(g, a, b).bitcast(FP8X4), scales=slot_scales[g][:, a:b], in_=slot_quads[g][:, 4 * a : 4 * b]
             )
 
         def product(bank, e, g, codes, scales):
@@ -222,15 +222,16 @@ def tile_moe_shr_lin_none_kernel(tc, xT, w_words, w_scales, gate, offs, out):
                 stop=(g == LAST),
             )
 
-        def slot_product(bank, g, a):
-            product(bank, a // C, g, slot_codes_of(g, a, a + GROUP), slot_scales[g][:, a : a + GROUP])
+        def slot_product(i, g):
+            a = GROUP * i
+            product(slot_banks[i][:], a // C, g, slot_codes_of(g, a, a + GROUP), slot_scales[g][:, a : a + GROUP])
 
         def token_product(bank, g, a, b):
             product(bank, E, g, token_codes_of(g, a, b), token_scales[g][:, a:b])
 
-        def token_products(g):
-            token_product(wide_bank[:], g, 0, WIDE)
-            token_product(narrow_bank[:, 0:GROUP], g, WIDE, WIDE + GROUP)
+        def empty_slot_banks(e):
+            for i in range(2):
+                nc.scalar.copy(out=y_sb[e][:, GROUP * i : GROUP * (i + 1)], in_=slot_banks[2 * e + i][:])
 
         def scatter(e):
             nc.vector.tensor_tensor(
@@ -247,65 +248,72 @@ def tile_moe_shr_lin_none_kernel(tc, xT, w_words, w_scales, gate, offs, out):
         gather(0, 0)
         cast(nc.vector.tensor_copy, 0, 1, T // 2, T)
         gather(0, 1)
-        token_quads_on_scalar(0, 0, T // 2)
-        token_quads_on_scalar(0, WIDE, T)
-        token_quads_on_scalar(0, T // 2, WIDE)
-        quantize_tokens(0, WIDE, T)
-        quantize_tokens(0, 0, WIDE)
-
-        cast(gpsimd_values, 1, 0, CUT_LATE_LOAD, T)
-        cast(nc.scalar.copy, 1, 0, 0, CUT_LATE_LOAD)
-        gather(1, 0)
-        shared_cast(1, 1, CUT_WHOLE_GATHER)
-        gather(1, 1)
-        slot_quads_on_scalar(0, 0, S)
+        token_quads("scalar", 0, 0, NARROW)
+        token_quads("scalar", 0, NARROW, 2 * NARROW)
+        token_quads("gpsimd", 0, 2 * NARROW, T)
+        quantize_tokens(0, 0, NARROW)
+        slot_quads_on("vector", 0, 0, S)
+        quantize_tokens(0, NARROW, T)
         quantize_slots(0, 0, S)
 
-        for g in (2, 3):
-            shared_cast(g, 0, CUT_WHOLE_GATHER)
-            gather(g, 0)
-            if g == 2:
-                token_quads_on_scalar(1, WIDE, T)
-            lead_slot_quads(g - 1)
-            shared_cast(g, 1, CUT_AFTER_LEAD)
-            gather(g, 1)
-            slot_quads_on_scalar(g - 1, LEAD_SLOTS, S)
-            quantize_slots(g - 1, 0, S)
+        cast(nc.scalar.copy, 1, 0, 0, T)
+        gather(1, 0)
+        shared_cast(1)
+        gather(1, 1)
+        token_quads("scalar", 1, 0, NARROW)
+        token_quads("gpsimd", 1, NARROW, T)
+        quantize_tokens(1, 0, NARROW)
+        quantize_tokens(1, NARROW, T)
 
-        copy_pairs(nc.vector.tensor_copy, I32, slot_quads_of(LAST, 0, C), slot_pairs[LAST], 0, C)
-        quantize_tokens(1, WIDE, T)
-        quantize_slots(LAST, 0, C)
-        token_quads_on_scalar(2, WIDE, T)
-        quantize_tokens(2, WIDE, T)
-        token_quads_on_scalar(1, 0, WIDE)
-        quantize_tokens(1, 0, WIDE)
-        slot_quads_on_scalar(LAST, C, S)
-        quantize_slots(LAST, C, S)
-        token_quads_on_scalar(2, 0, WIDE)
-        quantize_tokens(2, 0, WIDE)
-        for g in range(PASSES):
-            for i in range(2):
-                slot_product(expert0_banks[i][:], g, GROUP * i)
-        for i in range(2):
-            for g in range(PASSES):
-                slot_product(expert1_bank[:, GROUP * i : GROUP * (i + 1)], g, C + GROUP * i)
-        copy_pairs(nc.gpsimd.tensor_copy, I32, token_quads_of(LAST, WIDE, T), token_pairs[LAST], WIDE, T)
-        quantize_tokens(LAST, WIDE, T)
+        cast(nc.scalar.copy, 2, 0, 0, T)
+        gather(2, 0)
+        shared_cast(2)
+        gather(2, 1)
+        token_quads("scalar", 2, 0, NARROW)
+        slot_quads_on("gpsimd", 1, 0, S)
+        quantize_tokens(2, 0, NARROW)
+        quantize_slots(1, 0, S)
 
-        for i in range(2):
-            nc.scalar.copy(out=y_sb[0][:, GROUP * i : GROUP * (i + 1)], in_=expert0_banks[i][:])
+        cast(nc.scalar.copy, 3, 0, 0, T)
+        gather(3, 0)
+        shared_cast(3)
+        gather(3, 1, 0, C)
+        gather(3, 1, C, S)
+        slot_quads_on("scalar", 2, 0, S)
+        token_quads("gpsimd", 2, NARROW, T)
+        slot_quads_on("scalar", 3, 0, C)
+        slot_quads_on("scalar", 3, C, S)
+        token_quads("scalar", 3, 0, NARROW)
+        quantize_slots(2, 0, C)
+        quantize_slots(2, C, S)
+        quantize_slots(3, 0, C)
+        quantize_tokens(2, NARROW, T)
+        quantize_slots(3, C, S)
+        quantize_tokens(3, 0, NARROW)
+        for e in range(E):
+            for g in range(2):
+                for i in range(2):
+                    slot_product(2 * e + i, g)
+        for e in range(E):
+            for g in (2, 3):
+                for i in range(2):
+                    slot_product(2 * e + i, g)
+
+        empty_slot_banks(0)
         scatter(0)
         for g in range(LAST):
-            token_products(g)
-        token_quads_on_scalar(LAST, 0, WIDE)
-        quantize_tokens(LAST, 0, WIDE)
-        token_products(LAST)
+            token_product(wide_bank[:], g, NARROW, T)
+            token_product(narrow_bank[:, 0:GROUP], g, 0, GROUP)
+        token_product(narrow_bank[:, 0:GROUP], LAST, 0, GROUP)
         for g in range(PASSES):
-            token_product(narrow_bank[:, GROUP:NARROW], g, WIDE + GROUP, T)
-        nc.scalar.copy(out=y_sb[1][:], in_=expert1_bank[:])
+            token_product(narrow_bank[:, GROUP:NARROW], g, GROUP, NARROW)
+        token_quads("scalar", LAST, NARROW, T)
+        quantize_tokens(LAST, NARROW, T)
+        token_product(wide_bank[:], LAST, NARROW, T)
+        empty_slot_banks(1)
         scatter(1)
 
         result = keep.tile([P, T], F32, name="result")
-        for bank, a, b in ((wide_bank, 0, WIDE), (narrow_bank, WIDE, T)):
+        for bank, a, b in ((wide_bank, NARROW, T), (narrow_bank, 0, NARROW)):
             nc.vector.tensor_tensor(result[:, a:b], bank[:], window[:, a:b], ADD)
             nc.sync.dma_start(out[:, a:b], result[:, a:b])

@@ -21,11 +21,12 @@ LAST = PASSES - 1
 FLOPS = 2 * K * N * (T + S)
 
 ROWS = 2 * T
-NARROW = 256
-WIDE = T - NARROW
+WIDE = 512
+NARROW = T - WIDE
 GROUP = 128
 HOLD = 16
-SHARE = {1: 192, 2: 192, 3: 224}
+SHARE = 192
+GPSIMD_SLOTS = 128
 
 
 def tile_moe_shr_lin_none_kernel(tc, xT, w_words, w_scales, gate, offs, out):
@@ -38,23 +39,31 @@ def tile_moe_shr_lin_none_kernel(tc, xT, w_words, w_scales, gate, offs, out):
         x_view = xT.rearrange("(g p u e) w -> g u p e w", p=P, u=2, e=2)
         offsets = keep.tile([P, S // 16], U16, name="offsets")
         room = 2 * S - HOLD
-        stream_at = {(1, 0): 0, (1, 1): ROWS, (2, 0): 2 * ROWS, (2, 1): 3 * ROWS, (3, 0): 4 * ROWS + room, (3, 1): 5 * ROWS + 2 * room}
-        stream = keep.tile([P, 6 * ROWS + 3 * room], F32, name="stream", align_bytes=64)
+        pairs3_at = 3 * ROWS + room
+        narrow_quads1_at = pairs3_at + 2 * T - HOLD
+        stream_at = {(1, 0): 0, (1, 1): ROWS + room, (2, 0): 2 * ROWS + room, (2, 1): narrow_quads1_at + 2 * NARROW - HOLD}
+        stream_at[3, 0] = stream_at[2, 1] + ROWS + room
+        stream_at[3, 1] = stream_at[3, 0] + ROWS + room
+        stream = keep.tile([P, stream_at[3, 1] + ROWS + room], F32, name="stream", align_bytes=64)
 
-        cuts = {(0, 0): (0, T // 3, 2 * T // 3, T), (0, 1): (0, T // 2, T)}
-        loaded = {}
-        for g in range(PASSES):
-            for u in range(2):
-                edges = cuts.get((g, u), (0, T))
-                for a, b in zip(edges, edges[1:]):
-                    if g == 0:
-                        piece = keep.tile([P, 2, b - a], F32, name=f"first{u}_{a}", tag=f"first{u}_{a}", align_bytes=64)[:]
-                    else:
-                        piece = stream[:, stream_at[g, u] : stream_at[g, u] + ROWS].rearrange("p (e w) -> p e w", e=2)
-                    nc.sync.dma_start(piece, x_view[g, u, :, :, a:b])
-                    loaded[g, u, a] = piece
-                if g == u == 0:
+        third = T // 3
+        narrow_rows = keep.tile([P, 4, NARROW], F32, name="narrow_rows", align_bytes=64)
+        nc.sync.dma_start(narrow_rows[:], xT[0:512, WIDE:T].rearrange("(p t) w -> p t w", t=4))
+        loaded = {(0, u, WIDE): narrow_rows[:, 2 * u : 2 * u + 2, :] for u in range(2)}
+        for u in range(2):
+            for a in (0, third):
+                piece = keep.tile([P, 2, third], F32, name=f"first{u}_{a}", align_bytes=64)[:]
+                nc.sync.dma_start(piece, x_view[0, u, :, :, a : a + third])
+                loaded[0, u, a] = piece
+                if u == a == 0:
                     nc.sync.dma_start(offsets[:], offs)
+        for g in range(1, PASSES):
+            for u in range(2):
+                both_rows = stream[:, stream_at[g, u] : stream_at[g, u] + ROWS].rearrange("p (e w) -> p e w", e=2)
+                edges = (0, T // 2, T) if (g, u) == (1, 0) else (0, T)
+                for a, b in zip(edges, edges[1:]):
+                    nc.sync.dma_start(both_rows[:, :, a:b], x_view[g, u, :, :, a:b])
+                loaded[g, u, 0] = both_rows
 
         def rows(g, u, a, b):
             first = max(c for (i, j, c) in loaded if (i, j) == (g, u) and c <= a)
@@ -80,34 +89,36 @@ def tile_moe_shr_lin_none_kernel(tc, xT, w_words, w_scales, gate, offs, out):
         nc.sync.dma_start(w_codes[E][:].bitcast(I32), w_view[E])
 
         tail = 4 * T - 2 * HOLD
-        codes0_at = 8 * WIDE - 4 * HOLD
-        pairs2_at = codes0_at + 4 * C - 4 * HOLD
-        codes1_at = pairs2_at + 4 * HOLD
-        narrow_codes_at = codes1_at + 4 * C
-        codes_pass2_at = narrow_codes_at + 4 * NARROW
-        slot_pairs1_at = pairs2_at + 2 * (tail + 4 * NARROW)
-        slot_pairs3_at = slot_pairs1_at + 8 * S - 4 * HOLD
         front = 4 * NARROW - 2 * HOLD
-        pairs1_at = slot_pairs3_at + 2 * (front + 4 * S)
+        codes0_at = 8 * WIDE - 4 * HOLD
+        pairs1_at = codes0_at + 4 * C - 4 * HOLD
+        codes1_at = pairs1_at + 4 * HOLD
+        narrow_codes_at = codes1_at + 4 * C
+        wide_codes2_at = narrow_codes_at + 8 * NARROW
+        pairs0_at = pairs1_at + 16 * T
+        slot_pairs1_at = pairs0_at + 8 * T - 4 * HOLD
+        slot_pairs3_at = slot_pairs1_at + 8 * S - 4 * HOLD
+        pairs0_tile = late.tile([P, 4 * T], BF16, name="pairs0", align_bytes=64, offset=pairs0_at)
+        pairs1_tile = late.tile([P, 8 * T], BF16, name="pairs1", align_bytes=64, offset=pairs1_at)
+        pairs2_tile = keep.tile([P, tail + 4 * WIDE], BF16, name="pairs2", align_bytes=64)
         slot_pairs3_tile = late.tile([P, front + 4 * S], BF16, name="slot_pairs3", align_bytes=64, offset=slot_pairs3_at)
-        pairs_tiles = [
-            keep.tile([P, 4 * T], BF16, name="pairs0", align_bytes=64),
-            late.tile([P, tail + 4 * WIDE], BF16, name="pairs1", align_bytes=64, offset=pairs1_at),
-            late.tile([P, tail + 4 * NARROW], BF16, name="pairs2", align_bytes=64, offset=pairs2_at),
-            keep.tile([P, tail + 4 * NARROW], BF16, name="pairs3", align_bytes=64),
+        token_pairs = [
+            pairs0_tile[:],
+            pairs1_tile[:, 0 : 4 * T],
+            pairs2_tile[:, 0 : 4 * T],
+            stream[:, pairs3_at : pairs3_at + 2 * T].bitcast(BF16),
         ]
-        token_pairs = [t[:, 0 : 4 * T] for t in pairs_tiles]
         slot_pairs = [
             keep.tile([P, 4 * S], BF16, name="slot_pairs0", align_bytes=64)[:],
             late.tile([P, 4 * S], BF16, name="slot_pairs1", align_bytes=64, offset=slot_pairs1_at)[:],
-            late.tile([P, 4 * S], BF16, name="slot_pairs2", align_bytes=64, offset=pairs1_at)[:],
+            pairs1_tile[:],
             slot_pairs3_tile[:, front:],
         ]
         narrow_quads = [
             keep.tile([P, 4 * NARROW], BF16, name="narrow_quads0", align_bytes=64)[:],
-            pairs_tiles[2][:, tail:],
-            pairs_tiles[3][:, tail:],
+            stream[:, narrow_quads1_at : narrow_quads1_at + 2 * NARROW].bitcast(BF16),
             slot_pairs3_tile[:, 0 : 4 * NARROW],
+            slot_pairs3_tile[:, 4 * NARROW : 8 * NARROW],
         ]
 
         def behind(g, u):
@@ -119,27 +130,32 @@ def tile_moe_shr_lin_none_kernel(tc, xT, w_words, w_scales, gate, offs, out):
             return stream[:, end - 2 * S : end].bitcast(BF16)
 
         wide_quads = [
-            pairs_tiles[1][:, tail:],
-            keep.tile([P, 4 * WIDE], BF16, name="wide_quads1", align_bytes=64)[:],
-            behind(3, 1),
+            keep.tile([P, 4 * WIDE], BF16, name="wide_quads0", align_bytes=64)[:],
+            pairs2_tile[:, tail:],
+            ahead_of(3, 1),
             late.tile([P, 4 * WIDE], BF16, name="wide_quads3", align_bytes=64, offset=0)[:],
         ]
         slot_quads = [
-            pairs_tiles[0][:, 0 : 4 * S],
+            behind(1, 0),
             behind(2, 1),
-            ahead_of(3, 1),
+            behind(3, 1),
             keep.tile([P, 4 * S], BF16, name="slot_quads3", align_bytes=64)[:],
         ]
+        late_narrow_codes = late.tile([P, 2 * NARROW], U32, name="late_narrow_codes", align_bytes=64, offset=narrow_codes_at)
         narrow_codes = [
-            keep.tile([P, NARROW], U32, name="narrow_codes0", tag=f"first1_{T // 2}", align_bytes=64),
-            late.tile([P, NARROW], U32, name="narrow_codes1", align_bytes=64, offset=pairs1_at + 8 * S),
-            late.tile([P, NARROW], U32, name="narrow_codes2", align_bytes=64, offset=slot_pairs1_at),
-            late.tile([P, NARROW], U32, name="narrow_codes3", align_bytes=64, offset=narrow_codes_at),
+            keep.tile([P, NARROW], U32, name="narrow_codes0", align_bytes=64)[:],
+            late.tile([P, NARROW], U32, name="narrow_codes1", align_bytes=64, offset=slot_pairs1_at + 4 * HOLD)[:],
+            late_narrow_codes[:, 0:NARROW],
+            late_narrow_codes[:, NARROW:],
         ]
-        wide_codes = [keep.tile([P, WIDE], U32, name=f"wide_codes{g}", align_bytes=64) for g in range(PASSES)]
+        wide_codes = [
+            keep.tile([P, WIDE], U32, name="wide_codes0", align_bytes=64),
+            keep.tile([P, WIDE], U32, name="wide_codes1", align_bytes=64),
+            late.tile([P, WIDE], U32, name="wide_codes2", align_bytes=64, offset=wide_codes2_at),
+            keep.tile([P, WIDE], U32, name="wide_codes3", align_bytes=64),
+        ]
         token_scales = [keep.tile([P, T], U8, name=f"token_scales{g}", align_bytes=64) for g in range(PASSES)]
-        slot_codes = [keep.tile([P, S], U32, name=f"slot_codes{g}", align_bytes=64) for g in range(2)]
-        slot_codes.append(late.tile([P, S], U32, name="slot_codes2", align_bytes=64, offset=codes_pass2_at))
+        slot_codes = [keep.tile([P, S], U32, name=f"slot_codes{g}", align_bytes=64) for g in range(LAST)]
         last_slot_codes = [
             late.tile([P, C], U32, name=f"last_slot_codes{e}", align_bytes=64, offset=at) for e, at in enumerate((codes0_at, codes1_at))
         ]
@@ -151,14 +167,14 @@ def tile_moe_shr_lin_none_kernel(tc, xT, w_words, w_scales, gate, offs, out):
         y_sb = [keep.tile([P, C], F32, name=f"y_sb{e}") for e in range(E)]
 
         def token_quads_of(g, a, b):
-            if a < NARROW:
-                return narrow_quads[g][:, 4 * a : 4 * b]
-            return wide_quads[g][:, 4 * (a - NARROW) : 4 * (b - NARROW)]
+            if a < WIDE:
+                return wide_quads[g][:, 4 * a : 4 * b]
+            return narrow_quads[g][:, 4 * (a - WIDE) : 4 * (b - WIDE)]
 
         def token_codes_of(g, a, b):
-            if a < NARROW:
-                return narrow_codes[g][:, a:b]
-            return wide_codes[g][:, a - NARROW : b - NARROW]
+            if a < WIDE:
+                return wide_codes[g][:, a:b]
+            return narrow_codes[g][:, a - WIDE : b - WIDE]
 
         def slot_codes_of(g, a, b):
             if g < LAST:
@@ -175,13 +191,13 @@ def tile_moe_shr_lin_none_kernel(tc, xT, w_words, w_scales, gate, offs, out):
             )
 
         def shared_cast(g):
-            cast(gpsimd_values, g, 1, T - SHARE[g], T)
-            cast(nc.scalar.copy, g, 1, 0, NARROW)
-            cast(nc.scalar.copy, g, 1, NARROW, T - SHARE[g])
+            cast(gpsimd_values, g, 1, T - SHARE, T)
+            cast(nc.scalar.copy, g, 1, 0, third)
+            cast(nc.scalar.copy, g, 1, third, T - SHARE)
 
         def gather(g, u, a=0, b=S):
             nc.vector.tensor_copy(
-                slot_pairs[g][:, 2 * (u * S + a) : 2 * (u * S + b)].bitcast(U32),
+                slot_pairs[g].bitcast(U32).rearrange("p (u w) -> p u w", u=2)[:, u, a:b],
                 token_pairs[g][:, 2 * u * T : 2 * (u + 1) * T].bitcast(U32).indirect(offsets[:, a // 16 : b // 16]),
             )
 
@@ -241,37 +257,43 @@ def tile_moe_shr_lin_none_kernel(tc, xT, w_words, w_scales, gate, offs, out):
                 MULT,
             )
 
-        cast(nc.scalar.copy, 0, 0, 0, T // 3)
-        cast(nc.vector.tensor_copy, 0, 0, T // 3, 2 * T // 3)
-        cast(nc.vector.tensor_copy, 0, 0, 2 * T // 3, T)
-        cast(nc.scalar.copy, 0, 1, 0, T // 2)
+        cast(nc.scalar.copy, 0, 0, WIDE, T)
+        cast(nc.scalar.copy, 0, 1, WIDE, T)
+        nc.vector.tensor_copy(
+            out=narrow_quads[0].rearrange("p (w t) -> p w t", t=4), in_=narrow_rows[:].rearrange("p t w -> p w t")
+        )
+        cast(nc.scalar.copy, 0, 0, 0, third)
+        cast(nc.vector.tensor_copy, 0, 0, third, WIDE)
+        quantize_tokens(0, WIDE, T)
         gather(0, 0)
-        cast(nc.vector.tensor_copy, 0, 1, T // 2, T)
+        cast(nc.scalar.copy, 0, 1, 0, third)
+        cast(nc.scalar.copy, 0, 1, third, WIDE)
         gather(0, 1)
-        token_quads("scalar", 0, 0, NARROW)
-        token_quads("scalar", 0, NARROW, 2 * NARROW)
-        token_quads("gpsimd", 0, 2 * NARROW, T)
-        quantize_tokens(0, 0, NARROW)
-        slot_quads_on("vector", 0, 0, S)
-        quantize_tokens(0, NARROW, T)
-        quantize_slots(0, 0, S)
+        token_quads("gpsimd", 0, 0, third)
+        token_quads("gpsimd", 0, third, WIDE)
+        quantize_tokens(0, 0, WIDE)
 
-        cast(nc.scalar.copy, 1, 0, 0, T)
+        cast(nc.scalar.copy, 1, 0, 0, T // 2)
+        cast(nc.scalar.copy, 1, 0, T - GROUP, T)
+        cast(nc.scalar.copy, 1, 0, T // 2, T - GROUP)
         gather(1, 0)
-        shared_cast(1)
+        slot_quads_on("scalar", 0, 0, S - GPSIMD_SLOTS)
+        slot_quads_on("gpsimd", 0, S - GPSIMD_SLOTS, S)
+        quantize_slots(0, 0, S)
+        cast(gpsimd_values, 1, 1, WIDE - SHARE, WIDE)
+        cast(nc.scalar.copy, 1, 1, 0, WIDE - SHARE)
+        cast(nc.scalar.copy, 1, 1, WIDE, T)
         gather(1, 1)
-        token_quads("scalar", 1, 0, NARROW)
-        token_quads("gpsimd", 1, NARROW, T)
-        quantize_tokens(1, 0, NARROW)
-        quantize_tokens(1, NARROW, T)
+        token_quads("gpsimd", 1, 0, WIDE)
+        quantize_tokens(1, 0, WIDE)
 
         cast(nc.scalar.copy, 2, 0, 0, T)
         gather(2, 0)
         shared_cast(2)
         gather(2, 1)
-        token_quads("scalar", 2, 0, NARROW)
+        token_quads("scalar", 1, WIDE, T)
         slot_quads_on("gpsimd", 1, 0, S)
-        quantize_tokens(2, 0, NARROW)
+        quantize_tokens(1, WIDE, T)
         quantize_slots(1, 0, S)
 
         cast(nc.scalar.copy, 3, 0, 0, T)
@@ -279,17 +301,18 @@ def tile_moe_shr_lin_none_kernel(tc, xT, w_words, w_scales, gate, offs, out):
         shared_cast(3)
         gather(3, 1, 0, C)
         gather(3, 1, C, S)
-        slot_quads_on("scalar", 2, 0, S)
-        token_quads("gpsimd", 2, NARROW, T)
+        token_quads("scalar", 2, 0, WIDE)
+        slot_quads_on("gpsimd", 2, 0, S)
         slot_quads_on("scalar", 3, 0, C)
         slot_quads_on("scalar", 3, C, S)
-        token_quads("scalar", 3, 0, NARROW)
-        quantize_slots(2, 0, C)
-        quantize_slots(2, C, S)
+        token_quads("scalar", 2, WIDE, T)
+        token_quads("scalar", 3, WIDE, T)
+        quantize_slots(2, 0, S)
         quantize_slots(3, 0, C)
-        quantize_tokens(2, NARROW, T)
+        quantize_tokens(2, 0, WIDE)
         quantize_slots(3, C, S)
-        quantize_tokens(3, 0, NARROW)
+        quantize_tokens(2, WIDE, T)
+        quantize_tokens(3, WIDE, T)
         for e in range(E):
             for g in range(2):
                 for i in range(2):
@@ -302,18 +325,18 @@ def tile_moe_shr_lin_none_kernel(tc, xT, w_words, w_scales, gate, offs, out):
         empty_slot_banks(0)
         scatter(0)
         for g in range(LAST):
-            token_product(wide_bank[:], g, NARROW, T)
-            token_product(narrow_bank[:, 0:GROUP], g, 0, GROUP)
-        token_product(narrow_bank[:, 0:GROUP], LAST, 0, GROUP)
+            token_product(wide_bank[:], g, 0, WIDE)
+            token_product(narrow_bank[:, 0:GROUP], g, WIDE, WIDE + GROUP)
+        token_product(narrow_bank[:, 0:GROUP], LAST, WIDE, WIDE + GROUP)
         for g in range(PASSES):
-            token_product(narrow_bank[:, GROUP:NARROW], g, GROUP, NARROW)
-        token_quads("scalar", LAST, NARROW, T)
-        quantize_tokens(LAST, NARROW, T)
-        token_product(wide_bank[:], LAST, NARROW, T)
+            token_product(narrow_bank[:, GROUP:NARROW], g, WIDE + GROUP, T)
+        token_quads("scalar", LAST, 0, WIDE)
+        quantize_tokens(LAST, 0, WIDE)
+        token_product(wide_bank[:], LAST, 0, WIDE)
         empty_slot_banks(1)
         scatter(1)
 
         result = keep.tile([P, T], F32, name="result")
-        for bank, a, b in ((wide_bank, NARROW, T), (narrow_bank, 0, NARROW)):
+        for bank, a, b in ((wide_bank, 0, WIDE), (narrow_bank, WIDE, T)):
             nc.vector.tensor_tensor(result[:, a:b], bank[:], window[:, a:b], ADD)
             nc.sync.dma_start(out[:, a:b], result[:, a:b])

@@ -25,7 +25,9 @@ WIDE = 512
 NARROW = T - WIDE
 GROUP = 128
 HOLD = 16
-SHARE = 192
+SHARE = 224
+FIRST_SHARE = 192
+SCALAR_TOKENS = 128
 GPSIMD_SLOTS = 128
 
 
@@ -39,9 +41,12 @@ def tile_moe_shr_lin_none_kernel(tc, xT, w_words, w_scales, gate, offs, out):
         x_view = xT.rearrange("(g p u e) w -> g u p e w", p=P, u=2, e=2)
         offsets = keep.tile([P, S // 16], U16, name="offsets")
         room = 2 * S - HOLD
-        pairs3_at = 3 * ROWS + room
+        pairs2_start = ROWS + room
+        stream_at = {(1, 0): 0, (1, 1): pairs2_start + 2 * T - HOLD}
+        stream_at[2, 0] = stream_at[1, 1] + ROWS
+        pairs3_at = stream_at[2, 0] + ROWS
         narrow_quads1_at = pairs3_at + 2 * T - HOLD
-        stream_at = {(1, 0): 0, (1, 1): ROWS + room, (2, 0): 2 * ROWS + room, (2, 1): narrow_quads1_at + 2 * NARROW - HOLD}
+        stream_at[2, 1] = narrow_quads1_at + 2 * NARROW - HOLD
         stream_at[3, 0] = stream_at[2, 1] + ROWS + room
         stream_at[3, 1] = stream_at[3, 0] + ROWS + room
         stream = keep.tile([P, stream_at[3, 1] + ROWS + room], F32, name="stream", align_bytes=64)
@@ -50,13 +55,12 @@ def tile_moe_shr_lin_none_kernel(tc, xT, w_words, w_scales, gate, offs, out):
         narrow_rows = keep.tile([P, 4, NARROW], F32, name="narrow_rows", align_bytes=64)
         nc.sync.dma_start(narrow_rows[:], xT[0:512, WIDE:T].rearrange("(p t) w -> p t w", t=4))
         loaded = {(0, u, WIDE): narrow_rows[:, 2 * u : 2 * u + 2, :] for u in range(2)}
-        for u in range(2):
-            for a in (0, third):
-                piece = keep.tile([P, 2, third], F32, name=f"first{u}_{a}", align_bytes=64)[:]
-                nc.sync.dma_start(piece, x_view[0, u, :, :, a : a + third])
-                loaded[0, u, a] = piece
-                if u == a == 0:
-                    nc.sync.dma_start(offsets[:], offs)
+        for u, a, b in ((0, 0, WIDE), (1, 0, third), (1, third, WIDE)):
+            piece = keep.tile([P, 2, b - a], F32, name=f"first{u}_{a}", align_bytes=64)[:]
+            nc.sync.dma_start(piece, x_view[0, u, :, :, a:b])
+            loaded[0, u, a] = piece
+            if u == 0:
+                nc.sync.dma_start(offsets[:], offs)
         for g in range(1, PASSES):
             for u in range(2):
                 both_rows = stream[:, stream_at[g, u] : stream_at[g, u] + ROWS].rearrange("p (e w) -> p e w", e=2)
@@ -88,7 +92,6 @@ def tile_moe_shr_lin_none_kernel(tc, xT, w_words, w_scales, gate, offs, out):
         nc.sync.dma_start(gate_sb[:], gate)
         nc.sync.dma_start(w_codes[E][:].bitcast(I32), w_view[E])
 
-        tail = 4 * T - 2 * HOLD
         front = 4 * NARROW - 2 * HOLD
         codes0_at = 8 * WIDE - 4 * HOLD
         pairs1_at = codes0_at + 4 * C - 4 * HOLD
@@ -100,12 +103,11 @@ def tile_moe_shr_lin_none_kernel(tc, xT, w_words, w_scales, gate, offs, out):
         slot_pairs3_at = slot_pairs1_at + 8 * S - 4 * HOLD
         pairs0_tile = late.tile([P, 4 * T], BF16, name="pairs0", align_bytes=64, offset=pairs0_at)
         pairs1_tile = late.tile([P, 8 * T], BF16, name="pairs1", align_bytes=64, offset=pairs1_at)
-        pairs2_tile = keep.tile([P, tail + 4 * WIDE], BF16, name="pairs2", align_bytes=64)
         slot_pairs3_tile = late.tile([P, front + 4 * S], BF16, name="slot_pairs3", align_bytes=64, offset=slot_pairs3_at)
         token_pairs = [
             pairs0_tile[:],
             pairs1_tile[:, 0 : 4 * T],
-            pairs2_tile[:, 0 : 4 * T],
+            stream[:, pairs2_start : pairs2_start + 2 * T].bitcast(BF16),
             stream[:, pairs3_at : pairs3_at + 2 * T].bitcast(BF16),
         ]
         slot_pairs = [
@@ -131,7 +133,7 @@ def tile_moe_shr_lin_none_kernel(tc, xT, w_words, w_scales, gate, offs, out):
 
         wide_quads = [
             keep.tile([P, 4 * WIDE], BF16, name="wide_quads0", align_bytes=64)[:],
-            pairs2_tile[:, tail:],
+            keep.tile([P, 4 * WIDE], BF16, name="wide_quads1", align_bytes=64)[:],
             ahead_of(3, 1),
             late.tile([P, 4 * WIDE], BF16, name="wide_quads3", align_bytes=64, offset=0)[:],
         ]
@@ -280,11 +282,12 @@ def tile_moe_shr_lin_none_kernel(tc, xT, w_words, w_scales, gate, offs, out):
         slot_quads_on("scalar", 0, 0, S - GPSIMD_SLOTS)
         slot_quads_on("gpsimd", 0, S - GPSIMD_SLOTS, S)
         quantize_slots(0, 0, S)
-        cast(gpsimd_values, 1, 1, WIDE - SHARE, WIDE)
-        cast(nc.scalar.copy, 1, 1, 0, WIDE - SHARE)
+        cast(gpsimd_values, 1, 1, 0, FIRST_SHARE)
+        cast(nc.scalar.copy, 1, 1, FIRST_SHARE, WIDE)
         cast(nc.scalar.copy, 1, 1, WIDE, T)
         gather(1, 1)
-        token_quads("gpsimd", 1, 0, WIDE)
+        token_quads("gpsimd", 1, 0, WIDE - SCALAR_TOKENS)
+        token_quads("scalar", 1, WIDE - SCALAR_TOKENS, WIDE)
         quantize_tokens(1, 0, WIDE)
 
         cast(nc.scalar.copy, 2, 0, 0, T)
@@ -337,6 +340,6 @@ def tile_moe_shr_lin_none_kernel(tc, xT, w_words, w_scales, gate, offs, out):
         scatter(1)
 
         result = keep.tile([P, T], F32, name="result")
-        for bank, a, b in ((wide_bank, 0, WIDE), (narrow_bank, WIDE, T)):
-            nc.vector.tensor_tensor(result[:, a:b], bank[:], window[:, a:b], ADD)
-            nc.sync.dma_start(out[:, a:b], result[:, a:b])
+        for sums, a in ((wide_bank[:, 0:third], 0), (wide_bank[:, third:WIDE], third), (narrow_bank[:], WIDE)):
+            nc.vector.tensor_tensor(result[:, a : a + third], sums, window[:, a : a + third], ADD)
+            nc.sync.dma_start(out[:, a : a + third], result[:, a : a + third])

@@ -79,11 +79,10 @@ def tile_moe_shr_lin_none_kernel(tc, xT, w_words, w_scales, gate, offs, out):
         nc.gpsimd.memset(window[:], 0.0)
 
         w_codes = [keep.tile([P, PASSES, 2 * N], U8, name=f"w_codes{e}", align_bytes=64) for e in range(E + 1)]
-        scale_rows = w_scales.rearrange("e a q n -> q (e a) n")
-        for quadrant in range(4):
+        scale_rows = w_scales.rearrange("e a (q r) n -> r q (e a) n", r=4)
+        for r in range(4):
             nc.sync.dma_start(
-                w_planes[32 * quadrant : 32 * quadrant + 4, :].rearrange("p (m n) -> p m n", n=N).bitcast(I32),
-                scale_rows[4 * quadrant : 4 * quadrant + 4].bitcast(I32),
+                w_planes[r:P:32, :].rearrange("p (m n) -> p m n", n=N).bitcast(I32), scale_rows[r].bitcast(I32)
             )
         w_view = w_words.rearrange("e a p b -> e p a b").bitcast(I32)
         gate_sb = keep.tile([P, S], F32, name="gate_sb")
@@ -164,8 +163,8 @@ def tile_moe_shr_lin_none_kernel(tc, xT, w_words, w_scales, gate, offs, out):
         slot_scales = [keep.tile([P, S], U8, name=f"slot_scales{g}", align_bytes=64) for g in range(PASSES)]
 
         slot_banks = [psum.tile([P, GROUP], F32, name=f"slot_bank{i}", tag=f"bank{i}") for i in range(S // GROUP)]
-        wide_bank = psum.tile([P, WIDE], F32, name="wide_bank", tag="bank0")
-        narrow_bank = psum.tile([P, NARROW], F32, name="narrow_bank", tag="bank1")
+        wide_bank = psum.tile([P, WIDE], F32, name="wide_bank")
+        narrow_bank = psum.tile([P, NARROW], F32, name="narrow_bank")
         y_sb = [keep.tile([P, C], F32, name=f"y_sb{e}") for e in range(E)]
 
         def token_quads_of(g, a, b):
@@ -228,7 +227,7 @@ def tile_moe_shr_lin_none_kernel(tc, xT, w_words, w_scales, gate, offs, out):
                 out=slot_codes_of(g, a, b).bitcast(FP8X4), scales=slot_scales[g][:, a:b], in_=slot_quads[g][:, 4 * a : 4 * b]
             )
 
-        def product(bank, e, g, codes, scales):
+        def product(bank, e, g, codes, scales, closing=LAST):
             plane = e * PASSES + g
             nc.tensor.matmul_mx(
                 out=bank,
@@ -237,12 +236,12 @@ def tile_moe_shr_lin_none_kernel(tc, xT, w_words, w_scales, gate, offs, out):
                 rhs=codes.bitcast(FP8X4),
                 rhs_scale=scales,
                 start=(g == 0),
-                stop=(g == LAST),
+                stop=(g == closing),
             )
 
-        def slot_product(i, g):
+        def slot_product(i, g, closing=LAST):
             a = GROUP * i
-            product(slot_banks[i][:], a // C, g, slot_codes_of(g, a, a + GROUP), slot_scales[g][:, a : a + GROUP])
+            product(slot_banks[i][:], a // C, g, slot_codes_of(g, a, a + GROUP), slot_scales[g][:, a : a + GROUP], closing)
 
         def token_product(bank, g, a, b):
             product(bank, E, g, token_codes_of(g, a, b), token_scales[g][:, a:b])
@@ -319,11 +318,11 @@ def tile_moe_shr_lin_none_kernel(tc, xT, w_words, w_scales, gate, offs, out):
         for e in range(E):
             for g in range(2):
                 for i in range(2):
-                    slot_product(2 * e + i, g)
-        for e in range(E):
-            for g in (2, 3):
+                    slot_product(2 * e + i, g, closing=None)
+        for e, order in enumerate(((2, 3), (3, 2))):
+            for g in order:
                 for i in range(2):
-                    slot_product(2 * e + i, g)
+                    slot_product(2 * e + i, g, closing=order[-1])
 
         empty_slot_banks(0)
         scatter(0)

@@ -25,9 +25,8 @@ WIDE = 512
 NARROW = T - WIDE
 GROUP = 128
 HOLD = 16
-SHARE = 224
-FIRST_SHARE = 192
-SCALAR_TOKENS = 128
+SHARE = {1: 256, 2: 288, 3: 288}
+SCALAR_TOKENS = 48
 GPSIMD_SLOTS = 128
 
 
@@ -41,15 +40,13 @@ def tile_moe_shr_lin_none_kernel(tc, xT, w_words, w_scales, gate, offs, out):
         x_view = xT.rearrange("(g p u e) w -> g u p e w", p=P, u=2, e=2)
         offsets = keep.tile([P, S // 16], U16, name="offsets")
         room = 2 * S - HOLD
-        pairs2_start = ROWS + room
-        stream_at = {(1, 0): 0, (1, 1): pairs2_start + 2 * T - HOLD}
-        stream_at[2, 0] = stream_at[1, 1] + ROWS
-        pairs3_at = stream_at[2, 0] + ROWS
-        narrow_quads1_at = pairs3_at + 2 * T - HOLD
-        stream_at[2, 1] = narrow_quads1_at + 2 * NARROW - HOLD
-        stream_at[3, 0] = stream_at[2, 1] + ROWS + room
-        stream_at[3, 1] = stream_at[3, 0] + ROWS + room
-        stream = keep.tile([P, stream_at[3, 1] + ROWS + room], F32, name="stream", align_bytes=64)
+        stream_at = {(1, 1): 0, (1, 0): ROWS + room}
+        pairs2_at = stream_at[1, 0] + T + SHARE[1] - HOLD
+        stream_at[2, 1] = pairs2_at + 2 * T
+        stream_at[2, 0] = stream_at[2, 1] + ROWS + room
+        stream_at[3, 1] = stream_at[2, 0] + ROWS
+        stream_at[3, 0] = stream_at[3, 1] + ROWS + room
+        stream = keep.tile([P, stream_at[3, 0] + ROWS + room], F32, name="stream", align_bytes=64)
 
         third = T // 3
         narrow_rows = keep.tile([P, 4, NARROW], F32, name="narrow_rows", align_bytes=64)
@@ -62,9 +59,9 @@ def tile_moe_shr_lin_none_kernel(tc, xT, w_words, w_scales, gate, offs, out):
             if u == 0:
                 nc.sync.dma_start(offsets[:], offs)
         for g in range(1, PASSES):
-            for u in range(2):
+            for u in (1, 0):
                 both_rows = stream[:, stream_at[g, u] : stream_at[g, u] + ROWS].rearrange("p (e w) -> p e w", e=2)
-                edges = (0, T // 2, T) if (g, u) == (1, 0) else (0, T)
+                edges = (0, T // 2, T) if (g, u) == (1, 1) else (0, T)
                 for a, b in zip(edges, edges[1:]):
                     nc.sync.dma_start(both_rows[:, :, a:b], x_view[g, u, :, :, a:b])
                 loaded[g, u, 0] = both_rows
@@ -79,47 +76,49 @@ def tile_moe_shr_lin_none_kernel(tc, xT, w_words, w_scales, gate, offs, out):
         nc.gpsimd.memset(window[:], 0.0)
 
         w_codes = [keep.tile([P, PASSES, 2 * N], U8, name=f"w_codes{e}", align_bytes=64) for e in range(E + 1)]
-        scale_rows = w_scales.rearrange("e a (q r) n -> r q (e a) n", r=4)
-        for r in range(4):
+        scale_rows = w_scales.rearrange("e a q n -> q (e a) n")
+        for quadrant in range(4):
             nc.sync.dma_start(
-                w_planes[r:P:32, :].rearrange("p (m n) -> p m n", n=N).bitcast(I32), scale_rows[r].bitcast(I32)
+                w_planes[32 * quadrant : 32 * quadrant + 4, :].rearrange("p (m n) -> p m n", n=N).bitcast(I32),
+                scale_rows[4 * quadrant : 4 * quadrant + 4].bitcast(I32),
             )
         w_view = w_words.rearrange("e a p b -> e p a b").bitcast(I32)
         gate_sb = keep.tile([P, S], F32, name="gate_sb")
         for e in range(E):
             nc.sync.dma_start(w_codes[e][:].bitcast(I32), w_view[e])
-        nc.sync.dma_start(gate_sb[:], gate)
         nc.sync.dma_start(w_codes[E][:].bitcast(I32), w_view[E])
+        nc.sync.dma_start(gate_sb[:], gate)
 
         front = 4 * NARROW - 2 * HOLD
         codes0_at = 8 * WIDE - 4 * HOLD
-        pairs1_at = codes0_at + 4 * C - 4 * HOLD
-        codes1_at = pairs1_at + 4 * HOLD
-        narrow_codes_at = codes1_at + 4 * C
-        wide_codes2_at = narrow_codes_at + 8 * NARROW
-        pairs0_at = pairs1_at + 16 * T
+        slot_pairs2_at = codes0_at + 4 * C - 4 * HOLD
+        codes1_at = slot_pairs2_at + 4 * HOLD
+        narrow_codes3_at = codes1_at + 4 * C
+        wide_codes2_at = narrow_codes3_at + 4 * NARROW
+        narrow_codes1_at = wide_codes2_at + 4 * WIDE
+        pairs1_at = slot_pairs2_at
+        pairs0_at = pairs1_at + 8 * T
         slot_pairs1_at = pairs0_at + 8 * T - 4 * HOLD
         slot_pairs3_at = slot_pairs1_at + 8 * S - 4 * HOLD
-        pairs0_tile = late.tile([P, 4 * T], BF16, name="pairs0", align_bytes=64, offset=pairs0_at)
-        pairs1_tile = late.tile([P, 8 * T], BF16, name="pairs1", align_bytes=64, offset=pairs1_at)
+        pairs3_tile = keep.tile([P, front + 4 * T], BF16, name="pairs3", align_bytes=64)
         slot_pairs3_tile = late.tile([P, front + 4 * S], BF16, name="slot_pairs3", align_bytes=64, offset=slot_pairs3_at)
         token_pairs = [
-            pairs0_tile[:],
-            pairs1_tile[:, 0 : 4 * T],
-            stream[:, pairs2_start : pairs2_start + 2 * T].bitcast(BF16),
-            stream[:, pairs3_at : pairs3_at + 2 * T].bitcast(BF16),
+            late.tile([P, 4 * T], BF16, name="pairs0", align_bytes=64, offset=pairs0_at)[:],
+            late.tile([P, 4 * T], BF16, name="pairs1", align_bytes=64, offset=pairs1_at)[:],
+            stream[:, pairs2_at : pairs2_at + 2 * T].bitcast(BF16),
+            pairs3_tile[:, front:],
         ]
         slot_pairs = [
             keep.tile([P, 4 * S], BF16, name="slot_pairs0", align_bytes=64)[:],
             late.tile([P, 4 * S], BF16, name="slot_pairs1", align_bytes=64, offset=slot_pairs1_at)[:],
-            pairs1_tile[:],
+            late.tile([P, 4 * S], BF16, name="slot_pairs2", align_bytes=64, offset=slot_pairs2_at)[:],
             slot_pairs3_tile[:, front:],
         ]
         narrow_quads = [
             keep.tile([P, 4 * NARROW], BF16, name="narrow_quads0", align_bytes=64)[:],
-            stream[:, narrow_quads1_at : narrow_quads1_at + 2 * NARROW].bitcast(BF16),
+            keep.tile([P, 4 * NARROW], BF16, name="narrow_quads1", align_bytes=64)[:],
+            pairs3_tile[:, 0 : 4 * NARROW],
             slot_pairs3_tile[:, 0 : 4 * NARROW],
-            slot_pairs3_tile[:, 4 * NARROW : 8 * NARROW],
         ]
 
         def behind(g, u):
@@ -133,21 +132,20 @@ def tile_moe_shr_lin_none_kernel(tc, xT, w_words, w_scales, gate, offs, out):
         wide_quads = [
             keep.tile([P, 4 * WIDE], BF16, name="wide_quads0", align_bytes=64)[:],
             keep.tile([P, 4 * WIDE], BF16, name="wide_quads1", align_bytes=64)[:],
-            ahead_of(3, 1),
+            behind(3, 0),
             late.tile([P, 4 * WIDE], BF16, name="wide_quads3", align_bytes=64, offset=0)[:],
         ]
         slot_quads = [
-            behind(1, 0),
-            behind(2, 1),
-            behind(3, 1),
+            behind(1, 1),
+            ahead_of(2, 0),
+            ahead_of(3, 0),
             keep.tile([P, 4 * S], BF16, name="slot_quads3", align_bytes=64)[:],
         ]
-        late_narrow_codes = late.tile([P, 2 * NARROW], U32, name="late_narrow_codes", align_bytes=64, offset=narrow_codes_at)
         narrow_codes = [
-            keep.tile([P, NARROW], U32, name="narrow_codes0", align_bytes=64)[:],
-            late.tile([P, NARROW], U32, name="narrow_codes1", align_bytes=64, offset=slot_pairs1_at + 4 * HOLD)[:],
-            late_narrow_codes[:, 0:NARROW],
-            late_narrow_codes[:, NARROW:],
+            keep.tile([P, NARROW], U32, name="narrow_codes0", align_bytes=64),
+            late.tile([P, NARROW], U32, name="narrow_codes1", align_bytes=64, offset=narrow_codes1_at),
+            late.tile([P, NARROW], U32, name="narrow_codes2", align_bytes=64, offset=slot_pairs1_at + 4 * HOLD),
+            late.tile([P, NARROW], U32, name="narrow_codes3", align_bytes=64, offset=narrow_codes3_at),
         ]
         wide_codes = [
             keep.tile([P, WIDE], U32, name="wide_codes0", align_bytes=64),
@@ -192,9 +190,9 @@ def tile_moe_shr_lin_none_kernel(tc, xT, w_words, w_scales, gate, offs, out):
             )
 
         def shared_cast(g):
-            cast(gpsimd_values, g, 1, T - SHARE, T)
-            cast(nc.scalar.copy, g, 1, 0, third)
-            cast(nc.scalar.copy, g, 1, third, T - SHARE)
+            cast(gpsimd_values, g, 0, 0, SHARE[g])
+            cast(nc.scalar.copy, g, 0, WIDE, T)
+            cast(nc.scalar.copy, g, 0, SHARE[g], WIDE)
 
         def gather(g, u, a=0, b=S):
             nc.vector.tensor_copy(
@@ -227,7 +225,7 @@ def tile_moe_shr_lin_none_kernel(tc, xT, w_words, w_scales, gate, offs, out):
                 out=slot_codes_of(g, a, b).bitcast(FP8X4), scales=slot_scales[g][:, a:b], in_=slot_quads[g][:, 4 * a : 4 * b]
             )
 
-        def product(bank, e, g, codes, scales, closing=LAST):
+        def product(bank, e, g, order, codes, scales):
             plane = e * PASSES + g
             nc.tensor.matmul_mx(
                 out=bank,
@@ -235,16 +233,21 @@ def tile_moe_shr_lin_none_kernel(tc, xT, w_words, w_scales, gate, offs, out):
                 lhsT_scale=w_planes[:, plane * N : (plane + 1) * N],
                 rhs=codes.bitcast(FP8X4),
                 rhs_scale=scales,
-                start=(g == 0),
-                stop=(g == closing),
+                start=(g == order[0]),
+                stop=(g == order[-1]),
             )
 
-        def slot_product(i, g, closing=LAST):
-            a = GROUP * i
-            product(slot_banks[i][:], a // C, g, slot_codes_of(g, a, a + GROUP), slot_scales[g][:, a : a + GROUP], closing)
+        slot_orders = ((0, 1, 2, 3), (0, 1, 3, 2))
+        wide_order = (0, 2, 1, 3)
+        narrow_order = (3, 0, 1, 2)
 
-        def token_product(bank, g, a, b):
-            product(bank, E, g, token_codes_of(g, a, b), token_scales[g][:, a:b])
+        def slot_product(i, g):
+            a = GROUP * i
+            codes = slot_codes_of(g, a, a + GROUP)
+            product(slot_banks[i][:], a // C, g, slot_orders[a // C], codes, slot_scales[g][:, a : a + GROUP])
+
+        def token_product(bank, g, order, a, b):
+            product(bank, E, g, order, token_codes_of(g, a, b), token_scales[g][:, a:b])
 
         def empty_slot_banks(e):
             for i in range(2):
@@ -274,67 +277,67 @@ def tile_moe_shr_lin_none_kernel(tc, xT, w_words, w_scales, gate, offs, out):
         token_quads("gpsimd", 0, third, WIDE)
         quantize_tokens(0, 0, WIDE)
 
-        cast(nc.scalar.copy, 1, 0, 0, T // 2)
-        cast(nc.scalar.copy, 1, 0, T - GROUP, T)
-        cast(nc.scalar.copy, 1, 0, T // 2, T - GROUP)
-        gather(1, 0)
+        cast(nc.scalar.copy, 1, 1, 0, T // 2)
+        cast(nc.scalar.copy, 1, 1, T - GROUP, T)
+        cast(nc.scalar.copy, 1, 1, T // 2, T - GROUP)
+        gather(1, 1)
         slot_quads_on("scalar", 0, 0, S - GPSIMD_SLOTS)
         slot_quads_on("gpsimd", 0, S - GPSIMD_SLOTS, S)
         quantize_slots(0, 0, S)
-        cast(gpsimd_values, 1, 1, 0, FIRST_SHARE)
-        cast(nc.scalar.copy, 1, 1, FIRST_SHARE, WIDE)
-        cast(nc.scalar.copy, 1, 1, WIDE, T)
-        gather(1, 1)
+        shared_cast(1)
+        gather(1, 0)
+        token_quads("scalar", 1, WIDE, T)
         token_quads("gpsimd", 1, 0, WIDE - SCALAR_TOKENS)
         token_quads("scalar", 1, WIDE - SCALAR_TOKENS, WIDE)
+        quantize_tokens(1, WIDE, T)
         quantize_tokens(1, 0, WIDE)
 
-        cast(nc.scalar.copy, 2, 0, 0, T)
-        gather(2, 0)
-        shared_cast(2)
+        cast(nc.scalar.copy, 2, 1, 0, T)
         gather(2, 1)
-        token_quads("scalar", 1, WIDE, T)
+        shared_cast(2)
+        gather(2, 0)
+        token_quads("scalar", 2, WIDE, T)
         slot_quads_on("gpsimd", 1, 0, S)
-        quantize_tokens(1, WIDE, T)
+        quantize_tokens(2, WIDE, T)
         quantize_slots(1, 0, S)
 
-        cast(nc.scalar.copy, 3, 0, 0, T)
-        gather(3, 0)
+        cast(nc.scalar.copy, 3, 1, 0, T)
+        gather(3, 1)
         shared_cast(3)
-        gather(3, 1, 0, C)
-        gather(3, 1, C, S)
+        gather(3, 0, 0, C)
+        gather(3, 0, C, S)
         token_quads("scalar", 2, 0, WIDE)
         slot_quads_on("gpsimd", 2, 0, S)
-        slot_quads_on("scalar", 3, 0, C)
+        slot_quads_on("scalar", 3, 0, GROUP)
+        slot_quads_on("scalar", 3, GROUP, C)
         slot_quads_on("scalar", 3, C, S)
-        token_quads("scalar", 2, WIDE, T)
         token_quads("scalar", 3, WIDE, T)
         quantize_slots(2, 0, S)
-        quantize_slots(3, 0, C)
+        quantize_slots(3, 0, GROUP)
+        quantize_slots(3, GROUP, C)
         quantize_tokens(2, 0, WIDE)
         quantize_slots(3, C, S)
-        quantize_tokens(2, WIDE, T)
         quantize_tokens(3, WIDE, T)
         for e in range(E):
             for g in range(2):
                 for i in range(2):
-                    slot_product(2 * e + i, g, closing=None)
-        for e, order in enumerate(((2, 3), (3, 2))):
-            for g in order:
+                    slot_product(2 * e + i, g)
+        token_product(wide_bank[:], 0, wide_order, 0, WIDE)
+        for e in range(E):
+            for g in slot_orders[e][2:]:
                 for i in range(2):
-                    slot_product(2 * e + i, g, closing=order[-1])
+                    slot_product(2 * e + i, g)
 
         empty_slot_banks(0)
         scatter(0)
-        for g in range(LAST):
-            token_product(wide_bank[:], g, 0, WIDE)
-            token_product(narrow_bank[:, 0:GROUP], g, WIDE, WIDE + GROUP)
-        token_product(narrow_bank[:, 0:GROUP], LAST, WIDE, WIDE + GROUP)
-        for g in range(PASSES):
-            token_product(narrow_bank[:, GROUP:NARROW], g, WIDE + GROUP, T)
+        for g in wide_order[1:3]:
+            token_product(wide_bank[:], g, wide_order, 0, WIDE)
+        for i in range(2):
+            for g in narrow_order:
+                token_product(narrow_bank[:, GROUP * i : GROUP * (i + 1)], g, narrow_order, WIDE + GROUP * i, WIDE + GROUP * (i + 1))
         token_quads("scalar", LAST, 0, WIDE)
         quantize_tokens(LAST, 0, WIDE)
-        token_product(wide_bank[:], LAST, 0, WIDE)
+        token_product(wide_bank[:], LAST, wide_order, 0, WIDE)
         empty_slot_banks(1)
         scatter(1)
 

@@ -25,8 +25,8 @@ WIDE = 512
 NARROW = T - WIDE
 GROUP = 128
 HOLD = 16
-SHARE = {1: 256, 2: 288, 3: 288}
-SCALAR_TOKENS = 48
+SHARE = {1: 256, 2: 240, 3: 240}
+SCALAR_TOKENS = 80
 GPSIMD_SLOTS = 128
 
 
@@ -289,8 +289,8 @@ def tile_moe_shr_lin_none_kernel(tc, xT, w_words, w_scales, gate, offs, out):
         token_quads("scalar", 1, WIDE, T)
         token_quads("gpsimd", 1, 0, WIDE - SCALAR_TOKENS)
         token_quads("scalar", 1, WIDE - SCALAR_TOKENS, WIDE)
-        quantize_tokens(1, WIDE, T)
         quantize_tokens(1, 0, WIDE)
+        quantize_tokens(1, WIDE, T)
 
         cast(nc.scalar.copy, 2, 1, 0, T)
         gather(2, 1)

@@ -101,7 +101,8 @@ def tile_moe_shr_lin_none_kernel(tc, xT, w_words, w_scales, gate, offs, out):
         slot_pairs1_at = pairs0_at + 8 * T - 4 * HOLD
         slot_pairs3_at = slot_pairs1_at + 8 * S - 4 * HOLD
         pairs3_tile = keep.tile([P, front + 4 * T], BF16, name="pairs3", align_bytes=64)
-        slot_pairs3_tile = late.tile([P, front + 4 * S], BF16, name="slot_pairs3", align_bytes=64, offset=slot_pairs3_at)
+        front3 = 4 * S + front
+        slot_pairs3_tile = late.tile([P, front3 + 4 * S], BF16, name="slot_pairs3", align_bytes=64, offset=slot_pairs3_at)
         token_pairs = [
             late.tile([P, 4 * T], BF16, name="pairs0", align_bytes=64, offset=pairs0_at)[:],
             late.tile([P, 4 * T], BF16, name="pairs1", align_bytes=64, offset=pairs1_at)[:],
@@ -112,13 +113,13 @@ def tile_moe_shr_lin_none_kernel(tc, xT, w_words, w_scales, gate, offs, out):
             keep.tile([P, 4 * S], BF16, name="slot_pairs0", align_bytes=64)[:],
             late.tile([P, 4 * S], BF16, name="slot_pairs1", align_bytes=64, offset=slot_pairs1_at)[:],
             late.tile([P, 4 * S], BF16, name="slot_pairs2", align_bytes=64, offset=slot_pairs2_at)[:],
-            slot_pairs3_tile[:, front:],
+            slot_pairs3_tile[:, front3:],
         ]
         narrow_quads = [
             keep.tile([P, 4 * NARROW], BF16, name="narrow_quads0", align_bytes=64)[:],
             keep.tile([P, 4 * NARROW], BF16, name="narrow_quads1", align_bytes=64)[:],
             pairs3_tile[:, 0 : 4 * NARROW],
-            slot_pairs3_tile[:, 0 : 4 * NARROW],
+            slot_pairs3_tile[:, 4 * S : 4 * (S + NARROW)],
         ]
 
         def behind(g, u):
@@ -139,13 +140,12 @@ def tile_moe_shr_lin_none_kernel(tc, xT, w_words, w_scales, gate, offs, out):
             behind(1, 1),
             ahead_of(2, 0),
             ahead_of(3, 0),
-            keep.tile([P, 4 * S], BF16, name="slot_quads3", align_bytes=64)[:],
+            slot_pairs3_tile[:, 0 : 4 * S],
         ]
         narrow_codes = [
             keep.tile([P, NARROW], U32, name="narrow_codes0", align_bytes=64),
             late.tile([P, NARROW], U32, name="narrow_codes1", align_bytes=64, offset=narrow_codes1_at),
             late.tile([P, NARROW], U32, name="narrow_codes2", align_bytes=64, offset=slot_pairs1_at + 4 * HOLD),
-            late.tile([P, NARROW], U32, name="narrow_codes3", align_bytes=64, offset=narrow_codes3_at),
         ]
         wide_codes = [
             keep.tile([P, WIDE], U32, name="wide_codes0", align_bytes=64),
@@ -155,10 +155,11 @@ def tile_moe_shr_lin_none_kernel(tc, xT, w_words, w_scales, gate, offs, out):
         ]
         token_scales = [keep.tile([P, T], U8, name=f"token_scales{g}", align_bytes=64) for g in range(PASSES)]
         slot_codes = [keep.tile([P, S], U32, name=f"slot_codes{g}", align_bytes=64) for g in range(LAST)]
-        last_slot_codes = [
-            late.tile([P, C], U32, name=f"last_slot_codes{e}", align_bytes=64, offset=at) for e, at in enumerate((codes0_at, codes1_at))
-        ]
-        slot_scales = [keep.tile([P, S], U8, name=f"slot_scales{g}", align_bytes=64) for g in range(PASSES)]
+        first_codes = late.tile([P, C], U32, name="first_codes", align_bytes=64, offset=codes0_at)
+        joint_codes = late.tile([P, C + NARROW], U32, name="joint_codes", align_bytes=64, offset=codes1_at)
+        narrow_codes.append(joint_codes[:, C:])
+        slot_scales = [keep.tile([P, S], U8, name=f"slot_scales{g}", align_bytes=64) for g in range(LAST)]
+        slot_scales.append(keep.tile([P, S + NARROW], U8, name="last_scales", align_bytes=64))
 
         slot_banks = [psum.tile([P, GROUP], F32, name=f"slot_bank{i}", tag=f"bank{i}") for i in range(S // GROUP)]
         wide_bank = psum.tile([P, WIDE], F32, name="wide_bank")
@@ -178,7 +179,7 @@ def tile_moe_shr_lin_none_kernel(tc, xT, w_words, w_scales, gate, offs, out):
         def slot_codes_of(g, a, b):
             if g < LAST:
                 return slot_codes[g][:, a:b]
-            return last_slot_codes[a // C][:, a % C : a % C + b - a]
+            return (first_codes, joint_codes)[a // C][:, a % C : a % C + b - a]
 
         def gpsimd_values(out, in_):
             nc.gpsimd.tensor_scalar(out, in_, 1.0, 0.0, MULT, ADD)
@@ -215,6 +216,11 @@ def tile_moe_shr_lin_none_kernel(tc, xT, w_words, w_scales, gate, offs, out):
         def slot_quads_on(engine, g, a, b):
             copy_pairs(engine, slot_quads[g][:, 4 * a : 4 * b], slot_pairs[g], a, b)
 
+        def token_scales_of(g, a, b):
+            if g == LAST and a >= WIDE:
+                return slot_scales[LAST][:, S + a - WIDE : S + b - WIDE]
+            return token_scales[g][:, a:b]
+
         def quantize_tokens(g, a, b):
             nc.vector.quantize_mx(
                 out=token_codes_of(g, a, b).bitcast(FP8X4), scales=token_scales[g][:, a:b], in_=token_quads_of(g, a, b)
@@ -247,7 +253,7 @@ def tile_moe_shr_lin_none_kernel(tc, xT, w_words, w_scales, gate, offs, out):
             product(slot_banks[i][:], a // C, g, slot_orders[a // C], codes, slot_scales[g][:, a : a + GROUP])
 
         def token_product(bank, g, order, a, b):
-            product(bank, E, g, order, token_codes_of(g, a, b), token_scales[g][:, a:b])
+            product(bank, E, g, order, token_codes_of(g, a, b), token_scales_of(g, a, b))
 
         def empty_slot_banks(e):
             for i in range(2):
@@ -308,16 +314,15 @@ def tile_moe_shr_lin_none_kernel(tc, xT, w_words, w_scales, gate, offs, out):
         gather(3, 0, C, S)
         token_quads("scalar", 2, 0, WIDE)
         slot_quads_on("gpsimd", 2, 0, S)
-        slot_quads_on("scalar", 3, 0, GROUP)
-        slot_quads_on("scalar", 3, GROUP, C)
+        slot_quads_on("scalar", 3, 0, C)
         slot_quads_on("scalar", 3, C, S)
         token_quads("scalar", 3, WIDE, T)
         quantize_slots(2, 0, S)
-        quantize_slots(3, 0, GROUP)
-        quantize_slots(3, GROUP, C)
+        quantize_slots(3, 0, C)
         quantize_tokens(2, 0, WIDE)
-        quantize_slots(3, C, S)
-        quantize_tokens(3, WIDE, T)
+        nc.vector.quantize_mx(
+            out=joint_codes[:].bitcast(FP8X4), scales=slot_scales[LAST][:, C:], in_=slot_pairs3_tile[:, 4 * C : 4 * (S + NARROW)]
+        )
         for e in range(E):
             for g in range(2):
                 for i in range(2):

@@ -84,17 +84,15 @@ def tile_moe_shr_lin_none_kernel(tc, xT, w_words, w_scales, gate, offs, out):
             )
         w_view = w_words.rearrange("e a p b -> e p a b").bitcast(I32)
         gate_sb = keep.tile([P, S], F32, name="gate_sb")
-        for e in range(E):
+        for e in range(E + 1):
             nc.sync.dma_start(w_codes[e][:].bitcast(I32), w_view[e])
-        nc.sync.dma_start(w_codes[E][:].bitcast(I32), w_view[E])
         nc.sync.dma_start(gate_sb[:], gate)
 
         front = 4 * NARROW - 2 * HOLD
         codes0_at = 8 * WIDE - 4 * HOLD
         slot_pairs2_at = codes0_at + 4 * C - 4 * HOLD
-        codes1_at = slot_pairs2_at + 4 * HOLD
-        narrow_codes3_at = codes1_at + 4 * C
-        wide_codes2_at = narrow_codes3_at + 4 * NARROW
+        joint_codes_at = slot_pairs2_at + 4 * HOLD
+        wide_codes2_at = joint_codes_at + 4 * (C + NARROW)
         narrow_codes1_at = wide_codes2_at + 4 * WIDE
         pairs1_at = slot_pairs2_at
         pairs0_at = pairs1_at + 8 * T
@@ -115,9 +113,10 @@ def tile_moe_shr_lin_none_kernel(tc, xT, w_words, w_scales, gate, offs, out):
             late.tile([P, 4 * S], BF16, name="slot_pairs2", align_bytes=64, offset=slot_pairs2_at)[:],
             slot_pairs3_tile[:, front3:],
         ]
+        quads1 = keep.tile([P, 4 * T], BF16, name="quads1", align_bytes=64)
         narrow_quads = [
             keep.tile([P, 4 * NARROW], BF16, name="narrow_quads0", align_bytes=64)[:],
-            keep.tile([P, 4 * NARROW], BF16, name="narrow_quads1", align_bytes=64)[:],
+            quads1[:, 4 * WIDE :],
             pairs3_tile[:, 0 : 4 * NARROW],
             slot_pairs3_tile[:, 4 * S : 4 * (S + NARROW)],
         ]
@@ -132,7 +131,7 @@ def tile_moe_shr_lin_none_kernel(tc, xT, w_words, w_scales, gate, offs, out):
 
         wide_quads = [
             keep.tile([P, 4 * WIDE], BF16, name="wide_quads0", align_bytes=64)[:],
-            keep.tile([P, 4 * WIDE], BF16, name="wide_quads1", align_bytes=64)[:],
+            quads1[:, 0 : 4 * WIDE],
             behind(3, 0),
             late.tile([P, 4 * WIDE], BF16, name="wide_quads3", align_bytes=64, offset=0)[:],
         ]
@@ -156,7 +155,7 @@ def tile_moe_shr_lin_none_kernel(tc, xT, w_words, w_scales, gate, offs, out):
         token_scales = [keep.tile([P, T], U8, name=f"token_scales{g}", align_bytes=64) for g in range(PASSES)]
         slot_codes = [keep.tile([P, S], U32, name=f"slot_codes{g}", align_bytes=64) for g in range(LAST)]
         first_codes = late.tile([P, C], U32, name="first_codes", align_bytes=64, offset=codes0_at)
-        joint_codes = late.tile([P, C + NARROW], U32, name="joint_codes", align_bytes=64, offset=codes1_at)
+        joint_codes = late.tile([P, C + NARROW], U32, name="joint_codes", align_bytes=64, offset=joint_codes_at)
         narrow_codes.append(joint_codes[:, C:])
         slot_scales = [keep.tile([P, S], U8, name=f"slot_scales{g}", align_bytes=64) for g in range(LAST)]
         slot_scales.append(keep.tile([P, S + NARROW], U8, name="last_scales", align_bytes=64))
@@ -201,8 +200,8 @@ def tile_moe_shr_lin_none_kernel(tc, xT, w_words, w_scales, gate, offs, out):
                 token_pairs[g][:, 2 * u * T : 2 * (u + 1) * T].bitcast(U32).indirect(offsets[:, a // 16 : b // 16]),
             )
 
-        word_of = {"scalar": U32, "vector": I32, "gpsimd": I32}
-        copy_of = {"scalar": nc.scalar.copy, "vector": nc.vector.tensor_copy, "gpsimd": nc.gpsimd.tensor_copy}
+        word_of = {"scalar": U32, "gpsimd": I32}
+        copy_of = {"scalar": nc.scalar.copy, "gpsimd": nc.gpsimd.tensor_copy}
 
         def copy_pairs(engine, quads, pairs, a, b):
             copy_of[engine](
@@ -290,11 +289,13 @@ def tile_moe_shr_lin_none_kernel(tc, xT, w_words, w_scales, gate, offs, out):
         slot_quads_on("scalar", 0, 0, S - GPSIMD_SLOTS)
         slot_quads_on("gpsimd", 0, S - GPSIMD_SLOTS, S)
         quantize_slots(0, 0, S)
-        shared_cast(1)
+        cut = WIDE - SCALAR_TOKENS
+        cast(gpsimd_values, 1, 0, 0, SHARE[1])
+        cast(nc.scalar.copy, 1, 0, cut, T)
+        cast(nc.scalar.copy, 1, 0, SHARE[1], cut)
         gather(1, 0)
-        token_quads("scalar", 1, WIDE, T)
-        token_quads("gpsimd", 1, 0, WIDE - SCALAR_TOKENS)
-        token_quads("scalar", 1, WIDE - SCALAR_TOKENS, WIDE)
+        copy_pairs("scalar", quads1[:, 4 * cut :], token_pairs[1], cut, T)
+        token_quads("gpsimd", 1, 0, cut)
         quantize_tokens(1, 0, WIDE)
         quantize_tokens(1, WIDE, T)
 

@@ -12,6 +12,7 @@ FP8X4 = mybir.dt.float8_e4m3fn_x4
 FP4X4 = mybir.dt.float4_e2m1fn_x4
 MULT = mybir.AluOpType.mult
 ADD = mybir.AluOpType.add
+COPY = mybir.ActivationFunctionType.Copy
 
 P = 128
 K, T, E, C, N = 2048, 768, 2, 256, 128
@@ -20,14 +21,13 @@ PASSES = K // 512
 LAST = PASSES - 1
 FLOPS = 2 * K * N * (T + S)
 
-ROWS = 2 * T
-WIDE = 512
-NARROW = T - WIDE
-GROUP = 128
+THIRD = T // 3
+WIDE = 2 * THIRD
 HOLD = 16
-SHARE = {1: 256, 2: 240, 3: 240}
-SCALAR_TOKENS = 80
-GPSIMD_SLOTS = 128
+SC0 = 128
+SPLIT0 = 320
+GP0 = 192
+GP = 224
 
 
 def tile_moe_shr_lin_none_kernel(tc, xT, w_words, w_scales, gate, offs, out):
@@ -37,45 +37,61 @@ def tile_moe_shr_lin_none_kernel(tc, xT, w_words, w_scales, gate, offs, out):
         late = ctx.enter_context(tc.tile_pool(name="late", bufs=1))
         psum = ctx.enter_context(tc.psum_pool(name="psum", bufs=1))
 
-        x_view = xT.rearrange("(g p u e) w -> g u p e w", p=P, u=2, e=2)
         offsets = keep.tile([P, S // 16], U16, name="offsets")
-        room = 2 * S - HOLD
-        stream_at = {(1, 1): 0, (1, 0): ROWS + room}
-        pairs2_at = stream_at[1, 0] + T + SHARE[1] - HOLD
-        stream_at[2, 1] = pairs2_at + 2 * T
-        stream_at[2, 0] = stream_at[2, 1] + ROWS + room
-        stream_at[3, 1] = stream_at[2, 0] + ROWS
-        stream_at[3, 0] = stream_at[3, 1] + ROWS + room
-        stream = keep.tile([P, stream_at[3, 0] + ROWS + room], F32, name="stream", align_bytes=64)
 
-        third = T // 3
-        narrow_rows = keep.tile([P, 4, NARROW], F32, name="narrow_rows", align_bytes=64)
-        nc.sync.dma_start(narrow_rows[:], xT[0:512, WIDE:T].rearrange("(p t) w -> p t w", t=4))
-        loaded = {(0, u, WIDE): narrow_rows[:, 2 * u : 2 * u + 2, :] for u in range(2)}
-        for u, a, b in ((0, 0, WIDE), (1, 0, third), (1, third, WIDE)):
-            piece = keep.tile([P, 2, b - a], F32, name=f"first{u}_{a}", align_bytes=64)[:]
-            nc.sync.dma_start(piece, x_view[0, u, :, :, a:b])
-            loaded[0, u, a] = piece
-            if u == 0:
-                nc.sync.dma_start(offsets[:], offs)
+        def chain(name, sizes):
+            tile = keep.tile([P, sum(sizes) - HOLD * (len(sizes) - 1)], F32, name=name, align_bytes=64)
+            starts = [sum(sizes[:i]) - HOLD * i for i in range(len(sizes))]
+            return [tile[:, a : a + n] for a, n in zip(starts, sizes)]
+
+        def words(name, n):
+            return keep.tile([P, n], F32, name=name, align_bytes=64)[:]
+
+        def two_rows(x):
+            return x.rearrange("p (u w) -> p u w", u=2)
+
+        middle_pairs = words("middle_pairs", 4 * T)
+        token_pairs = [two_rows(x) for x in (words("pairs0", 2 * T), middle_pairs[:, 0 : 2 * T], middle_pairs[:, 2 * T :], words("pairs3", 2 * T))]
+        step3 = S - HOLD + 4 * WIDE
+        tail = words("tail", 2 * step3)
+        quads_b = tail[:, S - HOLD : step3]
+        quads_c = tail[:, step3 + S - HOLD : step3 + S - HOLD + 2 * WIDE]
+        slot_pairs = [two_rows(words(f"slot_pairs{g}", 2 * S)) for g in range(LAST)] + [two_rows(tail)[:, :, 0:S]]
+        early_quads = words("early_quads", 2 * THIRD)
+        quads0 = words("quads0", 2 * WIDE)
+        firsts = {g: words(f"first{g}", 2 * T) for g in range(1, PASSES)}
+        seconds, slot_quads = {0: words("second0", 2 * WIDE)}, {}
+        for g in range(1, LAST):
+            slot_quads[g - 1], seconds[g] = chain(f"second{g}", [2 * S, 2 * T])
+        slot_quads[LAST - 1], seconds[LAST], quads_a = chain("second3", [2 * S, 2 * T, 2 * WIDE])
+        slot_quads[LAST] = words("slot_quads3", 2 * S)
+        late_quads = [quads_a, quads_b, quads_c, words("quads_d", 2 * THIRD)]
+        late_thirds = [[(1, 1), (2, 1)], [(1, 2), (2, 2), (1, 0), (2, 0)], [(3, 1), (3, 2)], [(3, 0)]]
+        late_at = {key: (n, THIRD * j) for n, keys in enumerate(late_thirds) for j, key in enumerate(keys)}
+
+        x_view = xT.rearrange("(g p u e) w -> g u p e w", p=P, u=2, e=2)
+        early_rows = keep.tile([P, 4, THIRD], F32, name="early_rows", align_bytes=64)
+        nc.sync.dma_start(early_rows[:], xT[0:512, WIDE:T].rearrange("(p t) w -> p t w", t=4))
+        first0 = keep.tile([P, 2, T - THIRD], F32, name="first0", align_bytes=64)
+        nc.sync.dma_start(first0[:], x_view[0, 1, :, :, 0:WIDE])
+        nc.sync.dma_start(offsets[:], offs)
+        second0 = two_rows(seconds[0])
+        nc.sync.dma_start(second0, x_view[0, 0, :, :, 0:WIDE])
+        loaded = {(0, 1): first0[:], (0, 0): second0}
         for g in range(1, PASSES):
+            loaded[g, 1] = two_rows(firsts[g])
+            loaded[g, 0] = two_rows(seconds[g])
             for u in (1, 0):
-                both_rows = stream[:, stream_at[g, u] : stream_at[g, u] + ROWS].rearrange("p (e w) -> p e w", e=2)
-                edges = (0, T // 2, T) if (g, u) == (1, 1) else (0, T)
-                for a, b in zip(edges, edges[1:]):
-                    nc.sync.dma_start(both_rows[:, :, a:b], x_view[g, u, :, :, a:b])
-                loaded[g, u, 0] = both_rows
-
-        def rows(g, u, a, b):
-            first = max(c for (i, j, c) in loaded if (i, j) == (g, u) and c <= a)
-            return loaded[g, u, first][:, :, a - first : b - first]
+                nc.sync.dma_start(loaded[g, u], x_view[g, u])
 
         w_planes = keep.tile([P, (E + 1) * PASSES * N], U8, name="w_planes", align_bytes=64)
-        nc.gpsimd.memset(w_planes[:].bitcast(I32), 0)
+        nc.vector.memset(w_planes[:].bitcast(I32), 0)
         window = keep.tile([P, T], F32, name="window")
-        nc.gpsimd.memset(window[:], 0.0)
+        nc.vector.memset(window[:], 0.0)
 
         w_codes = [keep.tile([P, PASSES, 2 * N], U8, name=f"w_codes{e}", align_bytes=64) for e in range(E + 1)]
+        gate_sb = keep.tile([P, S], F32, name="gate_sb")
+        nc.sync.dma_start(gate_sb[:], gate)
         scale_rows = w_scales.rearrange("e a q n -> q (e a) n")
         for quadrant in range(4):
             nc.sync.dma_start(
@@ -83,271 +99,173 @@ def tile_moe_shr_lin_none_kernel(tc, xT, w_words, w_scales, gate, offs, out):
                 scale_rows[4 * quadrant : 4 * quadrant + 4].bitcast(I32),
             )
         w_view = w_words.rearrange("e a p b -> e p a b").bitcast(I32)
-        gate_sb = keep.tile([P, S], F32, name="gate_sb")
-        for e in range(E + 1):
+        for e in (1, 0, E):
             nc.sync.dma_start(w_codes[e][:].bitcast(I32), w_view[e])
-        nc.sync.dma_start(gate_sb[:], gate)
 
-        front = 4 * NARROW - 2 * HOLD
-        codes0_at = 8 * WIDE - 4 * HOLD
-        slot_pairs2_at = codes0_at + 4 * C - 4 * HOLD
-        joint_codes_at = slot_pairs2_at + 4 * HOLD
-        wide_codes2_at = joint_codes_at + 4 * (C + NARROW)
-        narrow_codes1_at = wide_codes2_at + 4 * WIDE
-        pairs1_at = slot_pairs2_at
-        pairs0_at = pairs1_at + 8 * T
-        slot_pairs1_at = pairs0_at + 8 * T - 4 * HOLD
-        slot_pairs3_at = slot_pairs1_at + 8 * S - 4 * HOLD
-        pairs3_tile = keep.tile([P, front + 4 * T], BF16, name="pairs3", align_bytes=64)
-        front3 = 4 * S + front
-        slot_pairs3_tile = late.tile([P, front3 + 4 * S], BF16, name="slot_pairs3", align_bytes=64, offset=slot_pairs3_at)
-        token_pairs = [
-            late.tile([P, 4 * T], BF16, name="pairs0", align_bytes=64, offset=pairs0_at)[:],
-            late.tile([P, 4 * T], BF16, name="pairs1", align_bytes=64, offset=pairs1_at)[:],
-            stream[:, pairs2_at : pairs2_at + 2 * T].bitcast(BF16),
-            pairs3_tile[:, front:],
-        ]
-        slot_pairs = [
-            keep.tile([P, 4 * S], BF16, name="slot_pairs0", align_bytes=64)[:],
-            late.tile([P, 4 * S], BF16, name="slot_pairs1", align_bytes=64, offset=slot_pairs1_at)[:],
-            late.tile([P, 4 * S], BF16, name="slot_pairs2", align_bytes=64, offset=slot_pairs2_at)[:],
-            slot_pairs3_tile[:, front3:],
-        ]
-        quads1 = keep.tile([P, 4 * T], BF16, name="quads1", align_bytes=64)
-        narrow_quads = [
-            keep.tile([P, 4 * NARROW], BF16, name="narrow_quads0", align_bytes=64)[:],
-            quads1[:, 4 * WIDE :],
-            pairs3_tile[:, 0 : 4 * NARROW],
-            slot_pairs3_tile[:, 4 * S : 4 * (S + NARROW)],
+        def placed(name, n, dtype, at):
+            if at is None:
+                return keep.tile([P, n], dtype, name=name, align_bytes=64)
+            return late.tile([P, n], dtype, name=name, align_bytes=64, offset=at)
+
+        def operand(name, n, codes_at=None, scales_at=None):
+            return placed(name + "_codes", n, U32, codes_at), placed(name + "_scales", n, U8, scales_at)
+
+        early0 = operand("early0", THIRD)
+        rest0 = operand("rest0", T - THIRD)
+        slots = [operand(f"slots{g}", S) for g in range(LAST)]
+        last0_at, last1_at = 4096, 1024
+        last = [operand("last0", C, last0_at), operand("last1", C, last1_at)]
+        lates = [
+            operand("late_a", WIDE, None, last1_at + 4 * HOLD),
+            operand("late_b", 2 * WIDE, None, last0_at - 2 * WIDE + 4 * HOLD),
+            operand("late_c", WIDE, None, last0_at + 4 * HOLD),
+            operand("late_d", THIRD, None, last0_at + 4 * HOLD + WIDE),
         ]
 
-        def behind(g, u):
-            start = stream_at[g, u] + ROWS - HOLD
-            return stream[:, start : start + 2 * S].bitcast(BF16)
+        def token_operand(g, i):
+            if g == 0:
+                (codes, scales), a = (early0, 0) if i == 2 else (rest0, THIRD * i)
+            else:
+                n, a = late_at[g, i]
+                codes, scales = lates[n]
+            return codes[:, a : a + THIRD], scales[:, a : a + THIRD]
 
-        def ahead_of(g, u):
-            end = stream_at[g, u] + HOLD
-            return stream[:, end - 2 * S : end].bitcast(BF16)
+        def slot_operand(g, e):
+            (codes, scales), a = (slots[g], e * C) if g < LAST else (last[e], 0)
+            return codes[:, a : a + C], scales[:, a : a + C]
 
-        wide_quads = [
-            keep.tile([P, 4 * WIDE], BF16, name="wide_quads0", align_bytes=64)[:],
-            quads1[:, 0 : 4 * WIDE],
-            behind(3, 0),
-            late.tile([P, 4 * WIDE], BF16, name="wide_quads3", align_bytes=64, offset=0)[:],
-        ]
-        slot_quads = [
-            behind(1, 1),
-            ahead_of(2, 0),
-            ahead_of(3, 0),
-            slot_pairs3_tile[:, 0 : 4 * S],
-        ]
-        narrow_codes = [
-            keep.tile([P, NARROW], U32, name="narrow_codes0", align_bytes=64),
-            late.tile([P, NARROW], U32, name="narrow_codes1", align_bytes=64, offset=narrow_codes1_at),
-            late.tile([P, NARROW], U32, name="narrow_codes2", align_bytes=64, offset=slot_pairs1_at + 4 * HOLD),
-        ]
-        wide_codes = [
-            keep.tile([P, WIDE], U32, name="wide_codes0", align_bytes=64),
-            keep.tile([P, WIDE], U32, name="wide_codes1", align_bytes=64),
-            late.tile([P, WIDE], U32, name="wide_codes2", align_bytes=64, offset=wide_codes2_at),
-            keep.tile([P, WIDE], U32, name="wide_codes3", align_bytes=64),
-        ]
-        token_scales = [keep.tile([P, T], U8, name=f"token_scales{g}", align_bytes=64) for g in range(PASSES)]
-        slot_codes = [keep.tile([P, S], U32, name=f"slot_codes{g}", align_bytes=64) for g in range(LAST)]
-        first_codes = late.tile([P, C], U32, name="first_codes", align_bytes=64, offset=codes0_at)
-        joint_codes = late.tile([P, C + NARROW], U32, name="joint_codes", align_bytes=64, offset=joint_codes_at)
-        narrow_codes.append(joint_codes[:, C:])
-        slot_scales = [keep.tile([P, S], U8, name=f"slot_scales{g}", align_bytes=64) for g in range(LAST)]
-        slot_scales.append(keep.tile([P, S + NARROW], U8, name="last_scales", align_bytes=64))
-
-        slot_banks = [psum.tile([P, GROUP], F32, name=f"slot_bank{i}", tag=f"bank{i}") for i in range(S // GROUP)]
-        wide_bank = psum.tile([P, WIDE], F32, name="wide_bank")
-        narrow_bank = psum.tile([P, NARROW], F32, name="narrow_bank")
-        y_sb = [keep.tile([P, C], F32, name=f"y_sb{e}") for e in range(E)]
-
-        def token_quads_of(g, a, b):
-            if a < WIDE:
-                return wide_quads[g][:, 4 * a : 4 * b]
-            return narrow_quads[g][:, 4 * (a - WIDE) : 4 * (b - WIDE)]
-
-        def token_codes_of(g, a, b):
-            if a < WIDE:
-                return wide_codes[g][:, a:b]
-            return narrow_codes[g][:, a - WIDE : b - WIDE]
-
-        def slot_codes_of(g, a, b):
-            if g < LAST:
-                return slot_codes[g][:, a:b]
-            return (first_codes, joint_codes)[a // C][:, a % C : a % C + b - a]
-
-        def gpsimd_values(out, in_):
-            nc.gpsimd.tensor_scalar(out, in_, 1.0, 0.0, MULT, ADD)
+        slot_banks = [psum.tile([P, C], F32, name=f"slot_bank{e}") for e in range(E)]
+        token_banks = [psum.tile([P, THIRD], F32, name=f"token_bank{i}") for i in range(3)]
+        gated = [keep.tile([P, C], F32, name=f"gated{e}") for e in range(E)]
 
         def cast(copy, g, u, a, b):
             copy(
-                out=token_pairs[g][:, 2 * (u * T + a) : 2 * (u * T + b)].rearrange("p (w e) -> p w e", e=2),
-                in_=rows(g, u, a, b).rearrange("p e w -> p w e"),
+                out=token_pairs[g][:, u, a:b].bitcast(BF16).rearrange("p (w e) -> p w e", e=2),
+                in_=loaded[g, u][:, :, a:b].rearrange("p e w -> p w e"),
             )
-
-        def shared_cast(g):
-            cast(gpsimd_values, g, 0, 0, SHARE[g])
-            cast(nc.scalar.copy, g, 0, WIDE, T)
-            cast(nc.scalar.copy, g, 0, SHARE[g], WIDE)
 
         def gather(g, u, a=0, b=S):
             nc.vector.tensor_copy(
-                slot_pairs[g].bitcast(U32).rearrange("p (u w) -> p u w", u=2)[:, u, a:b],
-                token_pairs[g][:, 2 * u * T : 2 * (u + 1) * T].bitcast(U32).indirect(offsets[:, a // 16 : b // 16]),
+                slot_pairs[g][:, u, a:b].bitcast(U32),
+                token_pairs[g][:, u, :].bitcast(U32).indirect(offsets[:, a // 16 : b // 16]),
             )
 
-        word_of = {"scalar": U32, "gpsimd": I32}
-        copy_of = {"scalar": nc.scalar.copy, "gpsimd": nc.gpsimd.tensor_copy}
+        word_of = {"scalar": U32, "gpsimd": I32, "vector": I32}
+        copy_of = {"scalar": nc.scalar.copy, "gpsimd": nc.gpsimd.tensor_copy, "vector": nc.vector.tensor_copy}
 
         def copy_pairs(engine, quads, pairs, a, b):
             copy_of[engine](
                 out=quads.bitcast(word_of[engine]).rearrange("p (w u) -> p w u", u=2),
-                in_=pairs.bitcast(word_of[engine]).rearrange("p (u w) -> p w u", u=2)[:, a:b],
+                in_=pairs[:, :, a:b].bitcast(word_of[engine]).rearrange("p u w -> p w u"),
             )
 
         def token_quads(engine, g, a, b):
-            copy_pairs(engine, token_quads_of(g, a, b), token_pairs[g], a, b)
+            if g == 0:
+                quads = quads0[:, 2 * a : 2 * b]
+            else:
+                n, at = late_at[g, a // THIRD]
+                at += a % THIRD
+                quads = late_quads[n][:, 2 * at : 2 * (at + b - a)]
+            copy_pairs(engine, quads, token_pairs[g], a, b)
 
-        def slot_quads_on(engine, g, a, b):
-            copy_pairs(engine, slot_quads[g][:, 4 * a : 4 * b], slot_pairs[g], a, b)
+        def quantize(target, quads):
+            nc.vector.quantize_mx(out=target[0][:].bitcast(FP8X4), scales=target[1][:], in_=quads.bitcast(BF16))
 
-        def token_scales_of(g, a, b):
-            if g == LAST and a >= WIDE:
-                return slot_scales[LAST][:, S + a - WIDE : S + b - WIDE]
-            return token_scales[g][:, a:b]
-
-        def quantize_tokens(g, a, b):
-            nc.vector.quantize_mx(
-                out=token_codes_of(g, a, b).bitcast(FP8X4), scales=token_scales[g][:, a:b], in_=token_quads_of(g, a, b)
-            )
-
-        def quantize_slots(g, a, b):
-            nc.vector.quantize_mx(
-                out=slot_codes_of(g, a, b).bitcast(FP8X4), scales=slot_scales[g][:, a:b], in_=slot_quads[g][:, 4 * a : 4 * b]
-            )
-
-        def product(bank, e, g, order, codes, scales):
+        def product(bank, e, g, order, moving):
             plane = e * PASSES + g
             nc.tensor.matmul_mx(
-                out=bank,
+                out=bank[:],
                 lhsT=w_codes[e][:, g, :].bitcast(FP4X4),
                 lhsT_scale=w_planes[:, plane * N : (plane + 1) * N],
-                rhs=codes.bitcast(FP8X4),
-                rhs_scale=scales,
+                rhs=moving[0].bitcast(FP8X4),
+                rhs_scale=moving[1],
                 start=(g == order[0]),
                 stop=(g == order[-1]),
             )
 
-        slot_orders = ((0, 1, 2, 3), (0, 1, 3, 2))
-        wide_order = (0, 2, 1, 3)
-        narrow_order = (3, 0, 1, 2)
+        def slot_product(e, g):
+            product(slot_banks[e], e, g, (0, 1, 2, 3), slot_operand(g, e))
 
-        def slot_product(i, g):
-            a = GROUP * i
-            codes = slot_codes_of(g, a, a + GROUP)
-            product(slot_banks[i][:], a // C, g, slot_orders[a // C], codes, slot_scales[g][:, a : a + GROUP])
+        token_order = ((0, 1, 2, 3), (1, 2, 0, 3), (0, 1, 2, 3))
 
-        def token_product(bank, g, order, a, b):
-            product(bank, E, g, order, token_codes_of(g, a, b), token_scales_of(g, a, b))
+        def token_product(i, g):
+            product(token_banks[i], E, g, token_order[i], token_operand(g, i))
 
-        def empty_slot_banks(e):
-            for i in range(2):
-                nc.scalar.copy(out=y_sb[e][:, GROUP * i : GROUP * (i + 1)], in_=slot_banks[2 * e + i][:])
+        def times_gate(e):
+            nc.vector.tensor_tensor(gated[e][:], slot_banks[e][:], gate_sb[:, e * C : (e + 1) * C], MULT)
 
         def scatter(e):
-            nc.vector.tensor_tensor(
-                window[:].indirect(offsets[:, e * (C // 16) : (e + 1) * (C // 16)]),
-                y_sb[e][:],
-                gate_sb[:, e * C : (e + 1) * C],
-                MULT,
+            nc.scalar.activation(window[:].indirect(offsets[:, e * (C // 16) : (e + 1) * (C // 16)]), gated[e][:], COPY)
+
+        nc.scalar.copy(
+            out=token_pairs[0][:, :, WIDE:T].bitcast(BF16).rearrange("p u (w e) -> p u w e", e=2),
+            in_=early_rows[:].rearrange("p (u e) w -> p u w e", u=2),
+        )
+        nc.vector.tensor_copy(
+            out=early_quads.bitcast(BF16).rearrange("p (w t) -> p w t", t=4), in_=early_rows[:].rearrange("p t w -> p w t")
+        )
+        cast(nc.scalar.copy, 0, 1, 0, SC0)
+        cast(nc.vector.tensor_copy, 0, 1, SC0, WIDE)
+        quantize(early0, early_quads)
+        gather(0, 1)
+        cast(nc.gpsimd.tensor_copy, 0, 0, 0, GP0)
+        cast(nc.scalar.copy, 0, 0, SPLIT0, WIDE)
+        cast(nc.scalar.copy, 0, 0, GP0, SPLIT0)
+        gather(0, 0)
+        token_quads("scalar", 0, SPLIT0, WIDE)
+        token_quads("gpsimd", 0, 0, SPLIT0)
+
+        quantize(rest0, quads0)
+
+        def slot_quads_on(engine, g, a, b):
+            copy_pairs(engine, slot_quads[g][:, 2 * a : 2 * b], slot_pairs[g], a, b)
+
+        for g in range(1, PASSES):
+            cast(nc.scalar.copy, g, 1, 0, T)
+            gather(g, 1)
+            cast(nc.gpsimd.tensor_copy, g, 0, 0, GP)
+            cast(nc.scalar.copy, g, 0, GP, T)
+            if g < LAST:
+                gather(g, 0)
+            else:
+                gather(g, 0, C, S)
+                gather(g, 0, 0, C)
+            slot_quads_on("gpsimd", g - 1, 0, S)
+            token_quads("gpsimd", g, 0, THIRD)
+            quantize(slots[g - 1], slot_quads[g - 1])
+
+        def middle_quads(quads, a):
+            nc.scalar.copy(
+                out=quads.bitcast(U32).rearrange("p (g w u) -> p g w u", g=2, u=2),
+                in_=middle_pairs.bitcast(U32).rearrange("p (g u w) -> p g w u", g=2, u=2)[:, :, a : a + THIRD],
             )
 
-        cast(nc.scalar.copy, 0, 0, WIDE, T)
-        cast(nc.scalar.copy, 0, 1, WIDE, T)
-        nc.vector.tensor_copy(
-            out=narrow_quads[0].rearrange("p (w t) -> p w t", t=4), in_=narrow_rows[:].rearrange("p t w -> p w t")
-        )
-        cast(nc.scalar.copy, 0, 0, 0, third)
-        cast(nc.vector.tensor_copy, 0, 0, third, WIDE)
-        quantize_tokens(0, WIDE, T)
-        gather(0, 0)
-        cast(nc.scalar.copy, 0, 1, 0, third)
-        cast(nc.scalar.copy, 0, 1, third, WIDE)
-        gather(0, 1)
-        token_quads("gpsimd", 0, 0, third)
-        token_quads("gpsimd", 0, third, WIDE)
-        quantize_tokens(0, 0, WIDE)
+        middle_quads(quads_a, THIRD)
+        slot_quads_on("scalar", LAST, C, S)
+        slot_quads_on("scalar", LAST, 0, C)
+        middle_quads(quads_b[:, 0 : 2 * WIDE], WIDE)
+        quantize(last[1], slot_quads[LAST][:, 2 * C :])
+        token_quads("vector", LAST, THIRD, T)
+        quantize(last[0], slot_quads[LAST][:, 0 : 2 * C])
+        for g in range(LAST):
+            for e in (1, 0):
+                slot_product(e, g)
+        for e in (1, 0):
+            slot_product(e, LAST)
 
-        cast(nc.scalar.copy, 1, 1, 0, T // 2)
-        cast(nc.scalar.copy, 1, 1, T - GROUP, T)
-        cast(nc.scalar.copy, 1, 1, T // 2, T - GROUP)
-        gather(1, 1)
-        slot_quads_on("scalar", 0, 0, S - GPSIMD_SLOTS)
-        slot_quads_on("gpsimd", 0, S - GPSIMD_SLOTS, S)
-        quantize_slots(0, 0, S)
-        cut = WIDE - SCALAR_TOKENS
-        cast(gpsimd_values, 1, 0, 0, SHARE[1])
-        cast(nc.scalar.copy, 1, 0, cut, T)
-        cast(nc.scalar.copy, 1, 0, SHARE[1], cut)
-        gather(1, 0)
-        copy_pairs("scalar", quads1[:, 4 * cut :], token_pairs[1], cut, T)
-        token_quads("gpsimd", 1, 0, cut)
-        quantize_tokens(1, 0, WIDE)
-        quantize_tokens(1, WIDE, T)
-
-        cast(nc.scalar.copy, 2, 1, 0, T)
-        gather(2, 1)
-        shared_cast(2)
-        gather(2, 0)
-        token_quads("scalar", 2, WIDE, T)
-        slot_quads_on("gpsimd", 1, 0, S)
-        quantize_tokens(2, WIDE, T)
-        quantize_slots(1, 0, S)
-
-        cast(nc.scalar.copy, 3, 1, 0, T)
-        gather(3, 1)
-        shared_cast(3)
-        gather(3, 0, 0, C)
-        gather(3, 0, C, S)
-        token_quads("scalar", 2, 0, WIDE)
-        slot_quads_on("gpsimd", 2, 0, S)
-        slot_quads_on("scalar", 3, 0, C)
-        slot_quads_on("scalar", 3, C, S)
-        token_quads("scalar", 3, WIDE, T)
-        quantize_slots(2, 0, S)
-        quantize_slots(3, 0, C)
-        quantize_tokens(2, 0, WIDE)
-        nc.vector.quantize_mx(
-            out=joint_codes[:].bitcast(FP8X4), scales=slot_scales[LAST][:, C:], in_=slot_pairs3_tile[:, 4 * C : 4 * (S + NARROW)]
-        )
-        for e in range(E):
-            for g in range(2):
-                for i in range(2):
-                    slot_product(2 * e + i, g)
-        token_product(wide_bank[:], 0, wide_order, 0, WIDE)
-        for e in range(E):
-            for g in slot_orders[e][2:]:
-                for i in range(2):
-                    slot_product(2 * e + i, g)
-
-        empty_slot_banks(0)
-        scatter(0)
-        for g in wide_order[1:3]:
-            token_product(wide_bank[:], g, wide_order, 0, WIDE)
-        for i in range(2):
-            for g in narrow_order:
-                token_product(narrow_bank[:, GROUP * i : GROUP * (i + 1)], g, narrow_order, WIDE + GROUP * i, WIDE + GROUP * (i + 1))
-        token_quads("scalar", LAST, 0, WIDE)
-        quantize_tokens(LAST, 0, WIDE)
-        token_product(wide_bank[:], LAST, wide_order, 0, WIDE)
-        empty_slot_banks(1)
+        times_gate(1)
         scatter(1)
+        quantize(lates[0], late_quads[0])
+        times_gate(0)
+        scatter(0)
+        quantize(lates[1], late_quads[1])
+        quantize(lates[2], late_quads[2])
+        quantize(lates[3], late_quads[3])
+        for g, i in late_thirds[0] + [(0, i) for i in range(3)] + late_thirds[1] + late_thirds[2] + late_thirds[3]:
+            token_product(i, g)
 
         result = keep.tile([P, T], F32, name="result")
-        for sums, a in ((wide_bank[:, 0:third], 0), (wide_bank[:, third:WIDE], third), (narrow_bank[:], WIDE)):
-            nc.vector.tensor_tensor(result[:, a : a + third], sums, window[:, a : a + third], ADD)
-            nc.sync.dma_start(out[:, a : a + third], result[:, a : a + third])
+        for i in (1, 2, 0):
+            cols = slice(THIRD * i, THIRD * (i + 1))
+            nc.vector.tensor_tensor(result[:, cols], token_banks[i][:], window[:, cols], ADD)
+            nc.sync.dma_start(out[:, cols], result[:, cols])

@@ -24,9 +24,9 @@ FLOPS = 2 * K * N * (T + S)
 THIRD = T // 3
 WIDE = 2 * THIRD
 HOLD = 16
-SC0 = 128
-SPLIT0 = 320
-GP0 = 192
+HEAD_A = (0, 512)
+HEAD_B = (192, 448)
+SPLIT0 = 448
 GP = 224
 
 
@@ -57,10 +57,9 @@ def tile_moe_shr_lin_none_kernel(tc, xT, w_words, w_scales, gate, offs, out):
         quads_b = tail[:, S - HOLD : step3]
         quads_c = tail[:, step3 + S - HOLD : step3 + S - HOLD + 2 * WIDE]
         slot_pairs = [two_rows(words(f"slot_pairs{g}", 2 * S)) for g in range(LAST)] + [two_rows(tail)[:, :, 0:S]]
-        early_quads = words("early_quads", 2 * THIRD)
-        quads0 = words("quads0", 2 * WIDE)
-        firsts = {g: words(f"first{g}", 2 * T) for g in range(1, PASSES)}
-        seconds, slot_quads = {0: words("second0", 2 * WIDE)}, {}
+        quads0 = words("quads0", 2 * T)
+        firsts = {g: words(f"first{g}", 2 * T) for g in range(PASSES)}
+        seconds, slot_quads = {0: words("second0", 2 * T)}, {}
         for g in range(1, LAST):
             slot_quads[g - 1], seconds[g] = chain(f"second{g}", [2 * S, 2 * T])
         slot_quads[LAST - 1], seconds[LAST], quads_a = chain("second3", [2 * S, 2 * T, 2 * WIDE])
@@ -70,19 +69,13 @@ def tile_moe_shr_lin_none_kernel(tc, xT, w_words, w_scales, gate, offs, out):
         late_at = {key: (n, THIRD * j) for n, keys in enumerate(late_thirds) for j, key in enumerate(keys)}
 
         x_view = xT.rearrange("(g p u e) w -> g u p e w", p=P, u=2, e=2)
-        early_rows = keep.tile([P, 4, THIRD], F32, name="early_rows", align_bytes=64)
-        nc.sync.dma_start(early_rows[:], xT[0:512, WIDE:T].rearrange("(p t) w -> p t w", t=4))
-        first0 = keep.tile([P, 2, T - THIRD], F32, name="first0", align_bytes=64)
-        nc.sync.dma_start(first0[:], x_view[0, 1, :, :, 0:WIDE])
-        nc.sync.dma_start(offsets[:], offs)
-        second0 = two_rows(seconds[0])
-        nc.sync.dma_start(second0, x_view[0, 0, :, :, 0:WIDE])
-        loaded = {(0, 1): first0[:], (0, 0): second0}
-        for g in range(1, PASSES):
-            loaded[g, 1] = two_rows(firsts[g])
-            loaded[g, 0] = two_rows(seconds[g])
+        loaded = {}
+        for g in range(PASSES):
+            loaded[g, 1], loaded[g, 0] = two_rows(firsts[g]), two_rows(seconds[g])
             for u in (1, 0):
                 nc.sync.dma_start(loaded[g, u], x_view[g, u])
+                if (g, u) == (0, 1):
+                    nc.sync.dma_start(offsets[:], offs)
 
         w_planes = keep.tile([P, (E + 1) * PASSES * N], U8, name="w_planes", align_bytes=64)
         nc.vector.memset(w_planes[:].bitcast(I32), 0)
@@ -197,25 +190,16 @@ def tile_moe_shr_lin_none_kernel(tc, xT, w_words, w_scales, gate, offs, out):
         def scatter(e):
             nc.scalar.activation(window[:].indirect(offsets[:, e * (C // 16) : (e + 1) * (C // 16)]), gated[e][:], COPY)
 
-        nc.scalar.copy(
-            out=token_pairs[0][:, :, WIDE:T].bitcast(BF16).rearrange("p u (w e) -> p u w e", e=2),
-            in_=early_rows[:].rearrange("p (u e) w -> p u w e", u=2),
-        )
-        nc.vector.tensor_copy(
-            out=early_quads.bitcast(BF16).rearrange("p (w t) -> p w t", t=4), in_=early_rows[:].rearrange("p t w -> p w t")
-        )
-        cast(nc.scalar.copy, 0, 1, 0, SC0)
-        cast(nc.vector.tensor_copy, 0, 1, SC0, WIDE)
-        quantize(early0, early_quads)
-        gather(0, 1)
-        cast(nc.gpsimd.tensor_copy, 0, 0, 0, GP0)
-        cast(nc.scalar.copy, 0, 0, SPLIT0, WIDE)
-        cast(nc.scalar.copy, 0, 0, GP0, SPLIT0)
-        gather(0, 0)
-        token_quads("scalar", 0, SPLIT0, WIDE)
+        for u, (a, b) in ((1, HEAD_A), (0, HEAD_B)):
+            if a:
+                cast(nc.gpsimd.tensor_copy, 0, u, 0, a)
+            cast(nc.vector.tensor_copy, 0, u, a, b)
+            cast(nc.scalar.copy, 0, u, b, T)
+            gather(0, u)
+        token_quads("scalar", 0, SPLIT0, T)
         token_quads("gpsimd", 0, 0, SPLIT0)
-
-        quantize(rest0, quads0)
+        quantize(early0, quads0[:, 2 * WIDE :])
+        quantize(rest0, quads0[:, 0 : 2 * WIDE])
 
         def slot_quads_on(engine, g, a, b):
             copy_pairs(engine, slot_quads[g][:, 2 * a : 2 * b], slot_pairs[g], a, b)

@@ -27,6 +27,7 @@ HOLD = 16
 HEAD_A = (0, 512)
 HEAD_B = (192, 448)
 SPLIT0 = 448
+EARLY = 256
 GP = 224
 
 
@@ -52,18 +53,15 @@ def tile_moe_shr_lin_none_kernel(tc, xT, w_words, w_scales, gate, offs, out):
 
         middle_pairs = words("middle_pairs", 4 * T)
         token_pairs = [two_rows(x) for x in (words("pairs0", 2 * T), middle_pairs[:, 0 : 2 * T], middle_pairs[:, 2 * T :], words("pairs3", 2 * T))]
-        step3 = S - HOLD + 4 * WIDE
-        tail = words("tail", 2 * step3)
-        quads_b = tail[:, S - HOLD : step3]
-        quads_c = tail[:, step3 + S - HOLD : step3 + S - HOLD + 2 * WIDE]
-        slot_pairs = [two_rows(words(f"slot_pairs{g}", 2 * S)) for g in range(LAST)] + [two_rows(tail)[:, :, 0:S]]
+        slot_pairs3, quads_c = chain("tail", [2 * S, 2 * WIDE])
+        quads_b = words("quads_b", 4 * WIDE)
+        slot_pairs = [two_rows(words(f"slot_pairs{g}", 2 * S)) for g in range(LAST)] + [two_rows(slot_pairs3)]
         quads0 = words("quads0", 2 * T)
         firsts = {g: words(f"first{g}", 2 * T) for g in range(PASSES)}
         seconds, slot_quads = {0: words("second0", 2 * T)}, {}
         for g in range(1, LAST):
             slot_quads[g - 1], seconds[g] = chain(f"second{g}", [2 * S, 2 * T])
-        slot_quads[LAST - 1], seconds[LAST], quads_a = chain("second3", [2 * S, 2 * T, 2 * WIDE])
-        slot_quads[LAST] = words("slot_quads3", 2 * S)
+        last_quads, seconds[LAST], quads_a = chain("second3", [4 * S, 2 * T, 2 * WIDE])
         late_quads = [quads_a, quads_b, quads_c, words("quads_d", 2 * THIRD)]
         late_thirds = [[(1, 1), (2, 1)], [(1, 2), (2, 2), (1, 0), (2, 0)], [(3, 1), (3, 2)], [(3, 0)]]
         late_at = {key: (n, THIRD * j) for n, keys in enumerate(late_thirds) for j, key in enumerate(keys)}
@@ -105,14 +103,16 @@ def tile_moe_shr_lin_none_kernel(tc, xT, w_words, w_scales, gate, offs, out):
 
         early0 = operand("early0", THIRD)
         rest0 = operand("rest0", T - THIRD)
-        slots = [operand(f"slots{g}", S) for g in range(LAST)]
-        last0_at, last1_at = 4096, 1024
-        last = [operand("last0", C, last0_at), operand("last1", C, last1_at)]
+        slots = [operand(f"slots{g}", S) for g in range(LAST - 1)]
+        early1 = operand("early1", C)
+        late0_at, last1_at = 8192, 2048
+        last = [operand("last0", C), operand("last1", C, last1_at)]
+        late0 = operand("late0", C, late0_at, last1_at + 4 * HOLD)
         lates = [
-            operand("late_a", WIDE, None, last1_at + 4 * HOLD),
-            operand("late_b", 2 * WIDE, None, last0_at - 2 * WIDE + 4 * HOLD),
-            operand("late_c", WIDE, None, last0_at + 4 * HOLD),
-            operand("late_d", THIRD, None, last0_at + 4 * HOLD + WIDE),
+            operand("late_a", WIDE, None, late0_at - WIDE + 4 * HOLD),
+            operand("late_b", 2 * WIDE, None, last1_at - 2 * WIDE + 4 * HOLD),
+            operand("late_c", WIDE, None, late0_at + 4 * HOLD),
+            operand("late_d", THIRD, None, late0_at + 4 * HOLD + WIDE),
         ]
 
         def token_operand(g, i):
@@ -123,13 +123,19 @@ def tile_moe_shr_lin_none_kernel(tc, xT, w_words, w_scales, gate, offs, out):
                 codes, scales = lates[n]
             return codes[:, a : a + THIRD], scales[:, a : a + THIRD]
 
-        def slot_operand(g, e):
-            (codes, scales), a = (slots[g], e * C) if g < LAST else (last[e], 0)
-            return codes[:, a : a + C], scales[:, a : a + C]
+        def slot_operand(g, e, lo, hi):
+            if g < LAST - 1:
+                (codes, scales), a = slots[g], e * C
+            elif e == 0:
+                (codes, scales), a = (late0, last[0])[g - 2], 0
+            else:
+                (codes, scales), a = (early1, last[1])[g - 2], 0
+            return codes[:, a + lo : a + hi], scales[:, a + lo : a + hi]
 
-        slot_banks = [psum.tile([P, C], F32, name=f"slot_bank{e}") for e in range(E)]
+        pieces = [(1, 0, C), (0, 0, C)]
+        slot_banks = [psum.tile([P, hi - lo], F32, name=f"slot_bank{n}") for n, (e, lo, hi) in enumerate(pieces)]
         token_banks = [psum.tile([P, THIRD], F32, name=f"token_bank{i}") for i in range(3)]
-        gated = [keep.tile([P, C], F32, name=f"gated{e}") for e in range(E)]
+        gated = [keep.tile([P, hi - lo], F32, name=f"gated{n}") for n, (e, lo, hi) in enumerate(pieces)]
 
         def cast(copy, g, u, a, b):
             copy(
@@ -176,19 +182,22 @@ def tile_moe_shr_lin_none_kernel(tc, xT, w_words, w_scales, gate, offs, out):
                 stop=(g == order[-1]),
             )
 
-        def slot_product(e, g):
-            product(slot_banks[e], e, g, (0, 1, 2, 3), slot_operand(g, e))
+        def slot_product(n, g):
+            e, lo, hi = pieces[n]
+            product(slot_banks[n], e, g, ((0, 1, 3, 2), (0, 1, 2, 3))[e], slot_operand(g, e, lo, hi))
 
-        token_order = ((0, 1, 2, 3), (1, 2, 0, 3), (0, 1, 2, 3))
+        token_order = ((1, 2, 0, 3), (0, 1, 2, 3), (1, 2, 0, 3))
 
         def token_product(i, g):
             product(token_banks[i], E, g, token_order[i], token_operand(g, i))
 
-        def times_gate(e):
-            nc.vector.tensor_tensor(gated[e][:], slot_banks[e][:], gate_sb[:, e * C : (e + 1) * C], MULT)
+        def times_gate(n):
+            e, lo, hi = pieces[n]
+            nc.vector.tensor_tensor(gated[n][:], slot_banks[n][:], gate_sb[:, e * C + lo : e * C + hi], MULT)
 
-        def scatter(e):
-            nc.scalar.activation(window[:].indirect(offsets[:, e * (C // 16) : (e + 1) * (C // 16)]), gated[e][:], COPY)
+        def scatter(n):
+            e, lo, hi = pieces[n]
+            nc.scalar.activation(window[:].indirect(offsets[:, (e * C + lo) // 16 : (e * C + hi) // 16]), gated[n][:], COPY)
 
         for u, (a, b) in ((1, HEAD_A), (0, HEAD_B)):
             if a:
@@ -208,44 +217,55 @@ def tile_moe_shr_lin_none_kernel(tc, xT, w_words, w_scales, gate, offs, out):
             cast(nc.scalar.copy, g, 1, 0, T)
             gather(g, 1)
             cast(nc.gpsimd.tensor_copy, g, 0, 0, GP)
-            cast(nc.scalar.copy, g, 0, GP, T)
             if g < LAST:
+                cast(nc.scalar.copy, g, 0, WIDE, T)
+                cast(nc.scalar.copy, g, 0, GP, WIDE)
                 gather(g, 0)
             else:
+                cast(nc.scalar.copy, g, 0, GP, T)
                 gather(g, 0, C, S)
                 gather(g, 0, 0, C)
-            slot_quads_on("gpsimd", g - 1, 0, S)
-            token_quads("gpsimd", g, 0, THIRD)
-            quantize(slots[g - 1], slot_quads[g - 1])
+            if g < LAST:
+                slot_quads_on("gpsimd", g - 1, 0, S)
+                token_quads("gpsimd", g, 0, THIRD)
+                token_quads("scalar", g, T - EARLY, T)
+                quantize(slots[g - 1], slot_quads[g - 1])
+        nc.gpsimd.tensor_copy(
+            out=last_quads.bitcast(I32).rearrange("p (e w u) -> p e w u", e=4, u=2)[:, 0:4:3],
+            in_=slot_pairs[LAST - 1].bitcast(I32).rearrange("p u (e w) -> p e w u", e=E),
+        )
+        token_quads("gpsimd", LAST, 0, THIRD)
+        quantize(early1, last_quads[:, 6 * C :])
 
-        def middle_quads(quads, a):
+        def middle_quads(quads, a, n=THIRD):
             nc.scalar.copy(
-                out=quads.bitcast(U32).rearrange("p (g w u) -> p g w u", g=2, u=2),
-                in_=middle_pairs.bitcast(U32).rearrange("p (g u w) -> p g w u", g=2, u=2)[:, :, a : a + THIRD],
+                out=quads.bitcast(U32).rearrange("p (g w u) -> p g w u", g=2, u=2)[:, :, 0:n],
+                in_=middle_pairs.bitcast(U32).rearrange("p (g u w) -> p g w u", g=2, u=2)[:, :, a : a + n],
             )
 
         middle_quads(quads_a, THIRD)
-        slot_quads_on("scalar", LAST, C, S)
-        slot_quads_on("scalar", LAST, 0, C)
-        middle_quads(quads_b[:, 0 : 2 * WIDE], WIDE)
-        quantize(last[1], slot_quads[LAST][:, 2 * C :])
-        token_quads("vector", LAST, THIRD, T)
-        quantize(last[0], slot_quads[LAST][:, 0 : 2 * C])
-        for g in range(LAST):
-            for e in (1, 0):
-                slot_product(e, g)
-        for e in (1, 0):
-            slot_product(e, LAST)
+        copy_pairs("scalar", last_quads[:, 4 * C : 6 * C], slot_pairs[LAST], C, S)
+        copy_pairs("scalar", last_quads[:, 2 * C : 4 * C], slot_pairs[LAST], 0, C)
+        token_quads("scalar", LAST, THIRD, T)
+        quantize(last[1], last_quads[:, 4 * C : 6 * C])
+        quantize(last[0], last_quads[:, 2 * C : 4 * C])
+        for g in range(2):
+            for n in range(2):
+                slot_product(n, g)
+        for n, g in ((0, 2), (0, 3), (1, 3)):
+            slot_product(n, g)
 
+        times_gate(0)
+        scatter(0)
+        quantize(late0, last_quads[:, 0 : 2 * C])
+        slot_product(1, 2)
+        quantize(lates[1], late_quads[1])
         times_gate(1)
         scatter(1)
         quantize(lates[0], late_quads[0])
-        times_gate(0)
-        scatter(0)
-        quantize(lates[1], late_quads[1])
         quantize(lates[2], late_quads[2])
         quantize(lates[3], late_quads[3])
-        for g, i in late_thirds[0] + [(0, i) for i in range(3)] + late_thirds[1] + late_thirds[2] + late_thirds[3]:
+        for g, i in late_thirds[1] + [(0, i) for i in range(3)] + late_thirds[0] + late_thirds[2] + late_thirds[3]:
             token_product(i, g)
 
         result = keep.tile([P, T], F32, name="result")

@@ -186,7 +186,7 @@ def tile_moe_shr_lin_none_kernel(tc, xT, w_words, w_scales, gate, offs, out):
             e, lo, hi = pieces[n]
             product(slot_banks[n], e, g, ((0, 1, 3, 2), (0, 1, 2, 3))[e], slot_operand(g, e, lo, hi))
 
-        token_order = ((1, 2, 0, 3), (0, 1, 2, 3), (1, 2, 0, 3))
+        token_order = ((0, 1, 2, 3),) * 3
 
         def token_product(i, g):
             product(token_banks[i], E, g, token_order[i], token_operand(g, i))
@@ -265,7 +265,7 @@ def tile_moe_shr_lin_none_kernel(tc, xT, w_words, w_scales, gate, offs, out):
         quantize(lates[0], late_quads[0])
         quantize(lates[2], late_quads[2])
         quantize(lates[3], late_quads[3])
-        for g, i in late_thirds[1] + [(0, i) for i in range(3)] + late_thirds[0] + late_thirds[2] + late_thirds[3]:
+        for g, i in [(0, i) for i in range(3)] + late_thirds[1] + late_thirds[0] + late_thirds[2] + late_thirds[3]:
             token_product(i, g)
 
         result = keep.tile([P, T], F32, name="result")

from contextlib import ExitStack

import concourse.mybir as mybir

F32 = mybir.dt.float32
BF16 = mybir.dt.bfloat16
I32 = mybir.dt.int32
U32 = mybir.dt.uint32
U16 = mybir.dt.uint16
U8 = mybir.dt.uint8
FP8X4 = mybir.dt.float8_e4m3fn_x4
FP4X4 = mybir.dt.float4_e2m1fn_x4
MULT = mybir.AluOpType.mult
ADD = mybir.AluOpType.add
COPY = mybir.ActivationFunctionType.Copy

P = 128
K, T, E, C, N = 2048, 768, 2, 256, 128
S = E * C
PASSES = K // 512
LAST = PASSES - 1
FLOPS = 2 * K * N * (T + S)

THIRD = T // 3
WIDE = 2 * THIRD
HOLD = 16
HEAD_A = (0, 512)
HEAD_B = (192, 448)
SPLIT0 = 448
EARLY = 256
GP = 224


def tile_moe_shr_lin_none_kernel(tc, xT, w_words, w_scales, gate, offs, out):
    nc = tc.nc
    with ExitStack() as ctx:
        keep = ctx.enter_context(tc.tile_pool(name="keep", bufs=1))
        late = ctx.enter_context(tc.tile_pool(name="late", bufs=1))
        psum = ctx.enter_context(tc.psum_pool(name="psum", bufs=1))

        offsets = keep.tile([P, S // 16], U16, name="offsets")

        def chain(name, sizes):
            tile = keep.tile([P, sum(sizes) - HOLD * (len(sizes) - 1)], F32, name=name, align_bytes=64)
            starts = [sum(sizes[:i]) - HOLD * i for i in range(len(sizes))]
            return [tile[:, a : a + n] for a, n in zip(starts, sizes)]

        def words(name, n):
            return keep.tile([P, n], F32, name=name, align_bytes=64)[:]

        def two_rows(x):
            return x.rearrange("p (u w) -> p u w", u=2)

        middle_pairs = words("middle_pairs", 4 * T)
        token_pairs = [two_rows(x) for x in (words("pairs0", 2 * T), middle_pairs[:, 0 : 2 * T], middle_pairs[:, 2 * T :], words("pairs3", 2 * T))]
        slot_pairs3, quads_c = chain("tail", [2 * S, 2 * WIDE])
        quads_b = words("quads_b", 4 * WIDE)
        slot_pairs = [two_rows(words(f"slot_pairs{g}", 2 * S)) for g in range(LAST)] + [two_rows(slot_pairs3)]
        quads0 = words("quads0", 2 * T)
        firsts = {g: words(f"first{g}", 2 * T) for g in range(PASSES)}
        seconds, slot_quads = {0: words("second0", 2 * T)}, {}
        for g in range(1, LAST):
            slot_quads[g - 1], seconds[g] = chain(f"second{g}", [2 * S, 2 * T])
        last_quads, seconds[LAST], quads_a = chain("second3", [4 * S, 2 * T, 2 * WIDE])
        late_quads = [quads_a, quads_b, quads_c, words("quads_d", 2 * THIRD)]
        late_thirds = [[(1, 1), (2, 1)], [(1, 2), (2, 2), (1, 0), (2, 0)], [(3, 1), (3, 2)], [(3, 0)]]
        late_at = {key: (n, THIRD * j) for n, keys in enumerate(late_thirds) for j, key in enumerate(keys)}

        x_view = xT.rearrange("(g p u e) w -> g u p e w", p=P, u=2, e=2)
        loaded = {}
        for g in range(PASSES):
            loaded[g, 1], loaded[g, 0] = two_rows(firsts[g]), two_rows(seconds[g])
            for u in (1, 0):
                nc.sync.dma_start(loaded[g, u], x_view[g, u])
                if (g, u) == (0, 1):
                    nc.sync.dma_start(offsets[:], offs)

        w_planes = keep.tile([P, (E + 1) * PASSES * N], U8, name="w_planes", align_bytes=64)
        nc.vector.memset(w_planes[:].bitcast(I32), 0)
        window = keep.tile([P, T], F32, name="window")
        nc.vector.memset(window[:], 0.0)

        w_codes = [keep.tile([P, PASSES, 2 * N], U8, name=f"w_codes{e}", align_bytes=64) for e in range(E + 1)]
        gate_sb = keep.tile([P, S], F32, name="gate_sb")
        nc.sync.dma_start(gate_sb[:], gate)
        scale_rows = w_scales.rearrange("e a q n -> q (e a) n")
        for quadrant in range(4):
            nc.sync.dma_start(
                w_planes[32 * quadrant : 32 * quadrant + 4, :].rearrange("p (m n) -> p m n", n=N).bitcast(I32),
                scale_rows[4 * quadrant : 4 * quadrant + 4].bitcast(I32),
            )
        w_view = w_words.rearrange("e a p b -> e p a b").bitcast(I32)
        for e in (1, 0, E):
            nc.sync.dma_start(w_codes[e][:].bitcast(I32), w_view[e])

        def placed(name, n, dtype, at):
            if at is None:
                return keep.tile([P, n], dtype, name=name, align_bytes=64)
            return late.tile([P, n], dtype, name=name, align_bytes=64, offset=at)

        def operand(name, n, codes_at=None, scales_at=None):
            return placed(name + "_codes", n, U32, codes_at), placed(name + "_scales", n, U8, scales_at)

        early0 = operand("early0", THIRD)
        rest0 = operand("rest0", T - THIRD)
        slots = [operand(f"slots{g}", S) for g in range(LAST - 1)]
        early1 = operand("early1", C)
        late0_at, last1_at = 8192, 2048
        last = [operand("last0", C), operand("last1", C, last1_at)]
        late0 = operand("late0", C, late0_at, last1_at + 4 * HOLD)
        lates = [
            operand("late_a", WIDE, None, late0_at - WIDE + 4 * HOLD),
            operand("late_b", 2 * WIDE, None, last1_at - 2 * WIDE + 4 * HOLD),
            operand("late_c", WIDE, None, late0_at + 4 * HOLD),
            operand("late_d", THIRD, None, late0_at + 4 * HOLD + WIDE),
        ]

        def token_operand(g, i):
            if g == 0:
                (codes, scales), a = (early0, 0) if i == 2 else (rest0, THIRD * i)
            else:
                n, a = late_at[g, i]
                codes, scales = lates[n]
            return codes[:, a : a + THIRD], scales[:, a : a + THIRD]

        def slot_operand(g, e, lo, hi):
            if g < LAST - 1:
                (codes, scales), a = slots[g], e * C
            elif e == 0:
                (codes, scales), a = (late0, last[0])[g - 2], 0
            else:
                (codes, scales), a = (early1, last[1])[g - 2], 0
            return codes[:, a + lo : a + hi], scales[:, a + lo : a + hi]

        pieces = [(1, 0, C), (0, 0, C)]
        slot_banks = [psum.tile([P, hi - lo], F32, name=f"slot_bank{n}") for n, (e, lo, hi) in enumerate(pieces)]
        token_banks = [psum.tile([P, THIRD], F32, name=f"token_bank{i}") for i in range(3)]
        gated = [keep.tile([P, hi - lo], F32, name=f"gated{n}") for n, (e, lo, hi) in enumerate(pieces)]

        def cast(copy, g, u, a, b):
            copy(
                out=token_pairs[g][:, u, a:b].bitcast(BF16).rearrange("p (w e) -> p w e", e=2),
                in_=loaded[g, u][:, :, a:b].rearrange("p e w -> p w e"),
            )

        def gather(g, u, a=0, b=S):
            nc.vector.tensor_copy(
                slot_pairs[g][:, u, a:b].bitcast(U32),
                token_pairs[g][:, u, :].bitcast(U32).indirect(offsets[:, a // 16 : b // 16]),
            )

        word_of = {"scalar": U32, "gpsimd": I32, "vector": I32}
        copy_of = {"scalar": nc.scalar.copy, "gpsimd": nc.gpsimd.tensor_copy, "vector": nc.vector.tensor_copy}

        def copy_pairs(engine, quads, pairs, a, b):
            copy_of[engine](
                out=quads.bitcast(word_of[engine]).rearrange("p (w u) -> p w u", u=2),
                in_=pairs[:, :, a:b].bitcast(word_of[engine]).rearrange("p u w -> p w u"),
            )

        def token_quads(engine, g, a, b):
            if g == 0:
                quads = quads0[:, 2 * a : 2 * b]
            else:
                n, at = late_at[g, a // THIRD]
                at += a % THIRD
                quads = late_quads[n][:, 2 * at : 2 * (at + b - a)]
            copy_pairs(engine, quads, token_pairs[g], a, b)

        def quantize(target, quads):
            nc.vector.quantize_mx(out=target[0][:].bitcast(FP8X4), scales=target[1][:], in_=quads.bitcast(BF16))

        def product(bank, e, g, order, moving):
            plane = e * PASSES + g
            nc.tensor.matmul_mx(
                out=bank[:],
                lhsT=w_codes[e][:, g, :].bitcast(FP4X4),
                lhsT_scale=w_planes[:, plane * N : (plane + 1) * N],
                rhs=moving[0].bitcast(FP8X4),
                rhs_scale=moving[1],
                start=(g == order[0]),
                stop=(g == order[-1]),
            )

        def slot_product(n, g):
            e, lo, hi = pieces[n]
            product(slot_banks[n], e, g, ((0, 1, 3, 2), (0, 1, 2, 3))[e], slot_operand(g, e, lo, hi))

        token_order = ((0, 1, 2, 3),) * 3

        def token_product(i, g):
            product(token_banks[i], E, g, token_order[i], token_operand(g, i))

        def times_gate(n):
            e, lo, hi = pieces[n]
            nc.vector.tensor_tensor(gated[n][:], slot_banks[n][:], gate_sb[:, e * C + lo : e * C + hi], MULT)

        def scatter(n):
            e, lo, hi = pieces[n]
            nc.scalar.activation(window[:].indirect(offsets[:, (e * C + lo) // 16 : (e * C + hi) // 16]), gated[n][:], COPY)

        for u, (a, b) in ((1, HEAD_A), (0, HEAD_B)):
            if a:
                cast(nc.gpsimd.tensor_copy, 0, u, 0, a)
            cast(nc.vector.tensor_copy, 0, u, a, b)
            cast(nc.scalar.copy, 0, u, b, T)
            gather(0, u)
        token_quads("scalar", 0, SPLIT0, T)
        token_quads("gpsimd", 0, 0, SPLIT0)
        quantize(early0, quads0[:, 2 * WIDE :])
        quantize(rest0, quads0[:, 0 : 2 * WIDE])

        def slot_quads_on(engine, g, a, b):
            copy_pairs(engine, slot_quads[g][:, 2 * a : 2 * b], slot_pairs[g], a, b)

        for g in range(1, PASSES):
            cast(nc.scalar.copy, g, 1, 0, T)
            gather(g, 1)
            cast(nc.gpsimd.tensor_copy, g, 0, 0, GP)
            if g < LAST:
                cast(nc.scalar.copy, g, 0, WIDE, T)
                cast(nc.scalar.copy, g, 0, GP, WIDE)
                gather(g, 0)
            else:
                cast(nc.scalar.copy, g, 0, GP, T)
                gather(g, 0, C, S)
                gather(g, 0, 0, C)
            if g < LAST:
                slot_quads_on("gpsimd", g - 1, 0, S)
                token_quads("gpsimd", g, 0, THIRD)
                token_quads("scalar", g, T - EARLY, T)
                quantize(slots[g - 1], slot_quads[g - 1])
        nc.gpsimd.tensor_copy(
            out=last_quads.bitcast(I32).rearrange("p (e w u) -> p e w u", e=4, u=2)[:, 0:4:3],
            in_=slot_pairs[LAST - 1].bitcast(I32).rearrange("p u (e w) -> p e w u", e=E),
        )
        token_quads("gpsimd", LAST, 0, THIRD)
        quantize(early1, last_quads[:, 6 * C :])

        def middle_quads(quads, a, n=THIRD):
            nc.scalar.copy(
                out=quads.bitcast(U32).rearrange("p (g w u) -> p g w u", g=2, u=2)[:, :, 0:n],
                in_=middle_pairs.bitcast(U32).rearrange("p (g u w) -> p g w u", g=2, u=2)[:, :, a : a + n],
            )

        middle_quads(quads_a, THIRD)
        copy_pairs("scalar", last_quads[:, 4 * C : 6 * C], slot_pairs[LAST], C, S)
        copy_pairs("scalar", last_quads[:, 2 * C : 4 * C], slot_pairs[LAST], 0, C)
        token_quads("scalar", LAST, THIRD, T)
        quantize(last[1], last_quads[:, 4 * C : 6 * C])
        quantize(last[0], last_quads[:, 2 * C : 4 * C])
        for g in range(2):
            for n in range(2):
                slot_product(n, g)
        for n, g in ((0, 2), (0, 3), (1, 3)):
            slot_product(n, g)

        times_gate(0)
        scatter(0)
        quantize(late0, last_quads[:, 0 : 2 * C])
        slot_product(1, 2)
        quantize(lates[1], late_quads[1])
        times_gate(1)
        scatter(1)
        quantize(lates[0], late_quads[0])
        quantize(lates[2], late_quads[2])
        quantize(lates[3], late_quads[3])
        for g, i in [(0, i) for i in range(3)] + late_thirds[1] + late_thirds[0] + late_thirds[2] + late_thirds[3]:
            token_product(i, g)

        result = keep.tile([P, T], F32, name="result")
        for i in (1, 2, 0):
            cols = slice(THIRD * i, THIRD * (i + 1))
            nc.vector.tensor_tensor(result[:, cols], token_banks[i][:], window[:, cols], ADD)
            nc.sync.dma_start(out[:, cols], result[:, cols])
